import numpy as np, ml_dtypes
CORES = [40,41,42,43,44,45,46,47]
N = 8
BF = ml_dtypes.bfloat16
L0, CAP, RO, B, OFF, H = 1024, 192, 3, 128, (7, 1, 6, 2), 80
G = B * len(OFF); LM = L0 + RO * CAP; W0 = G + L0
Q0 = B // 2
def fit(x):
    return np.minimum(np.maximum(x, 0.0009765625), 2.0).astype(np.float32)
def places(lev, a):
    return np.concatenate([lev[(a + o) % N, :B] for o in OFF] + [lev[a]])
def body(rng, lev, lo, hi):
    gf = np.exp2(rng.uniform(-0.4, 0.4, (N, 8, 1, L0)))
    return fit((lev[:, None, None, :] * gf * rng.uniform(lo, hi, (N, 8, 16, L0))).reshape(N, 128, L0))
def weave(rng, lev, l, share):
    for a in range(N):
        key = np.log2(places(lev, a))
        for g in range(8):
            o = np.argsort(key + 0.4 * rng.standard_normal(W0)); at = np.argsort(o)[G:]
            near = o[np.clip(at + rng.integers(-48, 49, (16, L0)), 0, W0 - 1)]
            l[a, g] = np.where(rng.random(L0) < share, near, l[a, g])
    return l
def two(rng, n):
    i = rng.integers(0, 16, (8, 1, n)); return i, (i + rng.integers(1, 16, (8, 1, n))) % 16
def knife(rng, n):
    F = np.float32; h = F(0.5); q = F(0.75); z = rng.uniform(0.1, 0.6, (8192, 1)).astype(np.float32)
    x = (0.5 * np.reciprocal(1.0 - 0.75 * z.astype(np.float64))).astype(np.float32) + F(2.0 ** -24) * np.arange(-8, 9).astype(np.float32)
    say = ((x + h) - q * (z * x)) > 1; xs = []; zs = []
    for o in (((x + h) - (q * z) * x) > 1, ((x + h) - z * (q * x)) > 1, (x * (F(1) - q * z) + h) > 1, ((x - q * (z * x)) + h) > 1):
        i, j = np.nonzero(say != o); s = rng.integers(0, len(i), n)
        xs.append(x[i[s], j[s]]); zs.append(z[i[s], 0])
    return np.concatenate(xs), np.concatenate(zs)
def late(rng, x, l):
    alt = np.arange(16)[None, :, None] % 2; hub = 2 + np.arange(8)[:, None, None] // 3; D = 2 ** (RO - 1); f = 8 * RO
    x[:, :8] = 0.5 * (4 - RO); l[:, :, :8] = Q0 + alt * hub
    v = np.arange(8, f); rk = np.argsort(rng.random((128, len(v))), axis=0)
    x[:, v] = np.where(rk < H - 1, 1.5, np.where(rk == H - 1, 1.0 + 2.0 ** -24 * (v % 4) - 0.125 * (v // 8 + 1), 0.0)); l[:, :, v] = Q0 + alt
    o = rng.permutation(np.concatenate([np.arange(f, Q0), np.arange(Q0 + 5, L0)]))
    for s in range(RO - 2):
        c = o[s * CAP:(s + 1) * CAP]; rk = np.argsort(rng.random((128, CAP)), axis=0); n = rng.choice(np.array([H, H + 1, 128]), CAP)
        x[:, c] = np.where(rk < n, rng.uniform(1.001, 1.015, (128, CAP)) - 0.125 * (s + 1), 0.0); l[:, :, c] = Q0 + alt
    o = o[(RO - 2) * CAP:]
    for i in range(6):
        c = o[(D + 1) * i:(D + 1) * (i + 1)]; x[:, c] = 0.0; l[:, :, c[:D]] = G + c[1:]; l[:, :, c[D]] = Q0
        if i < 3:
            l[:, :, c[D - 1]] = G + Q0 + 2 + i; x[48 * i:48 * i + 48, c[0]] = 2.0
        else:
            b = rng.uniform(0.004, 0.03, 128).astype(np.float32); hit = (np.arange(16)[None, :] == rng.integers(0, 16, (8, 1))).reshape(-1); up = np.repeat((np.arange(8) + i) % 2 == 1, 16)
            x[:, c[0]] = b; x[:, c[D]] = np.where(hit & up, np.nextafter(b, np.float32(1)), np.where(hit, np.nextafter(b, np.float32(0)), b))
    o = o[6 * (D + 1):]; c = o[:24]; e = o[24:]
    x[:, c] = np.where(rng.random((128, 24)) < 0.1, 0.0009765625, 0.0); l[:, :, c] = G + c[rng.integers(0, 24, (8, 16, 24))]
    l[:, :, e] = G + e[rng.integers(0, len(e), (8, 16, len(e)))]
def pack(x, l):
    return {"x0": np.ascontiguousarray(x).astype(np.float32), "nb": np.ascontiguousarray(l.reshape(N, 128, L0)).astype(np.int32)}
def setup_inputs(rng):
    lev = np.exp2(rng.uniform(-3, 0.8, (N, L0)))
    return pack(body(rng, lev, 0.7, 1.3), weave(rng, lev, rng.integers(0, W0, (N, 8, 16, L0)), 0.4))
def setup_inputs_spread(rng):
    lev = np.exp2(rng.uniform(-9, 1, (N, L0))); l = np.minimum((W0 * rng.random((N, 8, 16, L0)) ** 3).astype(np.int64), W0 - 1)
    q = rng.permutation(N)[:N // 4]; lev[q] = np.exp2(rng.uniform(-9, -3, (len(q), L0)))
    s = rng.permutation(8)[:4]; l[:, s] = W0 - 1 - l[:, s]
    x = body(rng, lev, 0.25, 2.0); l = weave(rng, lev, l, 0.3)
    x[:, :, Q0:Q0 + 5] = 0.0; x[:, :, Q0 + 1] = 0.5; l[:, :, :, Q0:Q0 + 5] = Q0
    for j in range(3): x[:, 48 * j:48 * j + 48, Q0 + 2 + j] = 2.0
    for a in q: late(rng, x[a], l[a])
    return pack(x, l)
def setup_inputs_ends(rng):
    x = np.zeros((N, 128, L0)); l = np.zeros((N, 8, 16, L0), np.int64)
    for a in range(N):
        odd = a % 2; o = 1 + rng.permutation(L0 - 2); n = CAP - 2 if odd else CAP + 1 + int(rng.integers(0, L0 // 8))
        c = rng.choice(np.array([0, H - 1, H - 1]), L0); c[o[:n]] = rng.choice(np.array([H, H, 128]), n)
        c[0] = 128 * odd; c[L0 - 1] = 128 * odd
        x[a] = 2.0 * (np.argsort(rng.random((128, L0)), axis=0) < c)
        e = np.where(rng.random((8, 16, L0)) < 0.5, 0, W0 - 1)
        k = np.where(rng.random((8, 16, L0)) < 0.72, e, rng.integers(0, W0, (8, 16, L0)))
        i, j = two(rng, L0); np.put_along_axis(k, i, 0, 1); np.put_along_axis(k, j, W0 - 1, 1)
        same = (rng.random((8, 1, L0)) < 0.15) & (c < H)
        l[a] = np.where(same, e[:, :1], k)
    return pack(x, l)
def setup_inputs_corners(rng):
    nc = L0 // 8; x = np.zeros((N, 128, L0)); l = rng.integers(0, W0, (N, 8, 16, L0)); me = G + np.arange(L0)
    want = np.array([CAP, CAP + 1, L0 - nc, CAP - 1, 0, 1, CAP, L0 - nc])[:N][rng.permutation(N)]
    for a in range(N):
        o = rng.permutation(L0)
        if want[a] == L0 - nc: o = np.concatenate([o[o >= 256], o[o < 256]])
        cold = o[:nc]; hot = o[nc:nc + int(want[a])]
        c = rng.choice(np.array([0, 1, H - 1, H - 1]), L0); c[hot] = rng.choice(np.array([H, H, H + 1, 127, 128]), len(hot))
        hi = np.where(rng.random((128, L0)) < 0.25, 2.0, rng.uniform(1.5, 2.0, (128, L0)))
        lo = np.where(rng.random((128, L0)) < 0.25, 0.5, rng.uniform(0.0625, 0.5, (128, L0)))
        x[a] = np.where(np.argsort(rng.random((128, L0)), axis=0) < c, hi, lo)
        x[a][:, cold] = rng.uniform(0.015625, 0.03125, (128, nc))
        kd = rng.permutation(8)
        l[a, kd[1]] = me
        l[a, kd[2]] = rng.choice(np.array([G, G + L0 - 1]), (16, L0))
        l[a, kd[3]] = rng.choice(np.array([0, G - 1]), (16, L0))
        l[a, kd[4]] = rng.integers(0, W0, L0)
        l[a, kd[5]] = np.maximum(me - 1, G)
        l[a, kd[6]] = G + (np.arange(L0) ^ 1)
        l[a, kd[7]] = int(rng.integers(0, W0))
        i, j = two(rng, L0); np.put_along_axis(l[a], i, G + cold[rng.integers(0, nc, (8, 1, L0))], 1)
        l[a][:, :, cold] = G + cold[rng.integers(0, nc, (8, 16, nc))]
    return pack(x, l)
def setup_inputs_close(rng):
    nq = L0 // 8; nf = 24; base = rng.uniform(0.25, 1.9, (nf, 128)).astype(np.float32); fam = rng.integers(0, nf, (N, L0))
    base[:, 96:] = base[:, 96:] * np.float32(0.03125)
    v = np.ascontiguousarray(base[fam].transpose(0, 2, 1)).reshape(N, 8, 16, L0)
    hit = np.arange(16)[None, None, :, None] == rng.integers(0, 16, (N, 8, 1, L0)); kind = rng.integers(0, 3, (N, 8, 1, L0))
    v = np.where(hit & (kind == 1), np.nextafter(v, np.float32(4)), np.where(hit & (kind == 2), np.nextafter(v, np.float32(0)), v))
    x = np.ascontiguousarray(v).reshape(N, 128, L0); l = rng.integers(0, W0, (N, 8, 16, L0)); unit = 2.0 ** -24
    for a in range(N):
        pf = places(fam, a); o = np.argsort(pf, kind="stable"); first = np.searchsorted(pf[o], np.arange(nf)); cnt = np.bincount(pf, minlength=nf)
        mates = o[first[fam[a]] + (rng.random((8, 16, L0)) * cnt[fam[a]]).astype(np.int64)]
        l[a] = np.where(rng.random((8, 16, L0)) < 0.75, mates, l[a])
        rk = np.argsort(rng.random((128, nq)), axis=0)
        x[a, :, :nq] = np.where(rk < H - 1, 1.5, np.where(rk == H - 1, 0.5 + unit * rng.integers(0, 4, nq), np.where(rk < H + 3, 0.5 + unit * rng.integers(0, 2, (128, nq)), 0.25)))
        x[a, :, nq:nq + 8] = 2.0; x[a, :, nq + 8:nq + 16] = 0.0
        i, j = two(rng, nq); k = l[a][:, :, :nq].copy()
        np.put_along_axis(k, i, G + nq + rng.integers(0, 8, (8, 1, nq)), 1); np.put_along_axis(k, j, G + nq + 8 + rng.integers(0, 8, (8, 1, nq)), 1)
        l[a][:, :, :nq] = k
        c = nq + 16 + np.arange(48); xe, ze = knife(rng, 12); rk = np.argsort(rng.random((128, 48)), axis=0)
        x[a][:, c] = np.where(rk < H - 1, 1.5, np.where(rk == H - 1, xe, 0.25))
        x[a][:, c + 48] = np.where(rk == H - 1, ze, rng.uniform(0.1, 0.6, (128, 48)))
        i, j = two(rng, 48); k = np.where(rng.random((8, 16, 48)) < 0.5, G + nq + rng.integers(0, 8, (8, 16, 48)), G + c + 48)
        np.put_along_axis(k, i, G + nq + rng.integers(0, 8, (8, 1, 48)), 1); np.put_along_axis(k, j, G + c[None, None, :] + 48, 1)
        l[a][:, :, c] = k
    return pack(x, l)
def setup_inputs_calm(rng):
    lev = rng.uniform(0.1, 0.35, (N, L0)); x = lev[:, None, :] * rng.uniform(0.9, 1.1, (N, 128, L0)); n = rng.permutation(N) % 4
    for a in range(N):
        x[a][:, rng.permutation(L0)[:int(n[a])]] = 2.0
    return pack(x, rng.integers(0, W0, (N, 8, 16, L0)))
def check_inputs(d):
    bad = []; x = np.asarray(d["x0"]).astype(np.float64)
    if not (np.min(x) >= 0 and np.max(x) <= 2): bad.append("range of x0")
    if np.any((x > 0) & (x < 0.0009765625)): bad.append("small numbers of x0")
    if np.min(d["nb"]) < 0 or np.max(d["nb"]) > W0 - 1: bad.append("range of nb")
    return bad
def reference(x0, nb):
    F = np.float32
    x = np.zeros((N, 128, LM), np.float32); x[:, :, :L0] = x0
    l = np.zeros((N, 8, 16, LM), np.int64); l[:, :, :, :L0] = nb.reshape(N, 8, 16, L0)
    live = [L0] * N
    for t in range(RO):
        old = np.array(x)
        for a in range(N):
            n = live[a]; own = old[a, :, :n]
            w = np.concatenate([old[(a + o) % N, :, :B] for o in OFF] + [own], axis=1)
            xn = np.zeros((128, n), np.float32); mv = np.zeros((8, 16, n), np.int64)
            for g in range(8):
                c = own[16 * g:16 * g + 16]; k = np.array(l[a, g, :, :n])
                p = np.take(w[16 * g:16 * g + 16], k, axis=1)
                y = np.maximum.reduce(p, axis=1); z = np.minimum.reduce(p, axis=1)
                xn[16 * g:16 * g + 16] = np.minimum(np.maximum((c + F(0.25) * y) - F(0.75) * (z * c), F(0)), F(2))
                none = np.logical_not(np.any(p > c[:, None, :], axis=0))
                mv[g] = np.where(none & (k >= G), np.take_along_axis(k, np.maximum(k - G, 0), 1), k)
            ready = (np.add.reduce((xn > 1).astype(np.int64), axis=0) >= H).astype(np.int64)
            m = np.flatnonzero((ready == 1) & (np.add.accumulate(ready) <= CAP)); ch = n + np.arange(len(m))
            xn[:, m] = xn[:, m] * F(0.5)
            x[a, :, :n] = xn; x[a][:, ch] = xn[:, m]
            l[a, :, :, :n] = mv; l[a][:, :, ch] = mv[:, :, m]
            l[a][:, t, ch] = G + m; l[a][:, t, m] = G + ch
            live[a] = n + len(m)
    return {"yx": x, "yn": l.reshape(N, 128, LM).astype(np.float32)}

@@ -1,0 +1,623 @@
+from concourse.bass import DstId, RemoteDMATransfer
+from concourse.mybir import AluOpType, ActivationFunctionType
+
+N = 8
+OFF = (7, 1, 6, 2)
+L0, CAP, RO, GH, H = 1024, 192, 3, 512, 80
+LM = L0 + RO * CAP
+OWN = LM + CAP
+CHUNKS = ((320, 384, 320), (320, 512, 384), (512, 512, 384))
+WIDTHS = (320, 384, 512)
+NMAX = 1408
+BIG = 4096.0
+
+NV_MAX = 16
+NV_MIN = 0
+A_GROUPS = ((0, 4, "S"), (4, 4, "S"), (8, 4, "S"), (12, 4, "S"))
+B_GROUPS = ((0, 4, "S"), (4, 4, "S"), (8, 4, "S"), (12, 4, "S"))
+B_FIRST = 1
+B_AFTER = (0, 4, 0)
+CARRY_FIRST = 1
+YW = NMAX if NV_MAX < 16 else 8
+RING = 7040 + 2 * (NMAX - YW)
+GHOST0_ENGINES = 2
+
+F, BF, I32, U16 = "float32", "bfloat16", "int32", "uint16"
+SCRATCH = {
+    "wa": ("sbuf", [128, GH + OWN], F), "wb": ("sbuf", [128, GH + OWN], F), "wc": ("sbuf", [128, GH + OWN], F),
+    "la": ("sbuf", [128, GH + OWN], F), "lb": ("sbuf", [128, GH + OWN], F), "lc": ("sbuf", [128, GH + OWN], F),
+    "pp": ("sbuf", [128, 16 * NMAX], F),
+    "pl": ("sbuf", [128, OWN], F),
+    "gr": ("sbuf", [128, RING], F),
+    "gd": ("sbuf", [128, NMAX], F),
+    "tt": ("sbuf", [128, 1056], F),
+    "zr": ("sbuf", [128, NMAX], F), "zl": ("sbuf", [128, NMAX], F),
+    "yr": ("sbuf", [128, YW], F), "yl": ("sbuf", [128, YW], F),
+    "nbi": ("sbuf", [128, L0], I32),
+    "idq": ("sbuf", [128, 128], F), "id1": ("sbuf", [128, 128], F),
+    "xc": ("sbuf", [128, CAP], F), "lk": ("sbuf", [128, CAP], F), "t1": ("sbuf", [128, CAP], F),
+    "t2": ("sbuf", [128, CAP], F), "bg": ("sbuf", [128, CAP], F),
+    "ex": ("sbuf", [128, 384], F),
+    "cmp": ("sbuf", [128, 4 * 512], BF),
+    "lt0": ("sbuf", [128, NMAX], U16), "lt1": ("sbuf", [128, NMAX], U16),
+    "vote": ("sbuf", [128, NMAX], BF),
+    "win": ("sbuf", [128, 1600], BF),
+    "val": ("sbuf", [128, 176], BF),
+    "sb": ("sbuf", [128, 144], BF), "wb16": ("sbuf", [128, 144], BF),
+    "negu": ("sbuf", [128, 128], BF), "ones": ("sbuf", [128, 128], BF),
+    "rl": ("sbuf", [128, 80], U16),
+    "ip": ("sbuf", [128, 8], I32), "col": ("sbuf", [128, 24], F),
+    "iot": ("sbuf", [128, 32], F), "jj": ("sbuf", [128, 32], F),
+    "kf": ("sbuf", [128, 32], F), "ki": ("sbuf", [128, 32], I32),
+    "dd": ("sbuf", [128, 12], F), "dump": ("sbuf", [128, 12], F),
+    "rr": ("sbuf", [128, 16], BF), "rin": ("sbuf", [128, 16], BF),
+    "sm": ("sbuf", [128, 48], F),
+    "pos": ("sbuf", [128, 12], U16), "ml": ("sbuf", [128, 12], U16), "cl": ("sbuf", [128, 12], U16),
+    "c0": ("psum", [128, 512], F), "c1": ("psum", [128, 512], F), "c2": ("psum", [128, 512], F),
+    "n0": ("psum", [128, 512], F), "n1": ("psum", [128, 512], F), "n2": ("psum", [128, 512], F),
+    "y0": ("psum", [128, 512], F), "y1": ("psum", [128, 512], F),
+}
+PSUM = ("c0", "c1", "c2", "n0", "n1", "n2", "y0", "y1")
+SEMAPHORES = (["qV", "qS", "qP", "qG"] + ["d%d" % i for i in range(60)]
+              + ["ga%d" % t for t in range(RO)] + ["gl%d" % t for t in range(RO)]
+              + ["%s%d" % (s, i) for s in ("fa", "fl", "ra", "rl") for i in range(9)])
+
+A = AluOpType
+ACT = ActivationFunctionType
+
+
+def partner_of(T, topo, core):
+    same = [c for c in T.cores if topo.chip(c) == topo.chip(core) and topo.die(c) == topo.die(core)]
+    i = same.index(core)
+    return same[i + 1] if i % 2 == 0 else same[i - 1]
+
+
+def rank_program(g, core, T, topo):
+    rank = T.rank_of(core)
+    if rank is None:
+        return
+    Q = {"V": g.vector, "S": g.scalar, "P": g.tensor, "G": g, "Y": g.sync}
+    count = {"V": 0, "S": 0, "P": 0, "G": 0}
+    known = {q: {} for q in Q}
+    seen = {}
+    total = {}
+    ndma = [0]
+
+    def wait(q, tok):
+        s, v = tok
+        if known[q].get(s, 0) < v:
+            Q[q].wait_ge(T.sem[s], v)
+            known[q][s] = v
+
+    def before(q, reads, writes):
+        need = {}
+        for acc, w in ((reads, False), (writes, True)):
+            for b, lo, hi in acc:
+                for e in seen.get(b, ()):
+                    if q == "P" and e[3] == "P":
+                        continue
+                    meet = e[0] < hi and lo < e[1] and (w or e[2])
+                    if meet or (b in PSUM and e[3] != q):
+                        need[e[4][0]] = max(need.get(e[4][0], 0), e[4][1])
+        for s in need:
+            wait(q, (s, need[s]))
+
+    def note(q, reads, writes, tok):
+        for b, lo, hi in writes:
+            seen[b] = [e for e in seen.get(b, ()) if not (lo <= e[0] and e[1] <= hi)]
+            seen[b].append([lo, hi, True, q, tok])
+        for b, lo, hi in reads:
+            keep = [e for e in seen.get(b, ())
+                    if not (not e[2] and e[4][0] == tok[0] and lo <= e[0] and e[1] <= hi)]
+            keep.append([lo, hi, False, q, tok])
+            seen[b] = keep
+        total[tok[0]] = max(total.get(tok[0], 0), tok[1])
+
+    def op(q, call, reads, writes):
+        before(q, reads, writes)
+        count[q] += 1
+        call().then_inc(T.sem["q" + q], 1)
+        note(q, reads, writes, ("q" + q, count[q]))
+
+    def dmas(q, items):
+        s = "d%d" % ndma[0]
+        ndma[0] += 1
+        for o, i, r, w in items:
+            before(q, r, w)
+        for o, i, r, w in items:
+            Q[q].dma_start(o, i).then_inc(T.sem[s], 16)
+        for o, i, r, w in items:
+            note("D", r, w, (s, 16 * len(items)))
+
+    def R(b, lo, hi):
+        return (b, lo, hi)
+
+    def ap(r):
+        return T[r[0]][:, r[1]:r[2]]
+
+    def sc(x):
+        return ap(x) if isinstance(x, tuple) else x
+
+    def regs(*xs):
+        return [x for x in xs if isinstance(x, tuple)]
+
+    def ts(out, in0, s1, o0, s2=None, o1=None, idx=None, step=None):
+        i = ap(in0) if idx is None else ap(in0).indirect(ap(idx))
+        o = ap(out) if step is None else T[out[0]][:, out[1]:out[2]:step]
+        if o1 is None:
+            f = lambda: g.vector.tensor_scalar(o, i, sc(s1), None, o0)
+        else:
+            f = lambda: g.vector.tensor_scalar(o, i, sc(s1), sc(s2), o0, o1)
+        op("V", f, regs(in0, s1, s2, idx), [out])
+
+    def tt(out, in0, in1, o, oidx=None):
+        oo = ap(out) if oidx is None else ap(out).indirect(ap(oidx))
+        op("V", lambda: g.vector.tensor_tensor(oo, ap(in0), ap(in1), o), regs(in0, in1, oidx), [out])
+
+    def cp(out, in_, idx=None, oidx=None):
+        i = ap(in_) if idx is None else ap(in_).indirect(ap(idx))
+        o = ap(out) if oidx is None else ap(out).indirect(ap(oidx))
+        op("V", lambda: g.vector.tensor_copy(o, i), regs(in_, idx, oidx), [out])
+
+    def ms(out, c):
+        op("V", lambda: g.vector.memset(ap(out), c), [], [out])
+
+    def act(out, in_, scale=1.0, idx=None):
+        i = ap(in_) if idx is None else ap(in_).indirect(ap(idx))
+        op("S", lambda: g.scalar.activation(ap(out), i, ACT.Identity, scale=sc(scale)),
+           regs(in_, idx, scale), [out])
+
+    def mm(out, lhsT, rhs, start, stop, step=None):
+        r = ap(rhs) if step is None else T[rhs[0]][:, rhs[1]:rhs[2]:step]
+        op("P", lambda: g.tensor.matmul(ap(out), ap(lhsT), r, start, stop), [lhsT, rhs], [out])
+
+    def iota(out, pattern, base, cm):
+        if SCRATCH[out[0]][2] == I32:
+            f = lambda: g.iota(ap(out), pattern, base, cm)
+        else:
+            f = lambda: g.iota(ap(out), pattern, base, cm, allow_small_or_imprecise_dtypes=True)
+        op("G", f, [], [out])
+
+    def remote(transfers, lsem, reads, waits, alone=True):
+        before("G", reads, [])
+        for tok in waits:
+            wait("G", tok)
+        trs, n = [], 0
+        for dst, engs, rsem, srcs, d, alu in transfers:
+            rid, pid, se = topo.addr(dst)
+            m = 0
+            for e in engs:
+                m |= 1 << e
+            trs.append(RemoteDMATransfer(dst_ids=[DstId(rid=rid, pnc=pid)], dma_engine_mask=m, remote_sem=T.sem[rsem],
+                                         srcs=[ap(s) for s in srcs], dsts=[ap(d)], alu_op=alu))
+            n += len(engs)
+        g.remote_dma_fused(trs, local_sem=T.sem[lsem])
+        if alone:
+            note("D", reads, [], (lsem, n))
+            total[lsem] = n
+        return n
+
+    mate = partner_of(T, topo, core)
+    mate_engs = topo.engines(core, mate)
+    WB = ("wa", "wb", "wc", "wa")
+    LB = ("la", "lb", "lc", "la")
+    NT = [L0 + CAP * t for t in range(RO + 1)]
+    V0 = [[sum(CHUNKS[t][:c]) for c in range(3)] for t in range(RO)]
+    RLO = {w: sum(x // 16 for x in WIDTHS[:i]) for i, w in enumerate(WIDTHS)}
+    FOLD_MAX, FOLD_MIN = NV_MAX < 16, NV_MIN < 16
+    PM, PG, PAR, PG16, WGT = (R("col", i, i + 1) for i in (0, 1, 2, 3, 4))
+    RM = [R("col", 8 + t, 9 + t) for t in range(3)]
+    NRM = [R("col", 12 + t, 13 + t) for t in range(3)]
+    NC_ = [R("col", 16 + t, 17 + t) for t in range(4)]
+    PARC = R("col", 20, 21)
+
+    def own(b, lo, hi):
+        return R(b, GH + lo, GH + hi)
+
+    def P(t, c, k, n=1):
+        C = CHUNKS[t][c]
+        o = 16 * V0[t][c] + k * C
+        return R("pp", o, o + n * C)
+
+    def LT(t, c, k, n):
+        Wc = CHUNKS[t][c] // 16
+        o = V0[t][c] + k * Wc
+        return R("lt%d" % (t % 2), o, o + n * Wc)
+
+    def send_ghosts(t):
+        trs, per = [], 0
+        for d in range(len(OFF)):
+            dst = T.cores[(rank - OFF[d]) % N]
+            engs = topo.engines(core, dst)
+            per = len(engs) // len(OFF)
+            mine = engs[d * per:(d + 1) * per]
+            if t == 0:
+                mine = mine[::per // GHOST0_ENGINES]
+            per = len(mine)
+            trs.append((dst, mine, "ga%d" % t, [own(WB[t], 0, 128)], R(WB[t], 128 * d, 128 * d + 128), 0))
+        remote(trs, "gl%d" % t, [own(WB[t], 0, 128)], [])
+        note("X", [], [R(WB[t], 0, GH)], ("ga%d" % t, per * len(OFF)))
+
+    def relayout_consts(C):
+        Wc = C // 16
+        kf, ki, j = R("kf", 0, Wc), R("ki", 0, Wc), R("jj", 0, Wc)
+        ts(kf, j, 1.0 / Wc, A.mult, 0.5 / Wc - 0.5, A.add)
+        ts(PARC, PAR, float(C + 16), A.mult)
+        cp(ki, kf)
+        cp(kf, ki)
+        ts(kf, kf, -(C - 1) / 16.0, A.mult)
+        tt(kf, kf, j, A.add)
+        ts(R("rl", RLO[C], RLO[C] + Wc), kf, 16.0, A.mult, PARC, A.add)
+
+    def relayout(t, c):
+        C, v0 = CHUNKS[t][c], V0[t][c]
+        a, b = own(LB[t], v0, v0 + C), own(LB[t], v0 - 16, v0 + C + 16)
+        o1, o2 = R("tt", 0, C), R("tt", C, 2 * C + 32)
+        op("V", lambda: g.vector.transpose(ap(o1), ap(a)), [a], [o1])
+        op("V", lambda: g.vector.transpose(ap(o2), ap(b)), [b], [o2])
+        cp(LT(t, c, 0, 16), R("tt", 0, 2 * C + 32), idx=R("rl", RLO[C], RLO[C] + C // 16))
+
+    def copy_c(t, c):
+        C, v0 = CHUNKS[t][c], V0[t][c]
+        mm(R("c%d" % c, 0, C), R("idq", 0, 128), own(WB[t], v0, v0 + C), True, True)
+
+    def copy_x(t, c):
+        C, v0 = CHUNKS[t][c], V0[t][c]
+        mm(R("y0", 0, C), R("id1", 0, 128), own(WB[t], v0, v0 + C), True, True)
+
+    def gather_a(t, c, grp):
+        k0, n, q = grp
+        w = R(WB[t], 0, GH + NT[t])
+        if q == "S":
+            act(P(t, c, k0, n), w, 0.25, idx=LT(t, c, k0, n))
+        else:
+            ts(P(t, c, k0, n), w, 0.25, A.mult, idx=LT(t, c, k0, n))
+
+    slot = [0]
+
+    def gather_b(t, c, grp):
+        k0, n, q = grp
+        C, v0 = CHUNKS[t][c], V0[t][c]
+        if slot[0] + n * C > RING:
+            slot[0] = 0
+        o = slot[0]
+        slot[0] += n * C
+        w = R(LB[t], 0, GH + NT[t])
+        if q == "S":
+            act(R("gr", o, o + n * C), w, 1.0, idx=LT(t, c, k0, n))
+        else:
+            cp(R("gr", o, o + n * C), w, idx=LT(t, c, k0, n))
+        dmas("Y", [(T.gd[k0 + i:128:16, v0:v0 + C], T.gr[k0 + i:128:16, o + i * C:o + (i + 1) * C],
+                    [R("gr", o + i * C, o + (i + 1) * C)], [R("gd#%d" % (k0 + i), v0, v0 + C)]) for i in range(n)])
+
+    cslot = [0]
+
+    def acc(t, c, k, nv, bank, o):
+        if k <= 16 - nv:
+            return
+        C, v0 = CHUNKS[t][c], V0[t][c]
+        out = own(WB[t + 1], v0, v0 + C) if (k == 15 and nv < 16) else R(bank, 0, C)
+        tt(out, P(t, c, k), P(t, c, k - 1) if k == 17 - nv else R(bank, 0, C), o)
+
+    def compare(t, c, k):
+        C = CHUNKS[t][c]
+        s = R("cmp", 512 * (cslot[0] % 4), 512 * (cslot[0] % 4) + C)
+        cslot[0] += 1
+        tt(s, P(t, c, k), R("c%d" % c, 0, C), A.is_gt)
+        mm(R("n%d" % c, 0, C), R("sb", 15 - k, 143 - k), s, k == 0, k == 15)
+        acc(t, c, k, NV_MIN, "y1", A.min)
+        acc(t, c, k, NV_MAX, "y0", A.max)
+
+    def after_compare(t, c):
+        C, v0 = CHUNKS[t][c], V0[t][c]
+        if not FOLD_MAX:
+            tt(own(WB[t + 1], v0, v0 + C), own(WB[t], v0, v0 + C), R("y0", 0, C), A.add)
+        if not FOLD_MIN:
+            tt(R("c%d" % c, 0, C), own(WB[t], v0, v0 + C), R("y1", 0, C), A.mult)
+
+    def fold(t, c):
+        C, v0, i = CHUNKS[t][c], V0[t][c], 3 * t + c
+        jobs = []
+        if FOLD_MIN:
+            jobs.append((NV_MIN, "zl", 3))
+        if FOLD_MAX:
+            jobs.append((NV_MAX, "yl", 2))
+        if not jobs:
+            return
+        n, reads = 0, []
+        for nv, land, alu in jobs:
+            srcs = [P(t, c, k) for k in range(16 - nv)]
+            n += remote([(mate, mate_engs, "fa%d" % i, srcs, R(land, v0, v0 + C), alu)], "fl%d" % i, srcs, [], False)
+            reads += srcs
+        note("D", reads, [], ("fl%d" % i, n))
+        arrived[i] = n
+        total["fa%d" % i] = n
+
+    arrived = {}
+
+    def back(t, c):
+        C, v0, i = CHUNKS[t][c], V0[t][c], 3 * t + c
+        if i not in arrived:
+            return
+        jobs = ([("zl", "zr")] if FOLD_MIN else []) + ([("yl", "yr")] if FOLD_MAX else [])
+        h = len(mate_engs) // len(jobs)
+        trs = [(mate, mate_engs[j * h:(j + 1) * h], "ra%d" % i, [R(a, v0, v0 + C)], R(b, v0, v0 + C), 0)
+               for j, (a, b) in enumerate(jobs)]
+        remote(trs, "rl%d" % i, [], [("fa%d" % i, arrived[i])])
+        note("X", [], [R(b, v0, v0 + C) for a, b in jobs], ("ra%d" % i, h * len(jobs)))
+
+    def update_steps(t, c):
+        C, v0 = CHUNKS[t][c], V0[t][c]
+        bank, xn = R("c%d" % c, 0, C), own(WB[t + 1], v0, v0 + C)
+        st = []
+        if FOLD_MIN:
+            st.append(lambda: tt(bank, R("zr", v0, v0 + C), bank, A.mult))
+        if FOLD_MAX:
+            def a_step():
+                tt(xn, xn if NV_MAX else R("yr", v0, v0 + C), R("y0", 0, C), A.add)
+                if c < 2:
+                    copy_x(t, c + 1)
+            if NV_MAX:
+                st.insert(0, lambda: tt(xn, xn, R("yr", v0, v0 + C), A.max))
+            st.append(a_step)
+        st.append(lambda: ts(bank, bank, 12.0 if FOLD_MIN else 3.0, A.mult))
+        st.append(lambda: tt(bank, xn, bank, A.subtract))
+
+        def vote_step():
+            ts(R("vote", v0, v0 + C), bank, 1.0, A.is_gt)
+            lo = -(-v0 // 128) if v0 % 128 == 0 else v0 // 128
+            hi = (v0 + C) // 128 if c < 2 else -(-(v0 + C) // 128)
+            for cb in range(lo, hi):
+                mm(R("y1", cb, cb + 1), R("vote", 128 * cb, 128 * cb + 128), R("ones", 0, 1), True, True)
+        st.append(vote_step)
+        st.append(lambda: ts(xn, bank, 0.0, A.max, 2.0, A.min))
+        return st
+
+    def keep_step(t, c):
+        C, v0 = CHUNKS[t][c], V0[t][c]
+        return lambda: tt(own(LB[t + 1], v0, v0 + C), own(LB[t], v0, v0 + C), R("n%d" % c, 0, C), A.min)
+
+    def move_step(t, c):
+        C, v0 = CHUNKS[t][c], V0[t][c]
+        bank = R("n%d" % c, 0, C)
+
+        def f():
+            rd = [R("gd#%d" % k, v0, v0 + C) for k in range(16)] + [bank]
+            op("V", lambda: g.vector.tensor_tensor(ap(bank), T.gd[:, v0:v0 + C], ap(bank), A.subtract), rd, [bank])
+        return f
+
+    def join_step(t, c):
+        C, v0 = CHUNKS[t][c], V0[t][c]
+        o = own(LB[t + 1], v0, v0 + C)
+        return lambda: tt(o, o, R("n%d" % c, 0, C), A.max)
+
+    def division_steps(t):
+        nb = -(-NT[t] // 128)
+        r, rin = R("rr", 0, nb), R("rin", 0, nb)
+        q, pf, lm = R("sm", 0, nb), R("sm", 16, 16 + nb), R("sm", 32, 44)
+        s = R("y1", 16, 16 + nb)
+
+        def scan():
+            op("V", lambda: g.vector.tensor_tensor_scan(ap(rin), ap(R("ones", 0, nb)), ap(r), 0.0, A.mult, A.add),
+               [r, R("ones", 0, nb)], [rin])
+            mm(s, R("ones", 0, 128), rin, True, False)
+            mm(s, R("negu", 0, 128), r, False, True)
+            mm(R("y1", 32, 33), R("ones", 0, 128), R("rin", nb - 1, nb), True, True)
+
+        def scatter():
+            cp(R("win", 0, 1600), R("val", 0, 16 * nb), oidx=R("pos", 0, nb))
+            for i in range(16):
+                mm(R("y1", 48, 60), R("wb16", 15 - i, 143 - i), R("win", 1 + i, 193), i == 0, i == 15, step=16)
+        return [lambda: ts(r, R("y1", 0, nb), float(H), A.is_ge),
+                scan,
+                lambda: ts(q, r, -BIG, A.mult),
+                lambda: tt(q, q, R("dd", 0, nb), A.add),
+                lambda: tt(pf, q, s, A.max),
+                lambda: ts(NC_[t + 1], R("y1", 32, 33), float(CAP), A.min, NC_[t], A.add),
+                lambda: cp(R("pos", 0, nb), pf),
+                scatter,
+                lambda: tt(lm, R("dump", 0, 12), R("y1", 48, 60), A.min),
+                lambda: ts(R("ml", 0, 12), lm, BIG, A.add)]
+
+    def round_consts(t):
+        ms(R("win", 0, 208), 0.0)
+        ts(R("t2", 0, CAP), R("pl", L0, L0 + CAP), NC_[t], A.add, RM[t], A.mult)
+        if t > 0:
+            ts(R("cl", 0, 12), R("jj", 0, 12), NC_[t], A.add)
+        if t == RO - 1:
+            ts(R("ex", 0, NT[t] - L0), R("pl", L0, NT[t]), float(GH + L0), A.subtract, NC_[t], A.is_lt)
+
+    ML, CL = R("ml", 0, 12), R("cl", 0, 12)
+
+    def children(t, buf, a, b):
+        if t == 0:
+            o = own(buf, L0, L0 + CAP)
+            cp(o, a) if b is None else tt(o, a, b, A.add)
+        elif b is None:
+            cp(own(buf, L0, OWN), a, oidx=CL)
+        else:
+            tt(own(buf, L0, OWN), a, b, A.add, oidx=CL)
+
+    def child_links(t):
+        ts(R("lk", 0, CAP), own(LB[t + 1], 0, OWN), NRM[t], A.mult, idx=ML)
+        return lambda: children(t, LB[t + 1], R("lk", 0, CAP), R("t1", 0, CAP))
+
+    def weave(*lists):
+        lists = [list(x) for x in lists]
+        while any(lists):
+            for x in lists:
+                if x:
+                    x.pop(0)()
+
+    C0 = CHUNKS[0][0]
+    dmas("Y", [(ap(own("wa", 0, 128)), T.x0[:, 0:128], [], [own("wa", 0, 128)])])
+    dmas("S", [(ap(R("nbi", 0, C0 + 16)), T.nb[:, 0:C0 + 16], [], [R("nbi", 0, C0 + 16)])])
+    dmas("Y", [(ap(own("wa", 128, L0)), T.x0[:, 128:L0], [], [own("wa", 128, L0)])])
+    dmas("S", [(ap(R("nbi", C0 + 16, L0)), T.nb[:, C0 + 16:L0], [], [R("nbi", C0 + 16, L0)])])
+    iota(R("ip", 0, 1), [[1, 1]], 0, 1)
+    iota(R("iot", 0, 32), [[16, 32]], 0, 0)
+    ms(R("idq", 0, 128), 0.25)
+    ms(own("wb", L0, OWN), 0.0)
+    iota(R("la", GH - 16, GH), [[1, 16]], GH - 16, 0)
+    op("G", lambda: g.affine_select(T.idq[:], T.idq[:], [[-1, 128]], A.is_equal, 0.0, 0, 1),
+       [R("idq", 0, 128)], [R("idq", 0, 128)])
+    send_ghosts(0)
+    iota(R("la", 0, GH - 16), [[1, GH - 16]], 0, 0)
+    ts(R("ip", 1, 2), R("ip", 0, 1), 15, A.bitwise_and)
+    ts(R("ip", 2, 3), R("ip", 0, 1), 4, A.arith_shift_right)
+    ts(R("ip", 4, 5), R("ip", 0, 1), 112, A.bitwise_and)
+    ms(R("sb", 0, 144), 0.0)
+    tt(R("ip", 5, 6), R("ip", 0, 1), R("ip", 2, 3), A.add)
+    ms(own("la", L0, L0 + 16), 0.0)
+    ts(R("ip", 3, 4), R("ip", 5, 6), 1, A.bitwise_and)
+    cp(R("col", 0, 4), R("ip", 1, 5))
+    ts(R("jj", 0, 32), R("iot", 0, 32), PM, A.add)
+    relayout_consts(C0)
+    cp(own("la", 0, C0 + 16), R("nbi", 0, C0 + 16))
+    relayout(0, 0)
+    cp(own("la", C0 + 16, L0), R("nbi", C0 + 16, L0))
+    ts(R("sb", 15, 143), R("iot", 0, 8), PG16, A.is_equal, BIG, A.mult, step=16)
+    zer = own("wb", L0, OWN)
+    for b, lo in (("lb", L0), ("wc", NT[1]), ("lc", NT[1]), ("wa", NT[2]), ("la", NT[2])):
+        act(own(b, lo, OWN), R("wb", GH + lo, GH + OWN))
+    act(R("pl", LM, OWN), own("wb", LM, OWN))
+    copy_c(0, 0)
+
+    def late_consts():
+        iota(R("xc", 0, 176), [[8, 11], [0, 16]], -256, 0)
+        iota(R("lk", 0, 176), [[0, 11], [1, 16]], 0, 0)
+        ms(R("negu", 0, 128), -1.0)
+        ms(R("ones", 0, 128), 1.0)
+        op("G", lambda: g.affine_select(T.negu[:], T.negu[:], [[-1, 128]], A.is_gt, 0.0, 0, 1),
+           [R("negu", 0, 128)], [R("negu", 0, 128)])
+        iota(R("pl", 0, LM), [[1, LM]], GH, 0)
+        ts(R("col", 8, 11), R("iot", 0, 3), 1.0 / 16, A.mult, PM, A.is_equal)
+        ms(R("wb16", 0, 144), 0.0)
+        ts(R("col", 12, 15), R("col", 8, 11), -1.0, A.mult, 1.0, A.add)
+        ts(WGT, RM[0], 16.0, A.mult, RM[1], A.add)
+        ts(R("xc", 0, 176), R("xc", 0, 176), PG, A.add, RM[0], A.mult)
+        ts(R("lk", 0, 176), R("lk", 0, 176), RM[1], A.mult)
+        ts(R("wb16", 15, 143), R("iot", 0, 8), 0.0, A.mult, WGT, A.add, step=16)
+        tt(R("val", 0, 176), R("xc", 0, 176), R("lk", 0, 176), A.add)
+        ts(R("dd", 0, 12), R("jj", 0, 12), float(NMAX + 1), A.add)
+        ts(R("dump", 0, 12), R("jj", 0, 12), LM - BIG, A.add)
+        ms(NC_[0], 0.0)
+        ms(R("vote", NT[1], NT[1] + 64), 0.0)
+        if FOLD_MAX:
+            ts(R("id1", 0, 128), R("idq", 0, 128), 4.0, A.mult)
+
+    carry = []
+    for t in range(RO):
+        last = t == RO - 1
+        bq = [(c, grp) for c in range(3) for grp in B_GROUPS]
+        if t == 0:
+            for c, grp in bq[:B_FIRST]:
+                gather_b(t, c, grp)
+            bq = bq[B_FIRST:]
+            late_consts()
+            made = [C0]
+
+            def lists_for(C):
+                if C not in made:
+                    made.append(C)
+                    relayout_consts(C)
+            lists_for(CHUNKS[0][1])
+            relayout(0, 1)
+            lists_for(CHUNKS[0][2])
+            carry = [lambda: relayout(0, 2), lambda: [lists_for(C) for C in WIDTHS]]
+            iota(R("lb", 0, GH), [[1, GH]], 0, 0)
+        for c in range(3):
+            for gi, grp in enumerate(A_GROUPS):
+                gather_a(t, c, grp)
+                if c == 0 and gi == 0:
+                    copy_c(t, 1)
+                    copy_c(t, 2)
+                    for f in carry[:CARRY_FIRST]:
+                        f()
+                    carry = carry[CARRY_FIRST:]
+                for k in range(grp[0], grp[0] + grp[1]):
+                    compare(t, c, k)
+                if c == 0 and carry:
+                    carry.pop(0)()
+            while carry:
+                carry.pop(0)()
+            after_compare(t, c)
+            fold(t, c)
+            if c > 0:
+                back(t, c - 1)
+            nb_ = max(0, sum(B_AFTER[:c + 1]) - (3 * len(B_GROUPS) - len(bq)))
+            for cb, grp in bq[:nb_]:
+                gather_b(t, cb, grp)
+            bq = bq[nb_:]
+            if t == 0 and c == 0:
+                iota(R("lc", 0, GH), [[1, GH]], 0, 0)
+        back(t, 2)
+        if FOLD_MAX:
+            copy_x(t, 0)
+        nxt = 0 if last else (1 if V0[t][1] >= CHUNKS[t + 1][0] else 2)
+        vb = [x for x in bq if x[1][2] == "V"]
+        early = [x for x in bq if x[0] < 2]
+        for c, grp in early:
+            gather_b(t, c, grp)
+        up = [update_steps(t, c) for c in range(3)]
+        weave(up[0][:-1], [keep_step(t, c) for c in range(3)] + [lambda: round_consts(t)])
+        weave(up[1][:-1], up[2][:-1])
+        fill = [up[0][-1], up[1][-1], up[2][-1], move_step(t, 0)]
+        if last:
+            o = own(WB[t + 1], L0, NT[t])
+            fill.append(lambda: tt(o, o, R("ex", 0, NT[t] - L0), A.mult))
+        fill.append(join_step(t, 0))
+        dv = division_steps(t)
+        for i, f in enumerate(dv):
+            f()
+            if i in (0, 1, 4, 6):
+                fill.pop(0)()
+            if i == 7:
+                while fill:
+                    fill.pop(0)()
+        wn, ln = own(WB[t + 1], 0, OWN), own(LB[t + 1], 0, OWN)
+        ts(R("xc", 0, CAP), wn, 0.5, A.mult, idx=ML)
+        cp(R("bg", 0, CAP), ln, idx=ML)
+        cp(wn, R("xc", 0, CAP), oidx=ML)
+        if not last:
+            send_ghosts(t + 1)
+        tt(ln, R("bg", 0, CAP), R("t2", 0, CAP), A.max, oidx=ML)
+        children(t, WB[t + 1], R("xc", 0, CAP), None)
+        if last:
+            dmas("G", [(T.yx[:, :], ap(own(WB[t + 1], 0, LM)), [own(WB[t + 1], 0, LM)], [])])
+        else:
+            copy_c(t + 1, 0)
+        if last or nxt == 2:
+            move_step(t, 1)()
+            join_step(t, 1)()
+        if last:
+            v2 = V0[t][2]
+            dmas("G", [(T.yn[:, 0:v2], ap(own(LB[t + 1], 0, v2)), [own(LB[t + 1], 0, v2)], [])])
+        else:
+            relayout(t + 1, 0)
+        for c, grp in bq[len(early):]:
+            gather_b(t, c, grp)
+        act(R("t1", 0, CAP), R("pl", 0, OWN), RM[t], idx=ML)
+        if last:
+            move_step(t, 2)()
+            join_step(t, 2)()
+            child_links(t)()
+            dmas("S", [(T.yn[:, v2:LM], ap(own(LB[t + 1], v2, LM)), [own(LB[t + 1], v2, LM)], [])])
+        else:
+            def first(t=t, nxt=nxt):
+                if nxt == 1:
+                    move_step(t, 1)()
+                move_step(t, 2)()
+                if nxt == 1:
+                    join_step(t, 1)()
+                join_step(t, 2)()
+                relayout(t + 1, 1)
+
+            def second(t=t):
+                child_links(t)()
+                relayout(t + 1, 2)
+            carry = [first, second]
+
+    for s in total:
+        if max(known[q].get(s, 0) for q in Q) < total[s]:
+            wait("G", (s, total[s]))

@@ -5,62 +5,80 @@ N = 8
 OFF = (7, 1, 6, 2)
 L0, CAP, RO, GH, H = 1024, 192, 3, 512, 80
 LM = L0 + RO * CAP
-OWN = LM + CAP
-CHUNKS = ((320, 384, 320), (320, 512, 384), (512, 512, 384))
-WIDTHS = (320, 384, 512)
+SP = CAP
+O0 = SP + GH
+TW = O0 + LM
+CHUNKS = ((512, 512), (512, 512), (512, 384, 320))
+FOLDED = (1024, 1024, 1216)
+NP = tuple(sum(c) for c in CHUNKS)
+WIDTHS = tuple(sorted(set(w for c in CHUNKS for w in c)))
 NMAX = 1408
 BIG = 4096.0
 
-NV_MAX = 16
-NV_MIN = 0
-A_GROUPS = ((0, 4, "S"), (4, 4, "S"), (8, 4, "S"), (12, 4, "S"))
-B_GROUPS = ((0, 4, "S"), (4, 4, "S"), (8, 4, "S"), (12, 4, "S"))
+GROUPS = ((0, 4), (4, 4), (8, 4), (12, 4))
+FIRST_GROUPS = ((0, 1), (1, 1), (2, 2), (4, 4), (8, 4), (12, 4))
+A_ON_V = ((4,), (2,), (2,))
 B_FIRST = 1
-B_AFTER = (0, 4, 0)
-CARRY_FIRST = 1
-YW = NMAX if NV_MAX < 16 else 8
-RING = 7040 + 2 * (NMAX - YW)
-GHOST0_ENGINES = 2
+B_HELD = 1
+LAG = (2, 1, 1)
+CARRY_AT = (-1, 0, 2, 6, 6, 8, 10)
+UPD_AT = {2: (((1, 8), (1, 9), (1, 11), (1, 12), (1, 13), (1, 14)),),
+          3: (((2, 1), (2, 2), (2, 4), (2, 5)), ((2, 8), (2, 9), (2, 10), (2, 11)))}
+DEFER = (3, 1)
+TWIN_AT = 10
+JOIN_AT = {2: ((1, 4), (1, 13)), 3: ((2, 8), (2, 13))}
+X_AT, NEXT_AT, D_AT = 7, 12, 6
+HEAD = (8, 8, 8)
+OUTQ = "Y"
+RING = 9728
+CS = 6
+GHOST0_ENGINES = 4
 
 F, BF, I32, U16 = "float32", "bfloat16", "int32", "uint16"
 SCRATCH = {
-    "wa": ("sbuf", [128, GH + OWN], F), "wb": ("sbuf", [128, GH + OWN], F), "wc": ("sbuf", [128, GH + OWN], F),
-    "la": ("sbuf", [128, GH + OWN], F), "lb": ("sbuf", [128, GH + OWN], F), "lc": ("sbuf", [128, GH + OWN], F),
-    "pp": ("sbuf", [128, 16 * NMAX], F),
-    "pl": ("sbuf", [128, OWN], F),
+    "wa": ("sbuf", [128, TW], F), "wb": ("sbuf", [128, TW], F), "wc": ("sbuf", [128, TW], F),
+    "la": ("sbuf", [128, TW], F), "lb": ("sbuf", [128, TW], F), "lc": ("sbuf", [128, TW], F),
+    "pp": ("sbuf", [128, 16 * NP[-1]], F),
+    "pl": ("sbuf", [128, TW], F),
     "gr": ("sbuf", [128, RING], F),
-    "gd": ("sbuf", [128, NMAX], F),
+    "gd": ("sbuf", [128, O0 + NMAX], F),
     "tt": ("sbuf", [128, 1056], F),
-    "zr": ("sbuf", [128, NMAX], F), "zl": ("sbuf", [128, NMAX], F),
-    "yr": ("sbuf", [128, YW], F), "yl": ("sbuf", [128, YW], F),
+    "zr": ("sbuf", [128, NP[-1]], F), "zl": ("sbuf", [128, NP[-1]], F),
+    "zh": ("sbuf", [128, NP[-1]], F),
     "nbi": ("sbuf", [128, L0], I32),
-    "idq": ("sbuf", [128, 128], F), "id1": ("sbuf", [128, 128], F),
+    "id1": ("sbuf", [128, 128], F), "idq": ("sbuf", [128, 128], F),
+    "idn": ("sbuf", [128, 128], F), "idb": ("sbuf", [128, 128], F),
     "xc": ("sbuf", [128, CAP], F), "lk": ("sbuf", [128, CAP], F), "t1": ("sbuf", [128, CAP], F),
-    "t2": ("sbuf", [128, CAP], F), "bg": ("sbuf", [128, CAP], F),
-    "ex": ("sbuf", [128, 384], F),
-    "cmp": ("sbuf", [128, 4 * 512], BF),
-    "lt0": ("sbuf", [128, NMAX], U16), "lt1": ("sbuf", [128, NMAX], U16),
-    "vote": ("sbuf", [128, NMAX], BF),
-    "win": ("sbuf", [128, 1600], BF),
+    "t2": ("sbuf", [128, CAP], F), "bg": ("sbuf", [128, CAP], F), "tw": ("sbuf", [128, CAP], F),
+    "gs": ("sbuf", [128, 128], F),
+    "cmp": ("sbuf", [128, CS * 512], BF),
+    "lt0": ("sbuf", [128, NP[-1]], U16), "lt1": ("sbuf", [128, NP[-1]], U16),
+    "vote": ("sbuf", [128, O0 + NMAX], BF),
+    "win": ("sbuf", [128, 1600], BF), "win2": ("sbuf", [128, CAP], BF),
     "val": ("sbuf", [128, 176], BF),
     "sb": ("sbuf", [128, 144], BF), "wb16": ("sbuf", [128, 144], BF),
     "negu": ("sbuf", [128, 128], BF), "ones": ("sbuf", [128, 128], BF),
-    "rl": ("sbuf", [128, 80], U16),
-    "ip": ("sbuf", [128, 8], I32), "col": ("sbuf", [128, 24], F),
+    "rl": ("sbuf", [128, sum(WIDTHS) // 16], U16),
+    "ip": ("sbuf", [128, 8], I32), "col": ("sbuf", [128, 32], F),
     "iot": ("sbuf", [128, 32], F), "jj": ("sbuf", [128, 32], F),
     "kf": ("sbuf", [128, 32], F), "ki": ("sbuf", [128, 32], I32),
-    "dd": ("sbuf", [128, 12], F), "dump": ("sbuf", [128, 12], F),
+    "dd": ("sbuf", [128, 12], F),
     "rr": ("sbuf", [128, 16], BF), "rin": ("sbuf", [128, 16], BF),
-    "sm": ("sbuf", [128, 48], F),
-    "pos": ("sbuf", [128, 12], U16), "ml": ("sbuf", [128, 12], U16), "cl": ("sbuf", [128, 12], U16),
-    "c0": ("psum", [128, 512], F), "c1": ("psum", [128, 512], F), "c2": ("psum", [128, 512], F),
-    "n0": ("psum", [128, 512], F), "n1": ("psum", [128, 512], F), "n2": ("psum", [128, 512], F),
-    "y0": ("psum", [128, 512], F), "y1": ("psum", [128, 512], F),
+    "sm": ("sbuf", [128, 80], F),
+    "pos": ("sbuf", [128, 12], U16), "ml": ("sbuf", [128, 48], U16), "cl": ("sbuf", [128, 36], U16),
+    "si": ("sbuf", [128, 12], U16),
+    "x0b": ("psum", [128, 512], F), "x1b": ("psum", [128, 512], F), "x2b": ("psum", [128, 512], F),
+    "n0": ("psum", [128, 512], F), "n1": ("psum", [128, 512], F),
+    "y0": ("psum", [128, 512], F), "y1": ("psum", [128, 512], F), "z0": ("psum", [128, 512], F),
 }
-PSUM = ("c0", "c1", "c2", "n0", "n1", "n2", "y0", "y1")
+PSUM = ("x0b", "x1b", "x2b", "n0", "n1", "y0", "y1", "z0")
+BANKS = {2: {"x": ("x0b", "x1b"), "n": ("n0", "n1"), "y": ("y0", "y1"), "d": ("y0", "n0"),
+             "j": ("z0", "n1", "z0"), "z": "z0", "m": "x2b"},
+         3: {"x": ("x0b", "x1b", "x2b"), "n": ("n0", "n1", "n0"), "y": ("y0", "y1", "z0"), "d": ("y0", "y1", "n1"),
+             "j": ("y0", "x1b", "x2b", "z0"), "z": "n1", "m": "x0b"}}
 SEMAPHORES = (["qV", "qS", "qP", "qG"] + ["d%d" % i for i in range(60)]
               + ["ga%d" % t for t in range(RO)] + ["gl%d" % t for t in range(RO)]
-              + ["%s%d" % (s, i) for s in ("fa", "fl", "ra", "rl") for i in range(9)])
+              + ["%s%d" % (s, i) for s in ("fa", "fl", "fh", "ra", "rl") for i in range(9)])
 
 A = AluOpType
 ACT = ActivationFunctionType
@@ -139,7 +157,11 @@ def rank_program(g, core, T, topo):
         return ap(x) if isinstance(x, tuple) else x
 
     def regs(*xs):
-        return [x for x in xs if isinstance(x, tuple)]
+        out = []
+        for x in xs:
+            if isinstance(x, tuple):
+                out += [("gd#%d" % k, x[1], x[2]) for k in range(16)] if x[0] == "gd" else [x]
+        return out
 
     def ts(out, in0, s1, o0, s2=None, o1=None, idx=None, step=None):
         i = ap(in0) if idx is None else ap(in0).indirect(ap(idx))
@@ -148,28 +170,29 @@ def rank_program(g, core, T, topo):
             f = lambda: g.vector.tensor_scalar(o, i, sc(s1), None, o0)
         else:
             f = lambda: g.vector.tensor_scalar(o, i, sc(s1), sc(s2), o0, o1)
-        op("V", f, regs(in0, s1, s2, idx), [out])
+        op("V", f, regs(in0, s1, s2, idx), regs(out))
 
-    def tt(out, in0, in1, o, oidx=None):
+    def tt(out, in0, in1, o, idx=None, oidx=None):
+        i = ap(in0) if idx is None else ap(in0).indirect(ap(idx))
         oo = ap(out) if oidx is None else ap(out).indirect(ap(oidx))
-        op("V", lambda: g.vector.tensor_tensor(oo, ap(in0), ap(in1), o), regs(in0, in1, oidx), [out])
+        op("V", lambda: g.vector.tensor_tensor(oo, i, ap(in1), o), regs(in0, in1, idx, oidx), regs(out))
 
     def cp(out, in_, idx=None, oidx=None):
         i = ap(in_) if idx is None else ap(in_).indirect(ap(idx))
         o = ap(out) if oidx is None else ap(out).indirect(ap(oidx))
-        op("V", lambda: g.vector.tensor_copy(o, i), regs(in_, idx, oidx), [out])
+        op("V", lambda: g.vector.tensor_copy(o, i), regs(in_, idx, oidx), regs(out))
 
     def ms(out, c):
-        op("V", lambda: g.vector.memset(ap(out), c), [], [out])
+        op("V", lambda: g.vector.memset(ap(out), c), [], regs(out))
 
     def act(out, in_, scale=1.0, idx=None):
         i = ap(in_) if idx is None else ap(in_).indirect(ap(idx))
         op("S", lambda: g.scalar.activation(ap(out), i, ACT.Identity, scale=sc(scale)),
-           regs(in_, idx, scale), [out])
+           regs(in_, idx, scale), regs(out))
 
     def mm(out, lhsT, rhs, start, stop, step=None):
         r = ap(rhs) if step is None else T[rhs[0]][:, rhs[1]:rhs[2]:step]
-        op("P", lambda: g.tensor.matmul(ap(out), ap(lhsT), r, start, stop), [lhsT, rhs], [out])
+        op("P", lambda: g.tensor.matmul(ap(out), ap(lhsT), r, start, stop), regs(lhsT, rhs), [out])
 
     def iota(out, pattern, base, cm):
         if SCRATCH[out[0]][2] == I32:
@@ -178,7 +201,7 @@ def rank_program(g, core, T, topo):
             f = lambda: g.iota(ap(out), pattern, base, cm, allow_small_or_imprecise_dtypes=True)
         op("G", f, [], [out])
 
-    def remote(transfers, lsem, reads, waits, alone=True):
+    def remote(transfers, lsem, reads, waits):
         before("G", reads, [])
         for tok in waits:
             wait("G", tok)
@@ -192,9 +215,8 @@ def rank_program(g, core, T, topo):
                                          srcs=[ap(s) for s in srcs], dsts=[ap(d)], alu_op=alu))
             n += len(engs)
         g.remote_dma_fused(trs, local_sem=T.sem[lsem])
-        if alone:
-            note("D", reads, [], (lsem, n))
-            total[lsem] = n
+        note("D", reads, [], (lsem, n))
+        total[lsem] = n
         return n
 
     mate = partner_of(T, topo, core)
@@ -202,29 +224,53 @@ def rank_program(g, core, T, topo):
     WB = ("wa", "wb", "wc", "wa")
     LB = ("la", "lb", "lc", "la")
     NT = [L0 + CAP * t for t in range(RO + 1)]
-    V0 = [[sum(CHUNKS[t][:c]) for c in range(3)] for t in range(RO)]
+    V0 = [[sum(ch[:c]) for c in range(len(ch))] for ch in CHUNKS]
+    BK = [BANKS[len(ch)] for ch in CHUNKS]
     RLO = {w: sum(x // 16 for x in WIDTHS[:i]) for i, w in enumerate(WIDTHS)}
-    FOLD_MAX, FOLD_MIN = NV_MAX < 16, NV_MIN < 16
     PM, PG, PAR, PG16, WGT = (R("col", i, i + 1) for i in (0, 1, 2, 3, 4))
-    RM = [R("col", 8 + t, 9 + t) for t in range(3)]
-    NRM = [R("col", 12 + t, 13 + t) for t in range(3)]
-    NC_ = [R("col", 16 + t, 17 + t) for t in range(4)]
+    RM = [R("col", 8 + t, 9 + t) for t in range(RO)]
+    NRM = [R("col", 12 + t, 13 + t) for t in range(RO)]
+    NC_ = [R("col", 16 + t, 17 + t) for t in range(RO + 1)]
     PARC = R("col", 20, 21)
+    RM8 = [R("col", 24 + t, 25 + t) for t in range(RO)]
+    ID1, IDQ, IDN, IDB = (R(b, 0, 128) for b in ("id1", "idq", "idn", "idb"))
+    ONES = R("ones", 0, 128)
+    ML = [R("ml", 12 * t, 12 * t + 12) for t in range(RO)]
+    TL = [None, ML[0], R("ml", 36, 48)]
+    CL = [R("cl", 12 * t, 12 * t + 12) for t in range(RO)]
 
     def own(b, lo, hi):
-        return R(b, GH + lo, GH + hi)
+        return R(b, O0 + lo, O0 + hi)
 
-    def P(t, c, k, n=1):
+    def upto(b, n):
+        return R(b, 0, O0 + n)
+
+    def places(b, n):
+        return R(b, SP, O0 + n)
+
+    def cells(t, c):
+        return V0[t][c], V0[t][c] + CHUNKS[t][c]
+
+    def twins(t):
+        return NP[t], NP[t] + CAP
+
+    def folded(t, c):
+        return max(0, min(CHUNKS[t][c], FOLDED[t] - V0[t][c]))
+
+    def bank(t, kind, c, lo=0, hi=None):
+        return R(BK[t][kind][c], lo, CHUNKS[t][c] if hi is None else hi)
+
+    def P(t, c, k, n=1, lo=0, hi=None):
         C = CHUNKS[t][c]
         o = 16 * V0[t][c] + k * C
-        return R("pp", o, o + n * C)
+        return R("pp", o + lo, o + (n * C if hi is None else hi))
 
     def LT(t, c, k, n):
         Wc = CHUNKS[t][c] // 16
         o = V0[t][c] + k * Wc
         return R("lt%d" % (t % 2), o, o + n * Wc)
 
-    def send_ghosts(t):
+    def send_ghosts(t, src):
         trs, per = [], 0
         for d in range(len(OFF)):
             dst = T.cores[(rank - OFF[d]) % N]
@@ -234,11 +280,16 @@ def rank_program(g, core, T, topo):
             if t == 0:
                 mine = mine[::per // GHOST0_ENGINES]
             per = len(mine)
-            trs.append((dst, mine, "ga%d" % t, [own(WB[t], 0, 128)], R(WB[t], 128 * d, 128 * d + 128), 0))
-        remote(trs, "gl%d" % t, [own(WB[t], 0, 128)], [])
-        note("X", [], [R(WB[t], 0, GH)], ("ga%d" % t, per * len(OFF)))
+            trs.append((dst, mine, "ga%d" % t, [src], R(WB[t], SP + 128 * d, SP + 128 * d + 128), 0))
+        remote(trs, "gl%d" % t, [src], [])
+        note("X", [], [R(WB[t], SP, O0)], ("ga%d" % t, per * len(OFF)))
+
+    made = []
 
     def relayout_consts(C):
+        if C in made:
+            return
+        made.append(C)
         Wc = C // 16
         kf, ki, j = R("kf", 0, Wc), R("ki", 0, Wc), R("jj", 0, Wc)
         ts(kf, j, 1.0 / Wc, A.mult, 0.5 / Wc - 0.5, A.add)
@@ -251,203 +302,207 @@ def rank_program(g, core, T, topo):
 
     def relayout(t, c):
         C, v0 = CHUNKS[t][c], V0[t][c]
+        relayout_consts(C)
         a, b = own(LB[t], v0, v0 + C), own(LB[t], v0 - 16, v0 + C + 16)
         o1, o2 = R("tt", 0, C), R("tt", C, 2 * C + 32)
         op("V", lambda: g.vector.transpose(ap(o1), ap(a)), [a], [o1])
         op("V", lambda: g.vector.transpose(ap(o2), ap(b)), [b], [o2])
         cp(LT(t, c, 0, 16), R("tt", 0, 2 * C + 32), idx=R("rl", RLO[C], RLO[C] + C // 16))
 
-    def copy_c(t, c):
-        C, v0 = CHUNKS[t][c], V0[t][c]
-        mm(R("c%d" % c, 0, C), R("idq", 0, 128), own(WB[t], v0, v0 + C), True, True)
+    def copy_x(t, c, kind="x", stop=True):
+        mm(bank(t, kind, c), ID1, own(WB[t], *cells(t, c)), True, stop)
 
-    def copy_x(t, c):
-        C, v0 = CHUNKS[t][c], V0[t][c]
-        mm(R("y0", 0, C), R("id1", 0, 128), own(WB[t], v0, v0 + C), True, True)
-
-    def gather_a(t, c, grp):
-        k0, n, q = grp
-        w = R(WB[t], 0, GH + NT[t])
-        if q == "S":
-            act(P(t, c, k0, n), w, 0.25, idx=LT(t, c, k0, n))
-        else:
-            ts(P(t, c, k0, n), w, 0.25, A.mult, idx=LT(t, c, k0, n))
+    def gather_a(t, c):
+        for k0, n in (FIRST_GROUPS if c == 0 else GROUPS):
+            (cp if c == 0 and k0 in A_ON_V[t] else act)(P(t, c, k0, n), places(WB[t], NT[t]), idx=LT(t, c, k0, n))
 
     slot = [0]
 
-    def gather_b(t, c, grp):
-        k0, n, q = grp
-        C, v0 = CHUNKS[t][c], V0[t][c]
-        if slot[0] + n * C > RING:
-            slot[0] = 0
-        o = slot[0]
-        slot[0] += n * C
-        w = R(LB[t], 0, GH + NT[t])
-        if q == "S":
-            act(R("gr", o, o + n * C), w, 1.0, idx=LT(t, c, k0, n))
+    def gather_b(t, c, grp, ring=False):
+        k0, n = grp
+        C, v0 = CHUNKS[t][c], O0 + V0[t][c]
+        if c == 0 and not ring:
+            b, o = P(t, c, k0, n)[:2]
         else:
-            cp(R("gr", o, o + n * C), w, idx=LT(t, c, k0, n))
-        dmas("Y", [(T.gd[k0 + i:128:16, v0:v0 + C], T.gr[k0 + i:128:16, o + i * C:o + (i + 1) * C],
-                    [R("gr", o + i * C, o + (i + 1) * C)], [R("gd#%d" % (k0 + i), v0, v0 + C)]) for i in range(n)])
+            if slot[0] + n * C > RING:
+                slot[0] = 0
+            b, o = "gr", slot[0]
+            slot[0] += n * C
+        act(R(b, o, o + n * C), places(LB[t], NT[t]), idx=LT(t, c, k0, n))
+        dmas("Y", [(T.gd[k0 + i:128:16, v0:v0 + C], T[b][k0 + i:128:16, o + i * C:o + (i + 1) * C],
+                    [R(b, o + i * C, o + (i + 1) * C)], [R("gd#%d" % (k0 + i), v0, v0 + C)]) for i in range(n)])
 
     cslot = [0]
 
-    def acc(t, c, k, nv, bank, o):
-        if k <= 16 - nv:
-            return
-        C, v0 = CHUNKS[t][c], V0[t][c]
-        out = own(WB[t + 1], v0, v0 + C) if (k == 15 and nv < 16) else R(bank, 0, C)
-        tt(out, P(t, c, k), P(t, c, k - 1) if k == 17 - nv else R(bank, 0, C), o)
+    def least(t, c):
+        return R(BK[t]["z"], 0, CHUNKS[t][c] - folded(t, c))
 
     def compare(t, c, k):
         C = CHUNKS[t][c]
-        s = R("cmp", 512 * (cslot[0] % 4), 512 * (cslot[0] % 4) + C)
-        cslot[0] += 1
-        tt(s, P(t, c, k), R("c%d" % c, 0, C), A.is_gt)
-        mm(R("n%d" % c, 0, C), R("sb", 15 - k, 143 - k), s, k == 0, k == 15)
-        acc(t, c, k, NV_MIN, "y1", A.min)
-        acc(t, c, k, NV_MAX, "y0", A.max)
+        if cslot[0] + C > CS * 512:
+            cslot[0] = 0
+        s = R("cmp", cslot[0], cslot[0] + C)
+        cslot[0] += C
+        tt(s, P(t, c, k), bank(t, "x", c), A.is_gt)
+        mm(bank(t, "n", c), R("sb", 15 - k, 143 - k), s, k == 0, k == 15)
 
-    def after_compare(t, c):
-        C, v0 = CHUNKS[t][c], V0[t][c]
-        if not FOLD_MAX:
-            tt(own(WB[t + 1], v0, v0 + C), own(WB[t], v0, v0 + C), R("y0", 0, C), A.add)
-        if not FOLD_MIN:
-            tt(R("c%d" % c, 0, C), own(WB[t], v0, v0 + C), R("y1", 0, C), A.mult)
+    def running(t, c, k):
+        C, y = CHUNKS[t][c], bank(t, "y", c)
+        tt(own(WB[t + 1], *cells(t, c)) if k == 15 else y, P(t, c, k), y, A.max)
+        if folded(t, c) < C:
+            tt(least(t, c), P(t, c, k, 1, folded(t, c), C), least(t, c), A.min)
 
-    def fold(t, c):
-        C, v0, i = CHUNKS[t][c], V0[t][c], 3 * t + c
-        jobs = []
-        if FOLD_MIN:
-            jobs.append((NV_MIN, "zl", 3))
-        if FOLD_MAX:
-            jobs.append((NV_MAX, "yl", 2))
-        if not jobs:
-            return
-        n, reads = 0, []
-        for nv, land, alu in jobs:
-            srcs = [P(t, c, k) for k in range(16 - nv)]
-            n += remote([(mate, mate_engs, "fa%d" % i, srcs, R(land, v0, v0 + C), alu)], "fl%d" % i, srcs, [], False)
-            reads += srcs
-        note("D", reads, [], ("fl%d" % i, n))
-        arrived[i] = n
-        total["fa%d" % i] = n
+    def lands(t, c):
+        v0, n = V0[t][c], folded(t, c)
+        if c < len(HEAD) and HEAD[c]:
+            return [(0, HEAD[c], R("zh", v0, v0 + n)), (HEAD[c], 16 - HEAD[c], R("zl", v0, v0 + n))]
+        return [(0, 16, R("zl", v0, v0 + n))]
 
-    arrived = {}
+    def fold(t, c, amid=None):
+        i = 3 * t + c
+        total["fa%d" % i] = 0
+        for j, (k0, n, land) in enumerate(lands(t, c)):
+            if amid and j == len(lands(t, c)) - 1:
+                amid()
+            srcs = [P(t, c, k, 1, 0, folded(t, c)) for k in range(k0, k0 + n)]
+            total["fa%d" % i] += remote([(mate, mate_engs, "fa%d" % i, srcs, land, 3)],
+                                        ("fl%d" % i, "fh%d" % i)[j], srcs, [])
 
     def back(t, c):
-        C, v0, i = CHUNKS[t][c], V0[t][c], 3 * t + c
-        if i not in arrived:
-            return
-        jobs = ([("zl", "zr")] if FOLD_MIN else []) + ([("yl", "yr")] if FOLD_MAX else [])
-        h = len(mate_engs) // len(jobs)
-        trs = [(mate, mate_engs[j * h:(j + 1) * h], "ra%d" % i, [R(a, v0, v0 + C)], R(b, v0, v0 + C), 0)
-               for j, (a, b) in enumerate(jobs)]
-        remote(trs, "rl%d" % i, [], [("fa%d" % i, arrived[i])])
-        note("X", [], [R(b, v0, v0 + C) for a, b in jobs], ("ra%d" % i, h * len(jobs)))
+        i = 3 * t + c
+        srcs = [x[2] for x in lands(t, c)]
+        z = R("zr", V0[t][c], V0[t][c] + folded(t, c))
+        n = remote([(mate, mate_engs, "ra%d" % i, srcs, z, 3 if len(srcs) > 1 else 0)],
+                   "rl%d" % i, [], [("fa%d" % i, total["fa%d" % i])])
+        note("X", [], [z], ("ra%d" % i, n))
+
+    def sum_a(t, c):
+        if BK[t]["d"][c] == BK[t]["y"][c]:
+            copy_x(t, c, "d", False)
+        mm(bank(t, "d", c), IDQ, own(WB[t + 1], *cells(t, c)), False, False)
+
+    voted, counted = [], []
+
+    def counts(t, lo, hi):
+        voted.append((lo, hi))
+        for cb in range(-(-NT[t] // 128)):
+            a, b = 128 * cb, min(128 * cb + 128, NT[t])
+            if cb not in counted and sum(max(0, min(b, y) - max(a, x)) for x, y in voted) == b - a:
+                counted.append(cb)
+                mm(R(BK[t]["m"], cb, cb + 1), own("vote", a, a + 128), R("ones", 0, 1), True, True)
 
     def update_steps(t, c):
-        C, v0 = CHUNKS[t][c], V0[t][c]
-        bank, xn = R("c%d" % c, 0, C), own(WB[t + 1], v0, v0 + C)
-        st = []
-        if FOLD_MIN:
-            st.append(lambda: tt(bank, R("zr", v0, v0 + C), bank, A.mult))
-        if FOLD_MAX:
-            def a_step():
-                tt(xn, xn if NV_MAX else R("yr", v0, v0 + C), R("y0", 0, C), A.add)
-                if c < 2:
-                    copy_x(t, c + 1)
-            if NV_MAX:
-                st.insert(0, lambda: tt(xn, xn, R("yr", v0, v0 + C), A.max))
-            st.append(a_step)
-        st.append(lambda: ts(bank, bank, 12.0 if FOLD_MIN else 3.0, A.mult))
-        st.append(lambda: tt(bank, xn, bank, A.subtract))
+        span, n = cells(t, c), folded(t, c)
+        z, d, xn = R("zr", *span), bank(t, "d", c), own(WB[t + 1], *span)
 
-        def vote_step():
-            ts(R("vote", v0, v0 + C), bank, 1.0, A.is_gt)
-            lo = -(-v0 // 128) if v0 % 128 == 0 else v0 // 128
-            hi = (v0 + C) // 128 if c < 2 else -(-(v0 + C) // 128)
-            for cb in range(lo, hi):
-                mm(R("y1", cb, cb + 1), R("vote", 128 * cb, 128 * cb + 128), R("ones", 0, 1), True, True)
-        st.append(vote_step)
-        st.append(lambda: ts(xn, bank, 0.0, A.max, 2.0, A.min))
-        return st
+        def product():
+            if span[0] + n < span[1]:
+                tt(R("zr", span[0] + n, span[1]), own(WB[t], span[0] + n, span[1]), least(t, c), A.mult)
+            if n:
+                tt(R("zr", span[0], span[0] + n), R("zr", span[0], span[0] + n), bank(t, "x", c, 0, n), A.mult)
 
-    def keep_step(t, c):
-        C, v0 = CHUNKS[t][c], V0[t][c]
-        return lambda: tt(own(LB[t + 1], v0, v0 + C), own(LB[t], v0, v0 + C), R("n%d" % c, 0, C), A.min)
+        def scale():
+            ts(z, z, 0.75, A.mult)
+            mm(d, IDN, z, False, True)
 
-    def move_step(t, c):
-        C, v0 = CHUNKS[t][c], V0[t][c]
-        bank = R("n%d" % c, 0, C)
+        def vote():
+            ts(own("vote", *span), d, 1.0, A.is_gt)
+            counts(t, *span)
+        return [product, scale, vote, lambda: ts(xn, d, 0.0, A.max, 2.0, A.min)]
 
-        def f():
-            rd = [R("gd#%d" % k, v0, v0 + C) for k in range(16)] + [bank]
-            op("V", lambda: g.vector.tensor_tensor(ap(bank), T.gd[:, v0:v0 + C], ap(bank), A.subtract), rd, [bank])
-        return f
+    def ghost_steps(t):
+        f = R(BK[t]["m"], 128, 256)
 
-    def join_step(t, c):
-        C, v0 = CHUNKS[t][c], V0[t][c]
-        o = own(LB[t + 1], v0, v0 + C)
-        return lambda: tt(o, o, R("n%d" % c, 0, C), A.max)
+        def factor():
+            mm(f, ONES, own("vote", 0, 128), True, True)
+            ts(f, f, float(H), A.is_lt, 0.5, A.max)
+
+        def send():
+            tt(R("gs", 0, 128), own(WB[t + 1], 0, 128), f, A.mult)
+            send_ghosts(t + 1, R("gs", 0, 128))
+        return [factor, send]
+
+    def keep(t, c):
+        span = cells(t, c)
+        tt(own(LB[t + 1], *span), own(LB[t], *span), bank(t, "n", c), A.min)
+
+    def link_span(t, c):
+        return cells(t, c) if c < len(CHUNKS[t]) else twins(t)
+
+    def join_sum(t, c, parts=(0, 1)):
+        span = link_span(t, c)
+        b = bank(t, "j", c, 0, span[1] - span[0])
+        if 0 in parts:
+            mm(b, IDB, own(LB[t + 1], *span), True, False)
+        if 1 in parts:
+            mm(b, ID1, own("gd", *span), False, True)
+
+    def join(t, c):
+        span = link_span(t, c)
+        o = own(LB[t + 1], *span)
+        tt(o, o, bank(t, "j", c, 0, span[1] - span[0]), A.max)
+
+    def mothers(win, first, s, tmp, out):
+        for i in range(16):
+            mm(s, R("wb16", 15 - i, 143 - i), R(win, first + i, first + CAP), i == 0, i == 15, step=16)
+        return [lambda: tt(tmp, R("jj", 0, 12), s, A.max), lambda: cp(out, tmp)]
 
     def division_steps(t):
-        nb = -(-NT[t] // 128)
+        nb, MB = -(-NT[t] // 128), BK[t]["m"]
         r, rin = R("rr", 0, nb), R("rin", 0, nb)
-        q, pf, lm = R("sm", 0, nb), R("sm", 16, 16 + nb), R("sm", 32, 44)
-        s = R("y1", 16, 16 + nb)
+        q, pf = R("sm", 0, nb), R("sm", 16, 16 + nb)
+        s = R(MB, 16, 16 + nb)
+        rest = []
 
         def scan():
             op("V", lambda: g.vector.tensor_tensor_scan(ap(rin), ap(R("ones", 0, nb)), ap(r), 0.0, A.mult, A.add),
                [r, R("ones", 0, nb)], [rin])
-            mm(s, R("ones", 0, 128), rin, True, False)
+            mm(s, ONES, rin, True, False)
             mm(s, R("negu", 0, 128), r, False, True)
-            mm(R("y1", 32, 33), R("ones", 0, 128), R("rin", nb - 1, nb), True, True)
+            mm(R(MB, 32, 33), ONES, R("rin", nb - 1, nb), True, True)
 
         def scatter():
             cp(R("win", 0, 1600), R("val", 0, 16 * nb), oidx=R("pos", 0, nb))
-            for i in range(16):
-                mm(R("y1", 48, 60), R("wb16", 15 - i, 143 - i), R("win", 1 + i, 193), i == 0, i == 15, step=16)
-        return [lambda: ts(r, R("y1", 0, nb), float(H), A.is_ge),
+            rest.extend(mothers("win", 1, R(MB, 48, 60), R("sm", 32, 44), ML[t]))
+        return [lambda: ts(r, R(MB, 0, nb), float(H), A.is_ge),
                 scan,
                 lambda: ts(q, r, -BIG, A.mult),
                 lambda: tt(q, q, R("dd", 0, nb), A.add),
                 lambda: tt(pf, q, s, A.max),
-                lambda: ts(NC_[t + 1], R("y1", 32, 33), float(CAP), A.min, NC_[t], A.add),
                 lambda: cp(R("pos", 0, nb), pf),
                 scatter,
-                lambda: tt(lm, R("dump", 0, 12), R("y1", 48, 60), A.min),
-                lambda: ts(R("ml", 0, 12), lm, BIG, A.add)]
+                lambda: rest[0](),
+                lambda: rest[1](),
+                lambda: ts(NC_[t + 1], R(MB, 32, 33), float(CAP), A.min, NC_[t], A.add)]
+
+    def twin_list():
+        a, m = R("sm", 48, 60), R("sm", 64, 76)
+        ts(a, R("jj", 0, 12), NC_[1], A.subtract, float(CAP + 1), A.add)
+        ts(m, a, float(CAP), A.is_le)
+        tt(a, a, m, A.mult)
+        cp(R("si", 0, 12), a)
+        cp(R("win2", 0, CAP), R("win", 0, 208), idx=R("si", 0, 12))
+        return mothers("win2", 0, R("y1", 0, 12), a, TL[2])
 
     def round_consts(t):
         ms(R("win", 0, 208), 0.0)
-        ts(R("t2", 0, CAP), R("pl", L0, L0 + CAP), NC_[t], A.add, RM[t], A.mult)
+        ts(R("t2", 0, CAP), own("pl", L0, L0 + CAP), NC_[t], A.add, RM[t], A.mult)
         if t > 0:
-            ts(R("cl", 0, 12), R("jj", 0, 12), NC_[t], A.add)
-        if t == RO - 1:
-            ts(R("ex", 0, NT[t] - L0), R("pl", L0, NT[t]), float(GH + L0), A.subtract, NC_[t], A.is_lt)
+            ts(CL[t], R("jj", 0, 12), NC_[t], A.add)
 
-    ML, CL = R("ml", 0, 12), R("cl", 0, 12)
-
-    def children(t, buf, a, b):
-        if t == 0:
-            o = own(buf, L0, L0 + CAP)
-            cp(o, a) if b is None else tt(o, a, b, A.add)
-        elif b is None:
-            cp(own(buf, L0, OWN), a, oidx=CL)
-        else:
-            tt(own(buf, L0, OWN), a, b, A.add, oidx=CL)
+    def twin_places(t):
+        act(R("tw", 0, CAP), upto("pl", LM), RM8[t - 1], idx=TL[t])
+        return lambda: tt(R("tw", 0, CAP), R("tw", 0, CAP), own("pl", *twins(t)), A.min)
 
     def child_links(t):
-        ts(R("lk", 0, CAP), own(LB[t + 1], 0, OWN), NRM[t], A.mult, idx=ML)
-        return lambda: children(t, LB[t + 1], R("lk", 0, CAP), R("t1", 0, CAP))
+        if t == 0:
+            tt(own(LB[1], L0, L0 + CAP), R("lk", 0, CAP), R("t1", 0, CAP), A.add)
+        else:
+            tt(own(LB[t + 1], L0, NT[t + 1]), R("lk", 0, CAP), R("t1", 0, CAP), A.add, oidx=CL[t])
 
-    def weave(*lists):
-        lists = [list(x) for x in lists]
-        while any(lists):
-            for x in lists:
-                if x:
-                    x.pop(0)()
+    def run(steps):
+        for f in steps:
+            f()
 
     C0 = CHUNKS[0][0]
     dmas("Y", [(ap(own("wa", 0, 128)), T.x0[:, 0:128], [], [own("wa", 0, 128)])])
@@ -456,13 +511,13 @@ def rank_program(g, core, T, topo):
     dmas("S", [(ap(R("nbi", C0 + 16, L0)), T.nb[:, C0 + 16:L0], [], [R("nbi", C0 + 16, L0)])])
     iota(R("ip", 0, 1), [[1, 1]], 0, 1)
     iota(R("iot", 0, 32), [[16, 32]], 0, 0)
-    ms(R("idq", 0, 128), 0.25)
-    ms(own("wb", L0, OWN), 0.0)
-    iota(R("la", GH - 16, GH), [[1, 16]], GH - 16, 0)
-    op("G", lambda: g.affine_select(T.idq[:], T.idq[:], [[-1, 128]], A.is_equal, 0.0, 0, 1),
-       [R("idq", 0, 128)], [R("idq", 0, 128)])
-    send_ghosts(0)
-    iota(R("la", 0, GH - 16), [[1, GH - 16]], 0, 0)
+    ms(ID1, 1.0)
+    zer = R("gd", 0, O0)
+    ms(zer, 0.0)
+    iota(R("la", O0 - 16, O0), [[1, 16]], GH - 16, 0)
+    op("G", lambda: g.affine_select(T.id1[:], T.id1[:], [[-1, 128]], A.is_equal, 0.0, 0, 1), [ID1], [ID1])
+    send_ghosts(0, own("wa", 0, 128))
+    iota(R("la", SP, O0 - 16), [[1, GH - 16]], 0, 0)
     ts(R("ip", 1, 2), R("ip", 0, 1), 15, A.bitwise_and)
     ts(R("ip", 2, 3), R("ip", 0, 1), 4, A.arith_shift_right)
     ts(R("ip", 4, 5), R("ip", 0, 1), 112, A.bitwise_and)
@@ -477,146 +532,189 @@ def rank_program(g, core, T, topo):
     relayout(0, 0)
     cp(own("la", C0 + 16, L0), R("nbi", C0 + 16, L0))
     ts(R("sb", 15, 143), R("iot", 0, 8), PG16, A.is_equal, BIG, A.mult, step=16)
-    zer = own("wb", L0, OWN)
-    for b, lo in (("lb", L0), ("wc", NT[1]), ("lc", NT[1]), ("wa", NT[2]), ("la", NT[2])):
-        act(own(b, lo, OWN), R("wb", GH + lo, GH + OWN))
-    act(R("pl", LM, OWN), own("wb", LM, OWN))
-    copy_c(0, 0)
+    for b in WB[:3] + LB[:3] + ("pl",):
+        act(R(b, 0, SP), R("gd", 0, SP))
+    for r in (own("wc", NT[1], NT[2]), own("lc", NT[1], NT[2]), own("wa", NT[2], LM), own("la", NT[2], LM)):
+        act(r, R("gd", 0, CAP))
+    act(own("lb", L0, L0 + 16), R("gd", 0, 16))
+    act(R("vote", 0, O0), zer)
+    copy_x(0, 0)
+
+    def late_fills():
+        act(own("vote", NT[1], NT[1] + 64), R("gd", 0, 64))
+        act(IDQ, ID1, 0.25)
+        act(IDN, ID1, -1.0)
+        act(IDB, ID1, -BIG)
 
     def late_consts():
-        iota(R("xc", 0, 176), [[8, 11], [0, 16]], -256, 0)
+        iota(R("xc", 0, 176), [[8, 11], [0, 16]], O0 // 16, 0)
         iota(R("lk", 0, 176), [[0, 11], [1, 16]], 0, 0)
         ms(R("negu", 0, 128), -1.0)
-        ms(R("ones", 0, 128), 1.0)
+        ms(ONES, 1.0)
         op("G", lambda: g.affine_select(T.negu[:], T.negu[:], [[-1, 128]], A.is_gt, 0.0, 0, 1),
            [R("negu", 0, 128)], [R("negu", 0, 128)])
-        iota(R("pl", 0, LM), [[1, LM]], GH, 0)
+        iota(places("pl", LM), [[1, GH + LM]], 0, 0)
         ts(R("col", 8, 11), R("iot", 0, 3), 1.0 / 16, A.mult, PM, A.is_equal)
         ms(R("wb16", 0, 144), 0.0)
         ts(R("col", 12, 15), R("col", 8, 11), -1.0, A.mult, 1.0, A.add)
+        ts(R("col", 24, 27), R("col", 8, 11), 8.0, A.mult)
         ts(WGT, RM[0], 16.0, A.mult, RM[1], A.add)
         ts(R("xc", 0, 176), R("xc", 0, 176), PG, A.add, RM[0], A.mult)
         ts(R("lk", 0, 176), R("lk", 0, 176), RM[1], A.mult)
         ts(R("wb16", 15, 143), R("iot", 0, 8), 0.0, A.mult, WGT, A.add, step=16)
         tt(R("val", 0, 176), R("xc", 0, 176), R("lk", 0, 176), A.add)
         ts(R("dd", 0, 12), R("jj", 0, 12), float(NMAX + 1), A.add)
-        ts(R("dump", 0, 12), R("jj", 0, 12), LM - BIG, A.add)
         ms(NC_[0], 0.0)
-        ms(R("vote", NT[1], NT[1] + 64), 0.0)
-        if FOLD_MAX:
-            ts(R("id1", 0, 128), R("idq", 0, 128), 4.0, A.mult)
 
-    carry = []
+    carry, between = {}, []
     for t in range(RO):
-        last = t == RO - 1
-        bq = [(c, grp) for c in range(3) for grp in B_GROUPS]
+        last, K = t == RO - 1, len(CHUNKS[t])
+        del voted[:], counted[:]
+        bq = [(c, grp) for c in range(K) for grp in GROUPS]
         if t == 0:
             for c, grp in bq[:B_FIRST]:
-                gather_b(t, c, grp)
+                gather_b(t, c, grp, True)
             bq = bq[B_FIRST:]
-            late_consts()
-            made = [C0]
-
-            def lists_for(C):
-                if C not in made:
-                    made.append(C)
-                    relayout_consts(C)
-            lists_for(CHUNKS[0][1])
+            late_fills()
             relayout(0, 1)
-            lists_for(CHUNKS[0][2])
-            carry = [lambda: relayout(0, 2), lambda: [lists_for(C) for C in WIDTHS]]
-            iota(R("lb", 0, GH), [[1, GH]], 0, 0)
-        for c in range(3):
-            for gi, grp in enumerate(A_GROUPS):
-                gather_a(t, c, grp)
-                if c == 0 and gi == 0:
-                    copy_c(t, 1)
-                    copy_c(t, 2)
-                    for f in carry[:CARRY_FIRST]:
-                        f()
-                    carry = carry[CARRY_FIRST:]
-                for k in range(grp[0], grp[0] + grp[1]):
+            late_consts()
+            for C in WIDTHS:
+                relayout_consts(C)
+            iota(R("lb", SP, O0), [[1, GH]], 0, 0)
+            iota(R("lc", SP, O0), [[1, GH]], 0, 0)
+            carry = {3: [lambda: round_consts(0)]}
+        held = 0 if last else B_HELD
+        up = [update_steps(t, c) for c in range(K)]
+        extra = {(0, k): carry[k] for k in carry}
+
+        def at(place, f):
+            extra[place] = extra.get(place, []) + [f]
+
+        def later_gathers():
+            run(between)
+            for c in range(1, K):
+                gather_a(t, c)
+            fold(t, 1, lambda: back(t, 0))
+            if K == 3 and folded(t, 2):
+                fold(t, 2, lambda: back(t, 1))
+                back(t, 2)
+            else:
+                back(t, 1)
+            if t > 0:
+                at((K - 1, TWIN_AT), twin_places(t))
+        gather_a(t, 0)
+        fold(t, 0)
+        at((0, NEXT_AT), later_gathers)
+        at((1, 0), lambda: [gather_b(t, c, grp) for c, grp in bq[:len(bq) - held]])
+        for c in range(1, K):
+            at((c - 1, X_AT), lambda c=c: copy_x(t, c))
+            at((c - 1, NEXT_AT), lambda c=c: mm(bank(t, "y", c), ID1, P(t, c, 0), True, True))
+            at((c, 0), lambda c=c: sum_a(t, c - 1))
+        at((K - 1, D_AT), lambda: copy_x(t, K - 1, "d", False))
+        if K == 3:
+            at((2, 11), lambda: join_sum(t, 1, (0,)))
+        for c in range(K - 1):
+            for place, f in zip(UPD_AT[K][c], up[c] + ([] if last else ghost_steps(t))):
+                at(place, f)
+        for part, place in enumerate(JOIN_AT[K]):
+            at(place, lambda part=part: join_sum(t, 0, (part,)))
+        run(extra.get((0, -1), []))
+        mm(bank(t, "y", 0), ID1, P(t, 0, 0), True, True)
+        for c in range(K):
+            if folded(t, c) < CHUNKS[t][c]:
+                mm(least(t, c), ID1, P(t, c, 0, 1, folded(t, c), CHUNKS[t][c]), True, True)
+            for k in range(16):
+                if c < K - 1 or k < 16 - sum(DEFER):
                     compare(t, c, k)
-                if c == 0 and carry:
-                    carry.pop(0)()
-            while carry:
-                carry.pop(0)()
-            after_compare(t, c)
-            fold(t, c)
-            if c > 0:
-                back(t, c - 1)
-            nb_ = max(0, sum(B_AFTER[:c + 1]) - (3 * len(B_GROUPS) - len(bq)))
-            for cb, grp in bq[:nb_]:
-                gather_b(t, cb, grp)
-            bq = bq[nb_:]
-            if t == 0 and c == 0:
-                iota(R("lc", 0, GH), [[1, GH]], 0, 0)
-        back(t, 2)
-        if FOLD_MAX:
-            copy_x(t, 0)
-        nxt = 0 if last else (1 if V0[t][1] >= CHUNKS[t + 1][0] else 2)
-        vb = [x for x in bq if x[1][2] == "V"]
-        early = [x for x in bq if x[0] < 2]
-        for c, grp in early:
-            gather_b(t, c, grp)
-        up = [update_steps(t, c) for c in range(3)]
-        weave(up[0][:-1], [keep_step(t, c) for c in range(3)] + [lambda: round_consts(t)])
-        weave(up[1][:-1], up[2][:-1])
-        fill = [up[0][-1], up[1][-1], up[2][-1], move_step(t, 0)]
-        if last:
-            o = own(WB[t + 1], L0, NT[t])
-            fill.append(lambda: tt(o, o, R("ex", 0, NT[t] - L0), A.mult))
-        fill.append(join_step(t, 0))
-        dv = division_steps(t)
-        for i, f in enumerate(dv):
+                if k - LAG[c] >= 1:
+                    running(t, c, k - LAG[c])
+                run(extra.get((c, k), []))
+            for k in range(16 - LAG[c], 16):
+                running(t, c, k)
+            if c < K - 1:
+                keep(t, c)
+        wn, ln = WB[t + 1], LB[t + 1]
+        sum_a(t, K - 1)
+        late = list(range(16 - sum(DEFER), 16))
+
+        def deferred(n):
+            for k in late[:n]:
+                compare(t, K - 1, k)
+            del late[:n]
+        run(up[K - 1][:2])
+        deferred(DEFER[0])
+        up[K - 1][2]()
+        if t > 0:
+            cp(own("vote", *twins(t)), upto("vote", NP[t]), idx=TL[t])
+            counts(t, *twins(t))
+        deferred(DEFER[1])
+        for i, f in enumerate(division_steps(t)):
             f()
-            if i in (0, 1, 4, 6):
-                fill.pop(0)()
-            if i == 7:
-                while fill:
-                    fill.pop(0)()
-        wn, ln = own(WB[t + 1], 0, OWN), own(LB[t + 1], 0, OWN)
-        ts(R("xc", 0, CAP), wn, 0.5, A.mult, idx=ML)
-        cp(R("bg", 0, CAP), ln, idx=ML)
-        cp(wn, R("xc", 0, CAP), oidx=ML)
-        if not last:
-            send_ghosts(t + 1)
-        tt(ln, R("bg", 0, CAP), R("t2", 0, CAP), A.max, oidx=ML)
-        children(t, WB[t + 1], R("xc", 0, CAP), None)
-        if last:
-            dmas("G", [(T.yx[:, :], ap(own(WB[t + 1], 0, LM)), [own(WB[t + 1], 0, LM)], [])])
-        else:
-            copy_c(t + 1, 0)
-        if last or nxt == 2:
-            move_step(t, 1)()
-            join_step(t, 1)()
+            if i == 1:
+                if last:
+                    join_sum(t, 1, (1,))
+                up[K - 1][3]()
+                if t > 0:
+                    act(own(wn, *twins(t)), upto(wn, NP[t]), idx=TL[t])
+            if i == 6:
+                join(t, 0)
+                keep(t, K - 1)
+                if t > 0:
+                    tt(own(ln, *twins(t)), upto(ln, NP[t]), R("tw", 0, CAP), A.max, idx=TL[t])
+                if last:
+                    join(t, 1)
+        xc = own(wn, L0, L0 + CAP) if t == 0 else R("xc", 0, CAP)
+        act(xc, upto(wn, NT[t]), 0.5, idx=ML[t])
+        cp(R("bg", 0, CAP), upto(ln, NT[t]), idx=ML[t])
+        tt(upto(ln, NT[t]), R("bg", 0, CAP), R("t2", 0, CAP), A.max, oidx=ML[t])
+        act(R("t1", 0, CAP), upto("pl", LM), RM[t], idx=ML[t])
+        for c, grp in bq[len(bq) - held:]:
+            gather_b(t, c, grp)
+        cp(upto(wn, NT[t]), xc, oidx=ML[t])
+        if t > 0:
+            cp(own(wn, L0, NT[t + 1]), xc, oidx=CL[t])
+
+        def kept_sums(t=t, K=K):
+            for c in range(K - 1, K + min(t, 1)):
+                join_sum(t, c, (0,))
+
+        def last_sums(t=t, K=K):
+            join_sum(t, K - 1, (1,))
+            if t > 0:
+                cp(own("gd", *twins(t)), upto("gd", NP[t]), idx=TL[t])
+                join_sum(t, K, (1,))
+
+        def twin_join(t=t, K=K):
+            if t > 0:
+                join(t, K)
+
+        def mothers_links(t=t):
+            ts(R("lk", 0, CAP), upto(LB[t + 1], NT[t]), NRM[t], A.mult, idx=ML[t])
+            child_links(t)
         if last:
             v2 = V0[t][2]
-            dmas("G", [(T.yn[:, 0:v2], ap(own(LB[t + 1], 0, v2)), [own(LB[t + 1], 0, v2)], [])])
+            kept_sums()
+            dmas(OUTQ, [(T.yn[:, 0:v2], ap(own(ln, 0, v2)), [own(ln, 0, v2)], [])])
+            dmas(OUTQ, [(T.yx[:, :], ap(own(wn, 0, LM)), [own(wn, 0, LM)], [])])
+            last_sums()
+            join(t, K - 1)
+            twin_join()
+            mothers_links()
+            dmas("S", [(T.yn[:, v2:LM], ap(own(ln, v2, LM)), [own(ln, v2, LM)], [])])
         else:
+            copy_x(t + 1, 0)
             relayout(t + 1, 0)
-        for c, grp in bq[len(early):]:
-            gather_b(t, c, grp)
-        act(R("t1", 0, CAP), R("pl", 0, OWN), RM[t], idx=ML)
-        if last:
-            move_step(t, 2)()
-            join_step(t, 2)()
-            child_links(t)()
-            dmas("S", [(T.yn[:, v2:LM], ap(own(LB[t + 1], v2, LM)), [own(LB[t + 1], v2, LM)], [])])
-        else:
-            def first(t=t, nxt=nxt):
-                if nxt == 1:
-                    move_step(t, 1)()
-                move_step(t, 2)()
-                if nxt == 1:
-                    join_step(t, 1)()
-                join_step(t, 2)()
-                relayout(t + 1, 1)
-
-            def second(t=t):
-                child_links(t)()
-                relayout(t + 1, 2)
-            carry = [first, second]
+            rest = []
+            steps = [lambda t=t: round_consts(t + 1), kept_sums, last_sums, lambda t=t: join(t, 1),
+                     lambda t=t: relayout(t + 1, 1), twin_join]
+            between = [mothers_links]
+            if t == 1:
+                steps[0] = lambda: rest.extend(twin_list())
+                steps.append(lambda: (run(rest), round_consts(2)))
+                between.append(lambda: relayout(2, 2))
+            carry = {}
+            for k, f in zip(CARRY_AT, steps):
+                carry[k] = carry.get(k, []) + [f]
 
     for s in total:
         if max(known[q].get(s, 0) for q in Q) < total[s]:

@@ -16,18 +16,21 @@ NMAX = 1408
 BIG = 4096.0
 
 GROUPS = ((0, 4), (4, 4), (8, 4), (12, 4))
-FIRST_GROUPS = ((0, 1), (1, 1), (2, 2), (4, 4), (8, 4), (12, 4))
-A_ON_V = ((4,), (2,), (2,))
+HALVES = ((0, 8), (8, 8))
+FIRST_GROUPS = ((0, 2), (2, 2), (4, 4), (8, 4), (12, 4))
+A_ON_V = ((4,), (4,), (2,))
 B_FIRST = 1
-B_HELD = 1
-LAG = (2, 1, 1)
-CARRY_AT = (-1, 0, 2, 6, 6, 8, 10)
-UPD_AT = {2: (((1, 8), (1, 9), (1, 11), (1, 12), (1, 13), (1, 14)),),
-          3: (((2, 1), (2, 2), (2, 4), (2, 5)), ((2, 8), (2, 9), (2, 10), (2, 11)))}
-DEFER = (3, 1)
-TWIN_AT = 10
-JOIN_AT = {2: ((1, 4), (1, 13)), 3: ((2, 8), (2, 13))}
-X_AT, NEXT_AT, D_AT = 7, 12, 6
+PICK_LATE = 1
+LAST_ON_V = True
+B_HELD = (1, 1, 0)
+SMALL_AT = (5, 8, 9, 15, 16)
+CARRY_AT = (-1, 1, 2, 3, 4, 5, 6, 7, 8, 8, 10)
+UPD_AT = {2: (((1, 8), (1, 9), (1, 11), (1, 13), (1, 15), (1, 16)),),
+          3: (((1, 10), (1, 11), (1, 14), (1, 15)), ((2, 7), (2, 8), (2, 11), (2, 13)))}
+DEFER = 2
+TWIN_AT = 15
+JOIN_AT = {2: (1, 11), 3: (2, 11)}
+KEEP_AT, X_AT, SUM_AT, NEXT_AT = 2, 2, 4, 12
 HEAD = (8, 8, 8)
 OUTQ = "Y"
 RING = 9728
@@ -42,7 +45,7 @@ SCRATCH = {
     "pl": ("sbuf", [128, TW], F),
     "gr": ("sbuf", [128, RING], F),
     "gd": ("sbuf", [128, O0 + NMAX], F),
-    "tt": ("sbuf", [128, 1056], F),
+    "tt": ("sbuf", [128, 1056], F), "io3": ("sbuf", [128, 32], F),
     "zr": ("sbuf", [128, NP[-1]], F), "zl": ("sbuf", [128, NP[-1]], F),
     "zh": ("sbuf", [128, NP[-1]], F),
     "nbi": ("sbuf", [128, L0], I32),
@@ -67,15 +70,14 @@ SCRATCH = {
     "sm": ("sbuf", [128, 80], F),
     "pos": ("sbuf", [128, 12], U16), "ml": ("sbuf", [128, 48], U16), "cl": ("sbuf", [128, 36], U16),
     "si": ("sbuf", [128, 12], U16),
-    "x0b": ("psum", [128, 512], F), "x1b": ("psum", [128, 512], F), "x2b": ("psum", [128, 512], F),
+    "xx": ("psum", [128, 1024], F), "yy": ("psum", [128, 1024], F),
     "n0": ("psum", [128, 512], F), "n1": ("psum", [128, 512], F),
-    "y0": ("psum", [128, 512], F), "y1": ("psum", [128, 512], F), "z0": ("psum", [128, 512], F),
+    "d0": ("psum", [128, 512], F), "mb": ("psum", [128, 512], F),
 }
-PSUM = ("x0b", "x1b", "x2b", "n0", "n1", "y0", "y1", "z0")
-BANKS = {2: {"x": ("x0b", "x1b"), "n": ("n0", "n1"), "y": ("y0", "y1"), "d": ("y0", "n0"),
-             "j": ("z0", "n1", "z0"), "z": "z0", "m": "x2b"},
-         3: {"x": ("x0b", "x1b", "x2b"), "n": ("n0", "n1", "n0"), "y": ("y0", "y1", "z0"), "d": ("y0", "y1", "n1"),
-             "j": ("y0", "x1b", "x2b", "z0"), "z": "n1", "m": "x0b"}}
+PSUM = ("xx", "yy", "n0", "n1", "d0", "mb")
+BANKS = {2: {"n": (("n0", 0), ("n1", 0)), "d": (("d0", 0),) * 2, "j": (("n0", 0), ("n1", 0), ("d0", 0))},
+         3: {"n": (("n0", 0), ("n1", 0), ("n0", 0)), "d": (("d0", 0),) * 3,
+             "j": (("n1", 0), ("yy", 0), ("yy", 512), ("d0", 0))}}
 SEMAPHORES = (["qV", "qS", "qP", "qG"] + ["d%d" % i for i in range(60)]
               + ["ga%d" % t for t in range(RO)] + ["gl%d" % t for t in range(RO)]
               + ["%s%d" % (s, i) for s in ("fa", "fl", "fh", "ra", "rl") for i in range(9)])
@@ -227,7 +229,7 @@ def rank_program(g, core, T, topo):
     V0 = [[sum(ch[:c]) for c in range(len(ch))] for ch in CHUNKS]
     BK = [BANKS[len(ch)] for ch in CHUNKS]
     RLO = {w: sum(x // 16 for x in WIDTHS[:i]) for i, w in enumerate(WIDTHS)}
-    PM, PG, PAR, PG16, WGT = (R("col", i, i + 1) for i in (0, 1, 2, 3, 4))
+    PM, PG, PG16, PAR, WGT = (R("col", i, i + 1) for i in range(5))
     RM = [R("col", 8 + t, 9 + t) for t in range(RO)]
     NRM = [R("col", 12 + t, 13 + t) for t in range(RO)]
     NC_ = [R("col", 16 + t, 17 + t) for t in range(RO + 1)]
@@ -258,7 +260,8 @@ def rank_program(g, core, T, topo):
         return max(0, min(CHUNKS[t][c], FOLDED[t] - V0[t][c]))
 
     def bank(t, kind, c, lo=0, hi=None):
-        return R(BK[t][kind][c], lo, CHUNKS[t][c] if hi is None else hi)
+        b, o = BK[t][kind][c]
+        return R(b, o + lo, o + (CHUNKS[t][c] if hi is None else hi))
 
     def P(t, c, k, n=1, lo=0, hi=None):
         C = CHUNKS[t][c]
@@ -288,32 +291,44 @@ def rank_program(g, core, T, topo):
 
     def relayout_consts(C):
         if C in made:
-            return
+            return []
         made.append(C)
         Wc = C // 16
         kf, ki, j = R("kf", 0, Wc), R("ki", 0, Wc), R("jj", 0, Wc)
-        ts(kf, j, 1.0 / Wc, A.mult, 0.5 / Wc - 0.5, A.add)
-        ts(PARC, PAR, float(C + 16), A.mult)
-        cp(ki, kf)
-        cp(kf, ki)
-        ts(kf, kf, -(C - 1) / 16.0, A.mult)
-        tt(kf, kf, j, A.add)
-        ts(R("rl", RLO[C], RLO[C] + Wc), kf, 16.0, A.mult, PARC, A.add)
+        return [lambda: (ts(kf, j, 1.0 / Wc, A.mult, 0.5 / Wc - 0.5, A.add), ts(PARC, PAR, (C + 16) / 16.0, A.mult)),
+                lambda: cp(ki, kf),
+                lambda: ts(kf, ki, -(C - 1) / 16.0, A.mult, PARC, A.add),
+                lambda: tt(kf, kf, j, A.add),
+                lambda: ts(R("rl", RLO[C], RLO[C] + Wc), kf, 16.0, A.mult)]
 
-    def relayout(t, c):
+    def turn(out, in_):
+        op("V", lambda: g.vector.transpose(ap(out), ap(in_)), [in_], [out])
+
+    def relayout_steps(t, c):
         C, v0 = CHUNKS[t][c], V0[t][c]
-        relayout_consts(C)
-        a, b = own(LB[t], v0, v0 + C), own(LB[t], v0 - 16, v0 + C + 16)
-        o1, o2 = R("tt", 0, C), R("tt", C, 2 * C + 32)
-        op("V", lambda: g.vector.transpose(ap(o1), ap(a)), [a], [o1])
-        op("V", lambda: g.vector.transpose(ap(o2), ap(b)), [b], [o2])
-        cp(LT(t, c, 0, 16), R("tt", 0, 2 * C + 32), idx=R("rl", RLO[C], RLO[C] + C // 16))
+        return [lambda: turn(R("tt", 0, C), own(LB[t], v0, v0 + C)),
+                lambda: turn(R("tt", C, 2 * C + 32), own(LB[t], v0 - 16, v0 + C + 16)),
+                lambda: cp(LT(t, c, 0, 16), R("tt", 0, 2 * C + 32), idx=R("rl", RLO[C], RLO[C] + C // 16))]
 
-    def copy_x(t, c, kind="x", stop=True):
+    def copy_wide(buf, o, src):
+        lo, hi = src[1], src[2]
+        while lo < hi:
+            n = min(hi - lo, 512 - o % 512)
+            mm(R(buf, o, o + n), ID1, R(src[0], lo, lo + n), True, True)
+            lo, o = lo + n, o + n
+
+    def copy_x(t, c):
+        for i in range(2):
+            copy_wide("xx", i * CHUNKS[t][c], own(WB[t], *cells(t, c)))
+
+    def first_planes(t, c):
+        copy_wide("yy", 0, P(t, c, 0, 2))
+
+    def copy_d(t, c, stop, kind="d"):
         mm(bank(t, kind, c), ID1, own(WB[t], *cells(t, c)), True, stop)
 
     def gather_a(t, c):
-        for k0, n in (FIRST_GROUPS if c == 0 else GROUPS):
+        for k0, n in (FIRST_GROUPS if c == 0 else HALVES):
             (cp if c == 0 and k0 in A_ON_V[t] else act)(P(t, c, k0, n), places(WB[t], NT[t]), idx=LT(t, c, k0, n))
 
     slot = [0]
@@ -334,23 +349,27 @@ def rank_program(g, core, T, topo):
 
     cslot = [0]
 
-    def least(t, c):
-        return R(BK[t]["z"], 0, CHUNKS[t][c] - folded(t, c))
-
-    def compare(t, c, k):
+    def compare(t, c, j, amid=None):
         C = CHUNKS[t][c]
-        if cslot[0] + C > CS * 512:
+        if cslot[0] + 2 * C > CS * 512:
             cslot[0] = 0
-        s = R("cmp", cslot[0], cslot[0] + C)
-        cslot[0] += C
-        tt(s, P(t, c, k), bank(t, "x", c), A.is_gt)
-        mm(bank(t, "n", c), R("sb", 15 - k, 143 - k), s, k == 0, k == 15)
+        o = cslot[0]
+        cslot[0] += 2 * C
+        tt(R("cmp", o, o + 2 * C), P(t, c, 2 * j, 2), R("xx", 0, 2 * C), A.is_gt)
+        if amid:
+            amid()
+        for i, k in enumerate((2 * j, 2 * j + 1)):
+            mm(bank(t, "n", c), R("sb", 15 - k, 143 - k), R("cmp", o + i * C, o + (i + 1) * C), k == 0, k == 15)
 
-    def running(t, c, k):
-        C, y = CHUNKS[t][c], bank(t, "y", c)
-        tt(own(WB[t + 1], *cells(t, c)) if k == 15 else y, P(t, c, k), y, A.max)
-        if folded(t, c) < C:
-            tt(least(t, c), P(t, c, k, 1, folded(t, c), C), least(t, c), A.min)
+    def running(t, c, j):
+        y = R("yy", 0, 2 * CHUNKS[t][c])
+        tt(y, P(t, c, 2 * j, 2), y, A.max)
+
+    def greatest(t, c):
+        C, xn = CHUNKS[t][c], own(WB[t + 1], *cells(t, c))
+        return [lambda: tt(xn, P(t, c, 15), R("yy", C, 2 * C), A.max),
+                lambda: tt(R("yy", 0, C), P(t, c, 14), R("yy", 0, C), A.max),
+                lambda: tt(xn, xn, R("yy", 0, C), A.max)]
 
     def lands(t, c):
         v0, n = V0[t][c], folded(t, c)
@@ -377,8 +396,6 @@ def rank_program(g, core, T, topo):
         note("X", [], [z], ("ra%d" % i, n))
 
     def sum_a(t, c):
-        if BK[t]["d"][c] == BK[t]["y"][c]:
-            copy_x(t, c, "d", False)
         mm(bank(t, "d", c), IDQ, own(WB[t + 1], *cells(t, c)), False, False)
 
     voted, counted = [], []
@@ -389,17 +406,17 @@ def rank_program(g, core, T, topo):
             a, b = 128 * cb, min(128 * cb + 128, NT[t])
             if cb not in counted and sum(max(0, min(b, y) - max(a, x)) for x, y in voted) == b - a:
                 counted.append(cb)
-                mm(R(BK[t]["m"], cb, cb + 1), own("vote", a, a + 128), R("ones", 0, 1), True, True)
+                mm(R("mb", cb, cb + 1), own("vote", a, a + 128), R("ones", 0, 1), True, True)
 
     def update_steps(t, c):
-        span, n = cells(t, c), folded(t, c)
+        span = cells(t, c)
         z, d, xn = R("zr", *span), bank(t, "d", c), own(WB[t + 1], *span)
 
         def product():
-            if span[0] + n < span[1]:
-                tt(R("zr", span[0] + n, span[1]), own(WB[t], span[0] + n, span[1]), least(t, c), A.mult)
-            if n:
-                tt(R("zr", span[0], span[0] + n), R("zr", span[0], span[0] + n), bank(t, "x", c, 0, n), A.mult)
+            if c == len(CHUNKS[t]) - 1:
+                tt(z, z, R("xx", 0, CHUNKS[t][c]), A.mult)
+            else:
+                tt(z, z, bank(t, "n", c), A.mult)
 
         def scale():
             ts(z, z, 0.75, A.mult)
@@ -407,14 +424,15 @@ def rank_program(g, core, T, topo):
 
         def vote():
             ts(own("vote", *span), d, 1.0, A.is_gt)
+            if c == 0 and t < RO - 1:
+                mm(R("mb", 128, 256), ONES, own("vote", 0, 128), True, True)
             counts(t, *span)
         return [product, scale, vote, lambda: ts(xn, d, 0.0, A.max, 2.0, A.min)]
 
     def ghost_steps(t):
-        f = R(BK[t]["m"], 128, 256)
+        f = R("mb", 128, 256)
 
         def factor():
-            mm(f, ONES, own("vote", 0, 128), True, True)
             ts(f, f, float(H), A.is_lt, 0.5, A.max)
 
         def send():
@@ -448,7 +466,7 @@ def rank_program(g, core, T, topo):
         return [lambda: tt(tmp, R("jj", 0, 12), s, A.max), lambda: cp(out, tmp)]
 
     def division_steps(t):
-        nb, MB = -(-NT[t] // 128), BK[t]["m"]
+        nb, MB = -(-NT[t] // 128), "mb"
         r, rin = R("rr", 0, nb), R("rin", 0, nb)
         q, pf = R("sm", 0, nb), R("sm", 16, 16 + nb)
         s = R(MB, 16, 16 + nb)
@@ -472,23 +490,24 @@ def rank_program(g, core, T, topo):
                 lambda: cp(R("pos", 0, nb), pf),
                 scatter,
                 lambda: rest[0](),
-                lambda: rest[1](),
-                lambda: ts(NC_[t + 1], R(MB, 32, 33), float(CAP), A.min, NC_[t], A.add)]
+                lambda: ts(NC_[t + 1], R(MB, 32, 33), float(CAP), A.min, NC_[t], A.add),
+                lambda: rest[1]()]
+
+    def twin_index():
+        a, m = R("sm", 48, 60), R("sm", 64, 76)
+        return [lambda: ts(a, R("jj", 0, 12), NC_[1], A.subtract, float(CAP + 1), A.add),
+                lambda: ts(m, a, float(CAP), A.is_le),
+                lambda: tt(a, a, m, A.mult),
+                lambda: cp(R("si", 0, 12), a)]
 
     def twin_list():
-        a, m = R("sm", 48, 60), R("sm", 64, 76)
-        ts(a, R("jj", 0, 12), NC_[1], A.subtract, float(CAP + 1), A.add)
-        ts(m, a, float(CAP), A.is_le)
-        tt(a, a, m, A.mult)
-        cp(R("si", 0, 12), a)
         cp(R("win2", 0, CAP), R("win", 0, 208), idx=R("si", 0, 12))
-        return mothers("win2", 0, R("y1", 0, 12), a, TL[2])
+        return mothers("win2", 0, R("d0", 0, 12), R("sm", 48, 60), TL[2])
 
     def round_consts(t):
-        ms(R("win", 0, 208), 0.0)
-        ts(R("t2", 0, CAP), own("pl", L0, L0 + CAP), NC_[t], A.add, RM[t], A.mult)
-        if t > 0:
-            ts(CL[t], R("jj", 0, 12), NC_[t], A.add)
+        return [lambda: ms(R("win", 0, 208), 0.0),
+                lambda: ts(R("t2", 0, CAP), own("pl", L0, L0 + CAP), NC_[t], A.add, RM[t], A.mult),
+                lambda: ts(CL[t], R("jj", 0, 12), NC_[t], A.add)]
 
     def twin_places(t):
         act(R("tw", 0, CAP), upto("pl", LM), RM8[t - 1], idx=TL[t])
@@ -506,32 +525,49 @@ def rank_program(g, core, T, topo):
 
     C0 = CHUNKS[0][0]
     dmas("Y", [(ap(own("wa", 0, 128)), T.x0[:, 0:128], [], [own("wa", 0, 128)])])
-    dmas("S", [(ap(R("nbi", 0, C0 + 16)), T.nb[:, 0:C0 + 16], [], [R("nbi", 0, C0 + 16)])])
+    C1 = C0 + 16
+    dmas("S", [(ap(R("nbi", 0, C1)), T.nb[:, 0:C1], [], [R("nbi", 0, C1)])])
+    dmas("S", [(ap(R("nbi", C1, L0)), T.nb[:, C1:L0], [], [R("nbi", C1, L0)])])
     dmas("Y", [(ap(own("wa", 128, L0)), T.x0[:, 128:L0], [], [own("wa", 128, L0)])])
-    dmas("S", [(ap(R("nbi", C0 + 16, L0)), T.nb[:, C0 + 16:L0], [], [R("nbi", C0 + 16, L0)])])
     iota(R("ip", 0, 1), [[1, 1]], 0, 1)
     iota(R("iot", 0, 32), [[16, 32]], 0, 0)
+    iota(R("io3", 0, 32), [[1, 16], [256, 2]], 0, 0)
     ms(ID1, 1.0)
     zer = R("gd", 0, O0)
-    ms(zer, 0.0)
     iota(R("la", O0 - 16, O0), [[1, 16]], GH - 16, 0)
     op("G", lambda: g.affine_select(T.id1[:], T.id1[:], [[-1, 128]], A.is_equal, 0.0, 0, 1), [ID1], [ID1])
     send_ghosts(0, own("wa", 0, 128))
     iota(R("la", SP, O0 - 16), [[1, GH - 16]], 0, 0)
-    ts(R("ip", 1, 2), R("ip", 0, 1), 15, A.bitwise_and)
     ts(R("ip", 2, 3), R("ip", 0, 1), 4, A.arith_shift_right)
-    ts(R("ip", 4, 5), R("ip", 0, 1), 112, A.bitwise_and)
+    ts(R("ip", 1, 2), R("ip", 0, 1), 15, A.bitwise_and)
+    ms(R("gd", 0, SP), 0.0)
+    tt(R("ip", 6, 7), R("ip", 0, 1), R("ip", 2, 3), A.add)
+    ts(R("ip", 3, 4), R("ip", 0, 1), 112, A.bitwise_and)
     ms(R("sb", 0, 144), 0.0)
-    tt(R("ip", 5, 6), R("ip", 0, 1), R("ip", 2, 3), A.add)
+    ts(R("ip", 4, 5), R("ip", 6, 7), 1, A.bitwise_and)
+    ms(R("wb16", 0, 144), 0.0)
     ms(own("la", L0, L0 + 16), 0.0)
-    ts(R("ip", 3, 4), R("ip", 5, 6), 1, A.bitwise_and)
     cp(R("col", 0, 4), R("ip", 1, 5))
+    ms(R("gd", SP, O0), 0.0)
+    ts(R("col", 21, 22), PM, 16.0, A.mult)
+    ts(R("col", 23, 24), PAR, float(C1), A.mult)
     ts(R("jj", 0, 32), R("iot", 0, 32), PM, A.add)
-    relayout_consts(C0)
-    cp(own("la", 0, C0 + 16), R("nbi", 0, C0 + 16))
-    relayout(0, 0)
-    cp(own("la", C0 + 16, L0), R("nbi", C0 + 16, L0))
+    ms(R("negu", 0, 128), -1.0)
+    ts(R("rl", RLO[C0], RLO[C0] + 32), R("io3", 0, 32), R("col", 21, 22), A.add, R("col", 23, 24), A.add)
+    ms(ONES, 1.0)
+    cp(own("la", 0, C1), R("nbi", 0, C1))
+    made.append(C0)
+    once, twice, pick = relayout_steps(0, 0)
+    ms(NC_[0], 0.0)
+    once()
+    twice()
+    cp(own("la", C1, L0), R("nbi", C1, L0))
+    pick()
+    ts(R("col", 8, 11), R("iot", 0, 3), 1.0 / 16, A.mult, PM, A.is_equal)
     ts(R("sb", 15, 143), R("iot", 0, 8), PG16, A.is_equal, BIG, A.mult, step=16)
+    ts(R("dd", 0, 12), R("jj", 0, 12), float(NMAX + 1), A.add)
+    ts(WGT, RM[0], 16.0, A.mult, RM[1], A.add)
+    ts(R("col", 12, 15), R("col", 8, 11), -1.0, A.mult, 1.0, A.add)
     for b in WB[:3] + LB[:3] + ("pl",):
         act(R(b, 0, SP), R("gd", 0, SP))
     for r in (own("wc", NT[1], NT[2]), own("lc", NT[1], NT[2]), own("wa", NT[2], LM), own("la", NT[2], LM)):
@@ -549,41 +585,33 @@ def rank_program(g, core, T, topo):
     def late_consts():
         iota(R("xc", 0, 176), [[8, 11], [0, 16]], O0 // 16, 0)
         iota(R("lk", 0, 176), [[0, 11], [1, 16]], 0, 0)
-        ms(R("negu", 0, 128), -1.0)
-        ms(ONES, 1.0)
         op("G", lambda: g.affine_select(T.negu[:], T.negu[:], [[-1, 128]], A.is_gt, 0.0, 0, 1),
            [R("negu", 0, 128)], [R("negu", 0, 128)])
         iota(places("pl", LM), [[1, GH + LM]], 0, 0)
-        ts(R("col", 8, 11), R("iot", 0, 3), 1.0 / 16, A.mult, PM, A.is_equal)
-        ms(R("wb16", 0, 144), 0.0)
-        ts(R("col", 12, 15), R("col", 8, 11), -1.0, A.mult, 1.0, A.add)
+        once, twice, pick = relayout_steps(0, 1)
         ts(R("col", 24, 27), R("col", 8, 11), 8.0, A.mult)
-        ts(WGT, RM[0], 16.0, A.mult, RM[1], A.add)
+        ts(R("wb16", 15, 143), R("iot", 0, 8), 0.0, A.mult, WGT, A.add, step=16)
         ts(R("xc", 0, 176), R("xc", 0, 176), PG, A.add, RM[0], A.mult)
         ts(R("lk", 0, 176), R("lk", 0, 176), RM[1], A.mult)
-        ts(R("wb16", 15, 143), R("iot", 0, 8), 0.0, A.mult, WGT, A.add, step=16)
-        tt(R("val", 0, 176), R("xc", 0, 176), R("lk", 0, 176), A.add)
-        ts(R("dd", 0, 12), R("jj", 0, 12), float(NMAX + 1), A.add)
-        ms(NC_[0], 0.0)
+        steps = relayout_consts(CHUNKS[2][1])
+        run([steps[0], once, steps[1], twice, steps[2], pick] + steps[3:])
+        return lambda: tt(R("val", 0, 176), R("xc", 0, 176), R("lk", 0, 176), A.add)
 
-    carry, between = {}, []
+    carry = {}
     for t in range(RO):
         last, K = t == RO - 1, len(CHUNKS[t])
         del voted[:], counted[:]
         bq = [(c, grp) for c in range(K) for grp in GROUPS]
         if t == 0:
+            late_fills()
             for c, grp in bq[:B_FIRST]:
                 gather_b(t, c, grp, True)
             bq = bq[B_FIRST:]
-            late_fills()
-            relayout(0, 1)
-            late_consts()
-            for C in WIDTHS:
-                relayout_consts(C)
+            values = late_consts()
             iota(R("lb", SP, O0), [[1, GH]], 0, 0)
             iota(R("lc", SP, O0), [[1, GH]], 0, 0)
-            carry = {3: [lambda: round_consts(0)]}
-        held = 0 if last else B_HELD
+            carry = {k: [f] for k, f in zip((13, 15, 16), round_consts(0)[:2] + [values])}
+        held = B_HELD[t]
         up = [update_steps(t, c) for c in range(K)]
         extra = {(0, k): carry[k] for k in carry}
 
@@ -591,7 +619,6 @@ def rank_program(g, core, T, topo):
             extra[place] = extra.get(place, []) + [f]
 
         def later_gathers():
-            run(between)
             for c in range(1, K):
                 gather_a(t, c)
             fold(t, 1, lambda: back(t, 0))
@@ -605,74 +632,78 @@ def rank_program(g, core, T, topo):
         gather_a(t, 0)
         fold(t, 0)
         at((0, NEXT_AT), later_gathers)
-        at((1, 0), lambda: [gather_b(t, c, grp) for c, grp in bq[:len(bq) - held]])
-        for c in range(1, K):
-            at((c - 1, X_AT), lambda c=c: copy_x(t, c))
-            at((c - 1, NEXT_AT), lambda c=c: mm(bank(t, "y", c), ID1, P(t, c, 0), True, True))
-            at((c, 0), lambda c=c: sum_a(t, c - 1))
-        at((K - 1, D_AT), lambda: copy_x(t, K - 1, "d", False))
-        if K == 3:
-            at((2, 11), lambda: join_sum(t, 1, (0,)))
+
+        def link_gathers():
+            s = "rl%d" % (3 * t + K - 1)
+            for c, grp in bq[:len(bq) - held]:
+                if c >= PICK_LATE:
+                    wait("Y", (s, total[s]))
+                gather_b(t, c, grp)
+        at((1, 0), link_gathers)
         for c in range(K - 1):
+            at((c + 1, KEEP_AT), lambda c=c: keep(t, c))
+            at((c + 1, X_AT), lambda c=c: copy_d(t, c, True, "n"))
+            at((c + 1, SUM_AT), lambda c=c: (copy_d(t, c, False), sum_a(t, c)))
             for place, f in zip(UPD_AT[K][c], up[c] + ([] if last else ghost_steps(t))):
                 at(place, f)
-        for part, place in enumerate(JOIN_AT[K]):
-            at(place, lambda part=part: join_sum(t, 0, (part,)))
+        at(UPD_AT[K][K - 2][3], lambda: copy_d(t, K - 1, False))
+        at(JOIN_AT[K], lambda: join_sum(t, 0, (0,)))
         run(extra.get((0, -1), []))
-        mm(bank(t, "y", 0), ID1, P(t, 0, 0), True, True)
         for c in range(K):
-            if folded(t, c) < CHUNKS[t][c]:
-                mm(least(t, c), ID1, P(t, c, 0, 1, folded(t, c), CHUNKS[t][c]), True, True)
-            for k in range(16):
-                if c < K - 1 or k < 16 - sum(DEFER):
-                    compare(t, c, k)
-                if k - LAG[c] >= 1:
-                    running(t, c, k - LAG[c])
-                run(extra.get((c, k), []))
-            for k in range(16 - LAG[c], 16):
-                running(t, c, k)
-            if c < K - 1:
-                keep(t, c)
+            first_planes(t, c)
+            for j in range(8):
+                if c < K - 1 or j < 8 - DEFER:
+                    compare(t, c, j, (lambda: copy_x(t, c + 1)) if j == 7 else None)
+                run(extra.get((c, 2 * j), []))
+                if j > 1:
+                    running(t, c, j - 1)
+                run(extra.get((c, 2 * j + 1), []))
+            ends = greatest(t, c)
+            run(ends[:2] + extra.get((c, 16), []) + ends[2:])
         wn, ln = WB[t + 1], LB[t + 1]
         sum_a(t, K - 1)
-        late = list(range(16 - sum(DEFER), 16))
-
-        def deferred(n):
-            for k in late[:n]:
-                compare(t, K - 1, k)
-            del late[:n]
-        run(up[K - 1][:2])
-        deferred(DEFER[0])
-        up[K - 1][2]()
+        late = [lambda j=j: compare(t, K - 1, j) for j in range(8 - DEFER, 8)]
+        product, scale, vote, clip = up[K - 1]
+        run(late[:-1] + [product, scale, late[-1], vote])
+        small = []
         if t > 0:
             cp(own("vote", *twins(t)), upto("vote", NP[t]), idx=TL[t])
             counts(t, *twins(t))
-        deferred(DEFER[1])
+        clip()
+        if t > 0 and not (last and LAST_ON_V):
+            act(own(wn, *twins(t)), upto(wn, NP[t]), idx=TL[t])
+        if t == 0:
+            small = [f for C in WIDTHS for f in relayout_consts(C)]
+        if t == 1:
+            small = twin_index()
+        if last and LAST_ON_V:
+            small = [lambda: cp(own(wn, *twins(t)), upto(wn, NP[t]), idx=TL[t])]
         for i, f in enumerate(division_steps(t)):
             f()
             if i == 1:
-                if last:
-                    join_sum(t, 1, (1,))
-                up[K - 1][3]()
-                if t > 0:
-                    act(own(wn, *twins(t)), upto(wn, NP[t]), idx=TL[t])
+                join_sum(t, 0, (1,))
             if i == 6:
-                join(t, 0)
+                if last:
+                    join_sum(t, 1)
                 keep(t, K - 1)
+                join(t, 0)
                 if t > 0:
                     tt(own(ln, *twins(t)), upto(ln, NP[t]), R("tw", 0, CAP), A.max, idx=TL[t])
-                if last:
-                    join(t, 1)
+            elif i in (0, 2, 3, 4, 5) and small:
+                small.pop(0)()
         xc = own(wn, L0, L0 + CAP) if t == 0 else R("xc", 0, CAP)
-        act(xc, upto(wn, NT[t]), 0.5, idx=ML[t])
-        cp(R("bg", 0, CAP), upto(ln, NT[t]), idx=ML[t])
-        tt(upto(ln, NT[t]), R("bg", 0, CAP), R("t2", 0, CAP), A.max, oidx=ML[t])
+        if last and LAST_ON_V:
+            ts(xc, upto(wn, NT[t]), 0.5, A.mult, idx=ML[t])
+        else:
+            act(xc, upto(wn, NT[t]), 0.5, idx=ML[t])
         act(R("t1", 0, CAP), upto("pl", LM), RM[t], idx=ML[t])
         for c, grp in bq[len(bq) - held:]:
             gather_b(t, c, grp)
-        cp(upto(wn, NT[t]), xc, oidx=ML[t])
-        if t > 0:
-            cp(own(wn, L0, NT[t + 1]), xc, oidx=CL[t])
+        cp(R("bg", 0, CAP), upto(ln, NT[t]), idx=ML[t])
+        if not last:
+            consts = round_consts(t + 1)
+            consts.pop()()
+        tt(upto(ln, NT[t]), R("bg", 0, CAP), R("t2", 0, CAP), A.max, oidx=ML[t])
 
         def kept_sums(t=t, K=K):
             for c in range(K - 1, K + min(t, 1)):
@@ -690,30 +721,43 @@ def rank_program(g, core, T, topo):
 
         def mothers_links(t=t):
             ts(R("lk", 0, CAP), upto(LB[t + 1], NT[t]), NRM[t], A.mult, idx=ML[t])
-            child_links(t)
+
+        def halve():
+            cp(upto(wn, NT[t]), xc, oidx=ML[t])
+
+        def children():
+            if t > 0:
+                cp(own(wn, L0, NT[t + 1]), xc, oidx=CL[t])
         if last:
             v2 = V0[t][2]
-            kept_sums()
+            run([kept_sums, halve])
+            dmas(OUTQ, [(T.yx[:, 0:L0], ap(own(wn, 0, L0)), [own(wn, 0, L0)], [])])
+            join(t, 1)
             dmas(OUTQ, [(T.yn[:, 0:v2], ap(own(ln, 0, v2)), [own(ln, 0, v2)], [])])
-            dmas(OUTQ, [(T.yx[:, :], ap(own(wn, 0, LM)), [own(wn, 0, LM)], [])])
+            children()
+            dmas(OUTQ, [(T.yx[:, L0:LM], ap(own(wn, L0, LM)), [own(wn, L0, LM)], [])])
             last_sums()
             join(t, K - 1)
             twin_join()
             mothers_links()
+            child_links(t)
             dmas("S", [(T.yn[:, v2:LM], ap(own(ln, v2, LM)), [own(ln, v2, LM)], [])])
         else:
+            once, twice, pick = relayout_steps(t + 1, 0)
+            run([kept_sums, halve, once, children])
             copy_x(t + 1, 0)
-            relayout(t + 1, 0)
             rest = []
-            steps = [lambda t=t: round_consts(t + 1), kept_sums, last_sums, lambda t=t: join(t, 1),
-                     lambda t=t: relayout(t + 1, 1), twin_join]
-            between = [mothers_links]
+            run([twice, consts[1], pick])
+            if t == 0:
+                consts[0]()
+            else:
+                small = [lambda: rest.extend(twin_list()), lambda: rest[0](), lambda: rest[1](), consts[0]]
+            steps = ([last_sums, lambda t=t: join(t, 1)] + relayout_steps(t + 1, 1)
+                     + [twin_join, mothers_links, lambda t=t: child_links(t)])
             if t == 1:
-                steps[0] = lambda: rest.extend(twin_list())
-                steps.append(lambda: (run(rest), round_consts(2)))
-                between.append(lambda: relayout(2, 2))
+                steps += relayout_steps(2, 2)
             carry = {}
-            for k, f in zip(CARRY_AT, steps):
+            for k, f in list(zip(CARRY_AT, steps)) + list(zip(SMALL_AT, small)):
                 carry[k] = carry.get(k, []) + [f]
 
     for s in total:

@@ -7,33 +7,34 @@ L0, CAP, RO, GH, H = 1024, 192, 3, 512, 80
 LM = L0 + RO * CAP
 SP = CAP
 O0 = SP + GH
-TW = O0 + LM
-CHUNKS = ((512, 512), (512, 512), (512, 384, 320))
-FOLDED = (1024, 1024, 1216)
+TW = O0 + LM + 8
+CHUNKS = ((512, 512), (512, 512), (512, 512, CAP))
 NP = tuple(sum(c) for c in CHUNKS)
 WIDTHS = tuple(sorted(set(w for c in CHUNKS for w in c)))
 NMAX = 1408
 BIG = 4096.0
 
-GROUPS = ((0, 4), (4, 4), (8, 4), (12, 4))
+QUARTERS = ((0, 4), (4, 4), (8, 4), (12, 4))
 HALVES = ((0, 8), (8, 8))
-FIRST_GROUPS = ((0, 2), (2, 2), (4, 4), (8, 4), (12, 4))
-A_ON_V = ((4,), (4,), (2,))
+FIRST_GROUPS = ((0, 2), (2, 2), (4, 4), (8, 8))
+ENDING = ((0, 8), (8, 4), (12, 4))
+B_GROUPS = ((((0, 4), (4, 4), (8, 8)), ENDING), (HALVES, ENDING), (HALVES, ((0, 2), (2, 8), (10, 4), (14, 2))))
+PICK_FIRST = 8
+DMA_FILLS = 4
+B_ON_V = ((), (), ((1, (0, 2), 3),))
+A_ON_V = ((4,), (4,), (4,))
 B_FIRST = 1
 PICK_LATE = 1
-LAST_ON_V = True
 B_HELD = (1, 1, 0)
-SMALL_AT = (5, 8, 9, 15, 16)
-CARRY_AT = (-1, 1, 2, 3, 4, 5, 6, 7, 8, 8, 10)
-UPD_AT = {2: (((1, 8), (1, 9), (1, 11), (1, 13), (1, 15), (1, 16)),),
-          3: (((1, 10), (1, 11), (1, 14), (1, 15)), ((2, 7), (2, 8), (2, 11), (2, 13)))}
-DEFER = 2
-TWIN_AT = 15
-JOIN_AT = {2: (1, 11), 3: (2, 11)}
+CARRY_AT = (-1, 1, 2, 3, 4, 5, 6, 7, 8, 9, 11)
+UPD_AT = (8, 8, 11, 13, 15, 16)
+DEFER = (2, 2, 4)
+KIN_AT = (9, 9, 10, 10, 11, 11, 12, 12, 13, 14)
+JOIN_AT = 11
 KEEP_AT, X_AT, SUM_AT, NEXT_AT = 2, 2, 4, 12
-HEAD = (8, 8, 8)
+HEAD = 8
 OUTQ = "Y"
-RING = 9728
+RING = 9216
 CS = 6
 GHOST0_ENGINES = 4
 
@@ -42,42 +43,40 @@ SCRATCH = {
     "wa": ("sbuf", [128, TW], F), "wb": ("sbuf", [128, TW], F), "wc": ("sbuf", [128, TW], F),
     "la": ("sbuf", [128, TW], F), "lb": ("sbuf", [128, TW], F), "lc": ("sbuf", [128, TW], F),
     "pp": ("sbuf", [128, 16 * NP[-1]], F),
-    "pl": ("sbuf", [128, TW], F),
+    "pl": ("sbuf", [128, O0 + NMAX], F),
     "gr": ("sbuf", [128, RING], F),
     "gd": ("sbuf", [128, O0 + NMAX], F),
     "tt": ("sbuf", [128, 1056], F), "io3": ("sbuf", [128, 32], F),
-    "zr": ("sbuf", [128, NP[-1]], F), "zl": ("sbuf", [128, NP[-1]], F),
-    "zh": ("sbuf", [128, NP[-1]], F),
+    "zr": ("sbuf", [128, NP[-1]], F), "zl": ("sbuf", [128, L0 + 2 * CAP], F),
+    "zh": ("sbuf", [128, L0], F),
     "nbi": ("sbuf", [128, L0], I32),
     "id1": ("sbuf", [128, 128], F), "idq": ("sbuf", [128, 128], F),
-    "idn": ("sbuf", [128, 128], F), "idb": ("sbuf", [128, 128], F),
+    "idn": ("sbuf", [128, 128], F), "idb": ("sbuf", [128, 128], F), "idm": ("sbuf", [128, 128], F),
     "xc": ("sbuf", [128, CAP], F), "lk": ("sbuf", [128, CAP], F), "t1": ("sbuf", [128, CAP], F),
-    "t2": ("sbuf", [128, CAP], F), "bg": ("sbuf", [128, CAP], F), "tw": ("sbuf", [128, CAP], F),
+    "t2": ("sbuf", [128, 4 * CAP], F), "bg": ("sbuf", [128, CAP], F),
     "gs": ("sbuf", [128, 128], F),
     "cmp": ("sbuf", [128, CS * 512], BF),
     "lt0": ("sbuf", [128, NP[-1]], U16), "lt1": ("sbuf", [128, NP[-1]], U16),
     "vote": ("sbuf", [128, O0 + NMAX], BF),
-    "win": ("sbuf", [128, 1600], BF), "win2": ("sbuf", [128, CAP], BF),
+    "win": ("sbuf", [128, 1600], BF),
     "val": ("sbuf", [128, 176], BF),
     "sb": ("sbuf", [128, 144], BF), "wb16": ("sbuf", [128, 144], BF),
     "negu": ("sbuf", [128, 128], BF), "ones": ("sbuf", [128, 128], BF),
     "rl": ("sbuf", [128, sum(WIDTHS) // 16], U16),
     "ip": ("sbuf", [128, 8], I32), "col": ("sbuf", [128, 32], F),
-    "iot": ("sbuf", [128, 32], F), "jj": ("sbuf", [128, 32], F),
+    "iot": ("sbuf", [128, 36], F), "jj": ("sbuf", [128, 36], F),
     "kf": ("sbuf", [128, 32], F), "ki": ("sbuf", [128, 32], I32),
     "dd": ("sbuf", [128, 12], F),
     "rr": ("sbuf", [128, 16], BF), "rin": ("sbuf", [128, 16], BF),
-    "sm": ("sbuf", [128, 80], F),
-    "pos": ("sbuf", [128, 12], U16), "ml": ("sbuf", [128, 48], U16), "cl": ("sbuf", [128, 36], U16),
-    "si": ("sbuf", [128, 12], U16),
+    "sm": ("sbuf", [128, 48], F), "fa": ("sbuf", [128, 36], F), "fb": ("sbuf", [128, 36], F),
+    "pos": ("sbuf", [128, 12], U16), "ml": ("sbuf", [128, 36], U16), "fl": ("sbuf", [128, 36], U16),
     "xx": ("psum", [128, 1024], F), "yy": ("psum", [128, 1024], F),
     "n0": ("psum", [128, 512], F), "n1": ("psum", [128, 512], F),
     "d0": ("psum", [128, 512], F), "mb": ("psum", [128, 512], F),
 }
 PSUM = ("xx", "yy", "n0", "n1", "d0", "mb")
-BANKS = {2: {"n": (("n0", 0), ("n1", 0)), "d": (("d0", 0),) * 2, "j": (("n0", 0), ("n1", 0), ("d0", 0))},
-         3: {"n": (("n0", 0), ("n1", 0), ("n0", 0)), "d": (("d0", 0),) * 3,
-             "j": (("n1", 0), ("yy", 0), ("yy", 512), ("d0", 0))}}
+BANKS = {"n": (("n0", 0), ("n1", 0), ("n0", 0)), "d": (("d0", 0), ("d0", 0), ("yy", 0)),
+         "j": (("n0", 0), ("n1", 0), ("d0", 0))}
 SEMAPHORES = (["qV", "qS", "qP", "qG"] + ["d%d" % i for i in range(60)]
               + ["ga%d" % t for t in range(RO)] + ["gl%d" % t for t in range(RO)]
               + ["%s%d" % (s, i) for s in ("fa", "fl", "fh", "ra", "rl") for i in range(9)])
@@ -117,7 +116,8 @@ def rank_program(g, core, T, topo):
                     if q == "P" and e[3] == "P":
                         continue
                     meet = e[0] < hi and lo < e[1] and (w or e[2])
-                    if meet or (b in PSUM and e[3] != q):
+                    shared = b in PSUM and e[3] != q and e[0] // 512 <= (hi - 1) // 512 and lo // 512 <= (e[1] - 1) // 512
+                    if meet or shared:
                         need[e[4][0]] = max(need.get(e[4][0], 0), e[4][1])
         for s in need:
             wait(q, (s, need[s]))
@@ -187,10 +187,10 @@ def rank_program(g, core, T, topo):
     def ms(out, c):
         op("V", lambda: g.vector.memset(ap(out), c), [], regs(out))
 
-    def act(out, in_, scale=1.0, idx=None):
+    def act(out, in_, scale=1.0, idx=None, bias=0.0):
         i = ap(in_) if idx is None else ap(in_).indirect(ap(idx))
-        op("S", lambda: g.scalar.activation(ap(out), i, ACT.Identity, scale=sc(scale)),
-           regs(in_, idx, scale), regs(out))
+        op("S", lambda: g.scalar.activation(ap(out), i, ACT.Identity, bias=sc(bias), scale=sc(scale)),
+           regs(in_, idx, scale, bias), regs(out))
 
     def mm(out, lhsT, rhs, start, stop, step=None):
         r = ap(rhs) if step is None else T[rhs[0]][:, rhs[1]:rhs[2]:step]
@@ -227,19 +227,21 @@ def rank_program(g, core, T, topo):
     LB = ("la", "lb", "lc", "la")
     NT = [L0 + CAP * t for t in range(RO + 1)]
     V0 = [[sum(ch[:c]) for c in range(len(ch))] for ch in CHUNKS]
-    BK = [BANKS[len(ch)] for ch in CHUNKS]
     RLO = {w: sum(x // 16 for x in WIDTHS[:i]) for i, w in enumerate(WIDTHS)}
     PM, PG, PG16, PAR, WGT = (R("col", i, i + 1) for i in range(5))
     RM = [R("col", 8 + t, 9 + t) for t in range(RO)]
     NRM = [R("col", 12 + t, 13 + t) for t in range(RO)]
     NC_ = [R("col", 16 + t, 17 + t) for t in range(RO + 1)]
     PARC = R("col", 20, 21)
-    RM8 = [R("col", 24 + t, 25 + t) for t in range(RO)]
-    ID1, IDQ, IDN, IDB = (R(b, 0, 128) for b in ("id1", "idq", "idn", "idb"))
+    FAR = [R("col", 24 + t, 25 + t) for t in range(RO)]
+    ID1, IDQ, IDN, IDB, IDM = (R(b, 0, 128) for b in ("id1", "idq", "idn", "idb", "idm"))
     ONES = R("ones", 0, 128)
     ML = [R("ml", 12 * t, 12 * t + 12) for t in range(RO)]
-    TL = [None, ML[0], R("ml", 36, 48)]
-    CL = [R("cl", 12 * t, 12 * t + 12) for t in range(RO)]
+    TL = [None] + ML
+    T2 = [R("t2", CAP * t, CAP * t + CAP) for t in range(RO + 1)]
+    KX = R("mb", 128, 128 + 2 * CAP)
+    OX, OL = R("lb", 0, RO * CAP), R("lb", RO * CAP, 2 * RO * CAP)
+    G1, M1 = R("lb", 6 * CAP, 7 * CAP), R("lb", 7 * CAP, 8 * CAP)
 
     def own(b, lo, hi):
         return R(b, O0 + lo, O0 + hi)
@@ -256,17 +258,14 @@ def rank_program(g, core, T, topo):
     def twins(t):
         return NP[t], NP[t] + CAP
 
-    def folded(t, c):
-        return max(0, min(CHUNKS[t][c], FOLDED[t] - V0[t][c]))
-
     def bank(t, kind, c, lo=0, hi=None):
-        b, o = BK[t][kind][c]
+        b, o = BANKS[kind][c]
         return R(b, o + lo, o + (CHUNKS[t][c] if hi is None else hi))
 
-    def P(t, c, k, n=1, lo=0, hi=None):
+    def P(t, c, k, n=1):
         C = CHUNKS[t][c]
         o = 16 * V0[t][c] + k * C
-        return R("pp", o + lo, o + (n * C if hi is None else hi))
+        return R("pp", o, o + n * C)
 
     def LT(t, c, k, n):
         Wc = CHUNKS[t][c] // 16
@@ -306,9 +305,13 @@ def rank_program(g, core, T, topo):
 
     def relayout_steps(t, c):
         C, v0 = CHUNKS[t][c], V0[t][c]
+
+        def pick(k0=0, k1=16):
+            cp(LT(t, c, k0, k1 - k0), R("tt", 0, 2 * C + 32),
+               idx=R("rl", RLO[C] + k0 * C // 256, RLO[C] + k1 * C // 256))
         return [lambda: turn(R("tt", 0, C), own(LB[t], v0, v0 + C)),
                 lambda: turn(R("tt", C, 2 * C + 32), own(LB[t], v0 - 16, v0 + C + 16)),
-                lambda: cp(LT(t, c, 0, 16), R("tt", 0, 2 * C + 32), idx=R("rl", RLO[C], RLO[C] + C // 16))]
+                pick]
 
     def copy_wide(buf, o, src):
         lo, hi = src[1], src[2]
@@ -328,12 +331,12 @@ def rank_program(g, core, T, topo):
         mm(bank(t, kind, c), ID1, own(WB[t], *cells(t, c)), True, stop)
 
     def gather_a(t, c):
-        for k0, n in (FIRST_GROUPS if c == 0 else HALVES):
+        for k0, n in (FIRST_GROUPS, HALVES, ((1, 15),))[c]:
             (cp if c == 0 and k0 in A_ON_V[t] else act)(P(t, c, k0, n), places(WB[t], NT[t]), idx=LT(t, c, k0, n))
 
     slot = [0]
 
-    def gather_b(t, c, grp, ring=False):
+    def gather_b(t, c, grp, ring=False, by=act):
         k0, n = grp
         C, v0 = CHUNKS[t][c], O0 + V0[t][c]
         if c == 0 and not ring:
@@ -343,7 +346,7 @@ def rank_program(g, core, T, topo):
                 slot[0] = 0
             b, o = "gr", slot[0]
             slot[0] += n * C
-        act(R(b, o, o + n * C), places(LB[t], NT[t]), idx=LT(t, c, k0, n))
+        by(R(b, o, o + n * C), places(LB[t], NT[t]), idx=LT(t, c, k0, n))
         dmas("Y", [(T.gd[k0 + i:128:16, v0:v0 + C], T[b][k0 + i:128:16, o + i * C:o + (i + 1) * C],
                     [R(b, o + i * C, o + (i + 1) * C)], [R("gd#%d" % (k0 + i), v0, v0 + C)]) for i in range(n)])
 
@@ -355,48 +358,53 @@ def rank_program(g, core, T, topo):
             cslot[0] = 0
         o = cslot[0]
         cslot[0] += 2 * C
-        tt(R("cmp", o, o + 2 * C), P(t, c, 2 * j, 2), R("xx", 0, 2 * C), A.is_gt)
+        ks = [k for k in (2 * j, 2 * j + 1) if c < 2 or k > 0]
+        x = R("xx", 0, 2 * C) if c < 2 else R(KX[0], KX[1], KX[1] + len(ks) * C)
+        tt(R("cmp", o, o + len(ks) * C), P(t, c, ks[0], len(ks)), x, A.is_gt)
         if amid:
             amid()
-        for i, k in enumerate((2 * j, 2 * j + 1)):
-            mm(bank(t, "n", c), R("sb", 15 - k, 143 - k), R("cmp", o + i * C, o + (i + 1) * C), k == 0, k == 15)
+        for i, k in enumerate(ks):
+            mm(bank(t, "n", c), R("sb", 15 - k, 143 - k), R("cmp", o + i * C, o + (i + 1) * C),
+               k == (0 if c < 2 else 1), k == 15)
+
+    def Y(t, c):
+        return own(WB[t + 1] if t < RO - 1 else WB[1], *cells(t, c))
 
     def running(t, c, j):
         y = R("yy", 0, 2 * CHUNKS[t][c])
         tt(y, P(t, c, 2 * j, 2), y, A.max)
 
     def greatest(t, c):
-        C, xn = CHUNKS[t][c], own(WB[t + 1], *cells(t, c))
+        C, xn = CHUNKS[t][c], Y(t, c)
         return [lambda: tt(xn, P(t, c, 15), R("yy", C, 2 * C), A.max),
                 lambda: tt(R("yy", 0, C), P(t, c, 14), R("yy", 0, C), A.max),
                 lambda: tt(xn, xn, R("yy", 0, C), A.max)]
 
     def lands(t, c):
-        v0, n = V0[t][c], folded(t, c)
-        if c < len(HEAD) and HEAD[c]:
-            return [(0, HEAD[c], R("zh", v0, v0 + n)), (HEAD[c], 16 - HEAD[c], R("zl", v0, v0 + n))]
-        return [(0, 16, R("zl", v0, v0 + n))]
+        v0, v1 = cells(t, c)
+        if c < 2:
+            return [(0, HEAD, 1, R("zh", v0, v1)), (HEAD, 16 - HEAD, 1, R("zl", v0, v1))]
+        return [(0, 16, 2, R("zl", v0, v0 + 2 * CAP))]
 
     def fold(t, c, amid=None):
         i = 3 * t + c
         total["fa%d" % i] = 0
-        for j, (k0, n, land) in enumerate(lands(t, c)):
+        for j, (k0, n, w, land) in enumerate(lands(t, c)):
             if amid and j == len(lands(t, c)) - 1:
                 amid()
-            srcs = [P(t, c, k, 1, 0, folded(t, c)) for k in range(k0, k0 + n)]
+            srcs = [P(t, c, k, w) for k in range(k0, k0 + n, w)]
             total["fa%d" % i] += remote([(mate, mate_engs, "fa%d" % i, srcs, land, 3)],
                                         ("fl%d" % i, "fh%d" % i)[j], srcs, [])
 
     def back(t, c):
-        i = 3 * t + c
-        srcs = [x[2] for x in lands(t, c)]
-        z = R("zr", V0[t][c], V0[t][c] + folded(t, c))
-        n = remote([(mate, mate_engs, "ra%d" % i, srcs, z, 3 if len(srcs) > 1 else 0)],
-                   "rl%d" % i, [], [("fa%d" % i, total["fa%d" % i])])
+        i, C = 3 * t + c, CHUNKS[t][c]
+        srcs = [R(x[3][0], x[3][1] + u * C, x[3][1] + (u + 1) * C) for x in lands(t, c) for u in range(x[2])]
+        z = R("zr", *cells(t, c))
+        n = remote([(mate, mate_engs, "ra%d" % i, srcs, z, 3)], "rl%d" % i, [], [("fa%d" % i, total["fa%d" % i])])
         note("X", [], [z], ("ra%d" % i, n))
 
     def sum_a(t, c):
-        mm(bank(t, "d", c), IDQ, own(WB[t + 1], *cells(t, c)), False, False)
+        mm(bank(t, "d", c), IDQ, Y(t, c), False, False)
 
     voted, counted = [], []
 
@@ -413,13 +421,9 @@ def rank_program(g, core, T, topo):
         z, d, xn = R("zr", *span), bank(t, "d", c), own(WB[t + 1], *span)
 
         def product():
-            if c == len(CHUNKS[t]) - 1:
-                tt(z, z, R("xx", 0, CHUNKS[t][c]), A.mult)
-            else:
-                tt(z, z, bank(t, "n", c), A.mult)
+            tt(z, z, (bank(t, "n", 0), R("xx", 0, CHUNKS[t][c]), R(KX[0], KX[1], KX[1] + CAP))[c], A.mult)
 
-        def scale():
-            ts(z, z, 0.75, A.mult)
+        def difference():
             mm(d, IDN, z, False, True)
 
         def vote():
@@ -427,7 +431,7 @@ def rank_program(g, core, T, topo):
             if c == 0 and t < RO - 1:
                 mm(R("mb", 128, 256), ONES, own("vote", 0, 128), True, True)
             counts(t, *span)
-        return [product, scale, vote, lambda: ts(xn, d, 0.0, A.max, 2.0, A.min)]
+        return [product, difference, vote, lambda: ts(xn, d, 0.0, A.max, 2.0, A.min)]
 
     def ghost_steps(t):
         f = R("mb", 128, 256)
@@ -445,15 +449,18 @@ def rank_program(g, core, T, topo):
         tt(own(LB[t + 1], *span), own(LB[t], *span), bank(t, "n", c), A.min)
 
     def link_span(t, c):
-        return cells(t, c) if c < len(CHUNKS[t]) else twins(t)
+        return cells(t, c) if c < 2 else (L0, NT[t])
 
     def join_sum(t, c, parts=(0, 1)):
         span = link_span(t, c)
         b = bank(t, "j", c, 0, span[1] - span[0])
+        kin = t == RO - 1 and c == 2
         if 0 in parts:
             mm(b, IDB, own(LB[t + 1], *span), True, False)
+            if kin:
+                mm(bank(t, "j", c, 0, CAP), ID1, G1, False, False)
         if 1 in parts:
-            mm(b, ID1, own("gd", *span), False, True)
+            mm(b, IDM if kin else ID1, own("gd", *span), False, True)
 
     def join(t, c):
         span = link_span(t, c)
@@ -468,7 +475,7 @@ def rank_program(g, core, T, topo):
     def division_steps(t):
         nb, MB = -(-NT[t] // 128), "mb"
         r, rin = R("rr", 0, nb), R("rin", 0, nb)
-        q, pf = R("sm", 0, nb), R("sm", 16, 16 + nb)
+        pf = R("sm", 16, 16 + nb)
         s = R(MB, 16, 16 + nb)
         rest = []
 
@@ -484,40 +491,41 @@ def rank_program(g, core, T, topo):
             rest.extend(mothers("win", 1, R(MB, 48, 60), R("sm", 32, 44), ML[t]))
         return [lambda: ts(r, R(MB, 0, nb), float(H), A.is_ge),
                 scan,
-                lambda: ts(q, r, -BIG, A.mult),
-                lambda: tt(q, q, R("dd", 0, nb), A.add),
-                lambda: tt(pf, q, s, A.max),
-                lambda: cp(R("pos", 0, nb), pf),
+                lambda: tt(pf, R("dd", 0, nb), s, A.min),
+                lambda: ts(R("pos", 0, nb), pf, BIG, A.add),
                 scatter,
                 lambda: rest[0](),
                 lambda: ts(NC_[t + 1], R(MB, 32, 33), float(CAP), A.min, NC_[t], A.add),
                 lambda: rest[1]()]
 
-    def twin_index():
-        a, m = R("sm", 48, 60), R("sm", 64, 76)
-        return [lambda: ts(a, R("jj", 0, 12), NC_[1], A.subtract, float(CAP + 1), A.add),
-                lambda: ts(m, a, float(CAP), A.is_le),
-                lambda: tt(a, a, m, A.mult),
-                lambda: cp(R("si", 0, 12), a)]
-
-    def twin_list():
-        cp(R("win2", 0, CAP), R("win", 0, 208), idx=R("si", 0, 12))
-        return mothers("win2", 0, R("d0", 0, 12), R("sm", 48, 60), TL[2])
+    def closing_list():
+        a, b, j = R("fa", 0, 36), R("fb", 0, 36), R("jj", 0, 36)
+        d0, d1 = R("col", 28, 29), R("col", 29, 30)
+        return [lambda: ts(d0, NC_[1], -1.0, A.mult, float(CAP), A.add),
+                lambda: ts(d1, NC_[1], NC_[2], A.subtract, float(CAP), A.add),
+                lambda: ts(a, j, NC_[1], A.is_ge, d0, A.mult),
+                lambda: ts(b, j, NC_[2], A.is_ge, d1, A.mult),
+                lambda: tt(a, a, j, A.add),
+                lambda: tt(a, a, b, A.add),
+                lambda: ts(R("fl", 0, 36), a, float(RO * CAP), A.min)]
 
     def round_consts(t):
-        return [lambda: ms(R("win", 0, 208), 0.0),
-                lambda: ts(R("t2", 0, CAP), own("pl", L0, L0 + CAP), NC_[t], A.add, RM[t], A.mult),
-                lambda: ts(CL[t], R("jj", 0, 12), NC_[t], A.add)]
-
-    def twin_places(t):
-        act(R("tw", 0, CAP), upto("pl", LM), RM8[t - 1], idx=TL[t])
-        return lambda: tt(R("tw", 0, CAP), R("tw", 0, CAP), own("pl", *twins(t)), A.min)
+        first = own("pl", L0, NT[1])
+        if t == 0:
+            act(R("win", 0, 208), R("gd", 0, 208))
+            act(T2[0], first, RM[0])
+            act(T2[RO], own("pl", NT[1], NT[2]), RM[1])
+            return
+        dmas("Y", [(T.win[:, 0:208], T.vote[:, 0:208], [R("vote", 0, 208)], [R("win", 0, 208)])])
+        if t == 1:
+            act(own("pl", NT[t], NT[t + 1]), first, bias=NC_[t])
+            act(T2[t], own("pl", NT[t], NT[t + 1]), RM[t])
+        else:
+            ts(R("col", 27, 28), NC_[t], RM[t], A.mult)
+            act(T2[t], first, RM[t], bias=R("col", 27, 28))
 
     def child_links(t):
-        if t == 0:
-            tt(own(LB[1], L0, L0 + CAP), R("lk", 0, CAP), R("t1", 0, CAP), A.add)
-        else:
-            tt(own(LB[t + 1], L0, NT[t + 1]), R("lk", 0, CAP), R("t1", 0, CAP), A.add, oidx=CL[t])
+        tt(own(LB[t + 1], NT[t], NT[t + 1]), upto(LB[t + 1], NT[t]), R("t1", 0, CAP), A.min, idx=ML[t])
 
     def run(steps):
         for f in steps:
@@ -530,12 +538,13 @@ def rank_program(g, core, T, topo):
     dmas("S", [(ap(R("nbi", C1, L0)), T.nb[:, C1:L0], [], [R("nbi", C1, L0)])])
     dmas("Y", [(ap(own("wa", 128, L0)), T.x0[:, 128:L0], [], [own("wa", 128, L0)])])
     iota(R("ip", 0, 1), [[1, 1]], 0, 1)
-    iota(R("iot", 0, 32), [[16, 32]], 0, 0)
+    iota(R("iot", 0, 36), [[16, 36]], 0, 0)
     iota(R("io3", 0, 32), [[1, 16], [256, 2]], 0, 0)
     ms(ID1, 1.0)
     zer = R("gd", 0, O0)
     iota(R("la", O0 - 16, O0), [[1, 16]], GH - 16, 0)
     op("G", lambda: g.affine_select(T.id1[:], T.id1[:], [[-1, 128]], A.is_equal, 0.0, 0, 1), [ID1], [ID1])
+    iota(own("pl", L0, NT[2]), [[1, 2 * CAP]], GH + L0, 0)
     send_ghosts(0, own("wa", 0, 128))
     iota(R("la", SP, O0 - 16), [[1, GH - 16]], 0, 0)
     ts(R("ip", 2, 3), R("ip", 0, 1), 4, A.arith_shift_right)
@@ -551,10 +560,12 @@ def rank_program(g, core, T, topo):
     ms(R("gd", SP, O0), 0.0)
     ts(R("col", 21, 22), PM, 16.0, A.mult)
     ts(R("col", 23, 24), PAR, float(C1), A.mult)
-    ts(R("jj", 0, 32), R("iot", 0, 32), PM, A.add)
+    ts(R("jj", 0, 36), R("iot", 0, 36), PM, A.add)
     ms(R("negu", 0, 128), -1.0)
     ts(R("rl", RLO[C0], RLO[C0] + 32), R("io3", 0, 32), R("col", 21, 22), A.add, R("col", 23, 24), A.add)
+    ts(R("col", 8, 11), R("iot", 0, 3), 1.0 / 16, A.mult, PM, A.is_equal)
     ms(ONES, 1.0)
+    ts(R("col", 12, 15), R("col", 8, 11), -1.0, A.mult, 1.0, A.add)
     cp(own("la", 0, C1), R("nbi", 0, C1))
     made.append(C0)
     once, twice, pick = relayout_steps(0, 0)
@@ -562,75 +573,83 @@ def rank_program(g, core, T, topo):
     once()
     twice()
     cp(own("la", C1, L0), R("nbi", C1, L0))
-    pick()
-    ts(R("col", 8, 11), R("iot", 0, 3), 1.0 / 16, A.mult, PM, A.is_equal)
+    pick(0, PICK_FIRST)
+    pick(PICK_FIRST, 16)
     ts(R("sb", 15, 143), R("iot", 0, 8), PG16, A.is_equal, BIG, A.mult, step=16)
-    ts(R("dd", 0, 12), R("jj", 0, 12), float(NMAX + 1), A.add)
-    ts(WGT, RM[0], 16.0, A.mult, RM[1], A.add)
-    ts(R("col", 12, 15), R("col", 8, 11), -1.0, A.mult, 1.0, A.add)
-    for b in WB[:3] + LB[:3] + ("pl",):
+    spare = WB[:3] + LB[:3] + ("pl",)
+    dmas("Y", [(ap(R(b, 0, SP)), T.gd[:, 0:SP], regs(R("gd", 0, SP)), [R(b, 0, SP)]) for b in spare[:DMA_FILLS]])
+    for b in spare[DMA_FILLS:]:
         act(R(b, 0, SP), R("gd", 0, SP))
-    for r in (own("wc", NT[1], NT[2]), own("lc", NT[1], NT[2]), own("wa", NT[2], LM), own("la", NT[2], LM)):
-        act(r, R("gd", 0, CAP))
     act(own("lb", L0, L0 + 16), R("gd", 0, 16))
+    for b in (WB[RO], LB[RO]):
+        act(own(b, LM, LM + 8), R("gd", 0, 8))
     act(R("vote", 0, O0), zer)
     copy_x(0, 0)
 
     def late_fills():
+        act(R("dd", 0, 12), R("jj", 0, 12), bias=NMAX + 1 - BIG)
+        act(WGT, RM[0], 16.0, bias=RM[1])
+        act(R("col", 24, 27), R("col", 12, 15), BIG)
         act(own("vote", NT[1], NT[1] + 64), R("gd", 0, 64))
         act(IDQ, ID1, 0.25)
-        act(IDN, ID1, -1.0)
+        act(IDN, ID1, -0.75)
         act(IDB, ID1, -BIG)
+        act(IDM, ID1, NRM[1])
+        round_consts(0)
 
     def late_consts():
         iota(R("xc", 0, 176), [[8, 11], [0, 16]], O0 // 16, 0)
         iota(R("lk", 0, 176), [[0, 11], [1, 16]], 0, 0)
         op("G", lambda: g.affine_select(T.negu[:], T.negu[:], [[-1, 128]], A.is_gt, 0.0, 0, 1),
            [R("negu", 0, 128)], [R("negu", 0, 128)])
-        iota(places("pl", LM), [[1, GH + LM]], 0, 0)
+        op("G", lambda: g.affine_select(T.negu[:], T.negu[:], [[-1, 128]], A.not_equal, -BIG, 0, 1),
+           [R("negu", 0, 128)], [R("negu", 0, 128)])
+        iota(places("pl", L0), [[1, GH + L0]], 0, 0)
         once, twice, pick = relayout_steps(0, 1)
-        ts(R("col", 24, 27), R("col", 8, 11), 8.0, A.mult)
+        once()
         ts(R("wb16", 15, 143), R("iot", 0, 8), 0.0, A.mult, WGT, A.add, step=16)
         ts(R("xc", 0, 176), R("xc", 0, 176), PG, A.add, RM[0], A.mult)
         ts(R("lk", 0, 176), R("lk", 0, 176), RM[1], A.mult)
-        steps = relayout_consts(CHUNKS[2][1])
-        run([steps[0], once, steps[1], twice, steps[2], pick] + steps[3:])
-        return lambda: tt(R("val", 0, 176), R("xc", 0, 176), R("lk", 0, 176), A.add)
+        twice()
+        tt(R("val", 0, 176), R("xc", 0, 176), R("lk", 0, 176), A.add)
+        pick()
 
     carry = {}
+    SMALL = (lambda: [], lambda: relayout_consts(CAP), closing_list)
     for t in range(RO):
         last, K = t == RO - 1, len(CHUNKS[t])
         del voted[:], counted[:]
-        bq = [(c, grp) for c in range(K) for grp in GROUPS]
+        bq = [(c, grp) for c in range(2) for grp in B_GROUPS[t][c]]
         if t == 0:
             late_fills()
             for c, grp in bq[:B_FIRST]:
                 gather_b(t, c, grp, True)
+            late_consts()
             bq = bq[B_FIRST:]
-            values = late_consts()
-            iota(R("lb", SP, O0), [[1, GH]], 0, 0)
-            iota(R("lc", SP, O0), [[1, GH]], 0, 0)
-            carry = {k: [f] for k, f in zip((13, 15, 16), round_consts(0)[:2] + [values])}
         held = B_HELD[t]
         up = [update_steps(t, c) for c in range(K)]
         extra = {(0, k): carry[k] for k in carry}
+        wn, ln = WB[t + 1], LB[t + 1]
 
         def at(place, f):
             extra[place] = extra.get(place, []) + [f]
 
         def later_gathers():
+            if last:
+                x = own(WB[t], *cells(t, 2))
+                dmas("Y", [(ap(P(t, 2, 0)), ap(x), [x], [P(t, 2, 0)])])
             for c in range(1, K):
                 gather_a(t, c)
-            fold(t, 1, lambda: back(t, 0))
-            if K == 3 and folded(t, 2):
-                fold(t, 2, lambda: back(t, 1))
-                back(t, 2)
-            else:
-                back(t, 1)
             if t > 0:
-                at((K - 1, TWIN_AT), twin_places(t))
+                round_consts(t)
+            fold(t, 1, lambda: back(t, 0))
+            if last:
+                act(G1, places(LB[t], NT[t]), RM[1], idx=LT(t, 2, 1, 1))
+                fold(t, 2)
+            for c in range(1, K):
+                back(t, c)
         gather_a(t, 0)
-        fold(t, 0)
+        fold(t, 0, (lambda: [iota(R(b, SP, O0), [[1, GH]], 0, 0) for b in LB[1:3]]) if t == 0 else None)
         at((0, NEXT_AT), later_gathers)
 
         def link_gathers():
@@ -640,124 +659,126 @@ def rank_program(g, core, T, topo):
                     wait("Y", (s, total[s]))
                 gather_b(t, c, grp)
         at((1, 0), link_gathers)
-        for c in range(K - 1):
-            at((c + 1, KEEP_AT), lambda c=c: keep(t, c))
-            at((c + 1, X_AT), lambda c=c: copy_d(t, c, True, "n"))
-            at((c + 1, SUM_AT), lambda c=c: (copy_d(t, c, False), sum_a(t, c)))
-            for place, f in zip(UPD_AT[K][c], up[c] + ([] if last else ghost_steps(t))):
-                at(place, f)
-        at(UPD_AT[K][K - 2][3], lambda: copy_d(t, K - 1, False))
-        at(JOIN_AT[K], lambda: join_sum(t, 0, (0,)))
+        for c, grp, place in B_ON_V[t]:
+            bq.remove((c, grp))
+            at((1, place), lambda c=c, grp=grp: gather_b(t, c, grp, True, cp))
+        at((1, KEEP_AT), lambda: keep(t, 0))
+        at((1, X_AT), lambda: copy_d(t, 0, True, "n"))
+        at((1, SUM_AT), lambda: (copy_d(t, 0, False), sum_a(t, 0)))
+        for place, f in zip(UPD_AT, up[0] + ([] if last else ghost_steps(t))):
+            at((1, place), f)
+        at((1, UPD_AT[3]), lambda: copy_d(t, 1, False))
+        if last:
+            for i in range(2):
+                at((0, 16), lambda i=i: copy_wide(KX[0], KX[1] + i * CAP, own(WB[t], *cells(t, 2))))
+            kin = [lambda j=j: compare(t, 2, j) for j in range(8)]
+            kin += [lambda: tt(M1, P(t, 2, 1), R(KX[0], KX[1], KX[1] + CAP), A.max),
+                    lambda: (keep(t, 2), join_sum(t, 0, (0,)))]
+            for place, f in zip(KIN_AT, kin):
+                at((1, place), f)
+        else:
+            at((1, JOIN_AT), lambda: join_sum(t, 0, (0,)))
         run(extra.get((0, -1), []))
-        for c in range(K):
+        for c in range(2):
             first_planes(t, c)
             for j in range(8):
-                if c < K - 1 or j < 8 - DEFER:
-                    compare(t, c, j, (lambda: copy_x(t, c + 1)) if j == 7 else None)
+                if c == 0 or j < 8 - DEFER[t]:
+                    compare(t, c, j, (lambda: copy_x(t, 1)) if c == 0 and j == 7 else None)
                 run(extra.get((c, 2 * j), []))
                 if j > 1:
                     running(t, c, j - 1)
                 run(extra.get((c, 2 * j + 1), []))
             ends = greatest(t, c)
             run(ends[:2] + extra.get((c, 16), []) + ends[2:])
-        wn, ln = WB[t + 1], LB[t + 1]
-        sum_a(t, K - 1)
-        late = [lambda j=j: compare(t, K - 1, j) for j in range(8 - DEFER, 8)]
-        product, scale, vote, clip = up[K - 1]
-        run(late[:-1] + [product, scale, late[-1], vote])
-        small = []
+        sum_a(t, 1)
+        late = [lambda j=j: compare(t, 1, j) for j in range(8 - DEFER[t], 8)]
+        product, difference, vote, clip = up[1]
+        if last:
+            tt(Y(t, 2), upto(WB[1], L0), M1, A.max, idx=ML[0])
+            copy_d(t, 2, False)
+            sum_a(t, 2)
+            run(late[:-1] + [product, difference] + up[2][:2] + late[-1:] + [vote] + up[2][2:])
+        else:
+            run(late[:-1] + [product, difference] + late[-1:] + [vote])
         if t > 0:
             cp(own("vote", *twins(t)), upto("vote", NP[t]), idx=TL[t])
             counts(t, *twins(t))
+        small = SMALL[t]()
+
+        def fill(n=1):
+            run(small[:n])
+            del small[:n]
+        ready, scan, place, offsets, scatter, named, number, listed = division_steps(t)
+        if last:
+            join_sum(t, 0, (1,))
+        keep(t, 1)
+        fill(2 if last else 0)
+        run([ready, fill, scan])
+        join_sum(t, *((1, (0,)) if last else (0, (1,))))
         clip()
-        if t > 0 and not (last and LAST_ON_V):
+        if t > 0:
             act(own(wn, *twins(t)), upto(wn, NP[t]), idx=TL[t])
-        if t == 0:
-            small = [f for C in WIDTHS for f in relayout_consts(C)]
-        if t == 1:
-            small = twin_index()
-        if last and LAST_ON_V:
-            small = [lambda: cp(own(wn, *twins(t)), upto(wn, NP[t]), idx=TL[t])]
-        for i, f in enumerate(division_steps(t)):
-            f()
-            if i == 1:
-                join_sum(t, 0, (1,))
-            if i == 6:
-                if last:
-                    join_sum(t, 1)
-                keep(t, K - 1)
-                join(t, 0)
-                if t > 0:
-                    tt(own(ln, *twins(t)), upto(ln, NP[t]), R("tw", 0, CAP), A.max, idx=TL[t])
-            elif i in (0, 2, 3, 4, 5) and small:
-                small.pop(0)()
-        xc = own(wn, L0, L0 + CAP) if t == 0 else R("xc", 0, CAP)
-        if last and LAST_ON_V:
-            ts(xc, upto(wn, NT[t]), 0.5, A.mult, idx=ML[t])
-        else:
-            act(xc, upto(wn, NT[t]), 0.5, idx=ML[t])
-        act(R("t1", 0, CAP), upto("pl", LM), RM[t], idx=ML[t])
+        run([place, fill, offsets, fill, scatter])
+        if t > 0:
+            tt(own(ln, *twins(t)), upto(ln, NP[t]), T2[t - 1], A.max, idx=TL[t])
+        if last:
+            join_sum(t, 2, (0,))
+        join(t, 0)
+        run([named, fill if last else number, listed, fill])
+        xc = own(wn, NT[t], NT[t + 1])
+        act(xc, upto(wn, NT[t]), 0.5, idx=ML[t])
+        act(R("t1", 0, CAP), upto("pl", NT[t]), RM[t], idx=ML[t], bias=FAR[t])
         for c, grp in bq[len(bq) - held:]:
             gather_b(t, c, grp)
         cp(R("bg", 0, CAP), upto(ln, NT[t]), idx=ML[t])
-        if not last:
-            consts = round_consts(t + 1)
-            consts.pop()()
-        tt(upto(ln, NT[t]), R("bg", 0, CAP), R("t2", 0, CAP), A.max, oidx=ML[t])
-
-        def kept_sums(t=t, K=K):
-            for c in range(K - 1, K + min(t, 1)):
-                join_sum(t, c, (0,))
-
-        def last_sums(t=t, K=K):
-            join_sum(t, K - 1, (1,))
-            if t > 0:
-                cp(own("gd", *twins(t)), upto("gd", NP[t]), idx=TL[t])
-                join_sum(t, K, (1,))
-
-        def twin_join(t=t, K=K):
-            if t > 0:
-                join(t, K)
-
-        def mothers_links(t=t):
-            ts(R("lk", 0, CAP), upto(LB[t + 1], NT[t]), NRM[t], A.mult, idx=ML[t])
 
         def halve():
             cp(upto(wn, NT[t]), xc, oidx=ML[t])
-
-        def children():
-            if t > 0:
-                cp(own(wn, L0, NT[t + 1]), xc, oidx=CL[t])
+        fill(len(small))
         if last:
-            v2 = V0[t][2]
-            run([kept_sums, halve])
+            halve()
+        tt(upto(ln, NT[t]), R("bg", 0, CAP), T2[RO if t == 1 else t], A.max, oidx=ML[t])
+        if not last:
+            for c in range(1, 2 + t):
+                join_sum(t, c, (0,))
+
+        def last_sums(t=t):
+            join_sum(t, 1, (1,))
+            if t == RO - 1:
+                tt(own("gd", *cells(t, 2)), upto("gd", L0), T2[0], A.max, idx=ML[0])
+            if t > 0:
+                cp(own("gd", *twins(t)), upto("gd", NP[t]), idx=TL[t])
+                join_sum(t, 2, (1,))
+
+        def twin_join(t=t):
+            if t > 0:
+                join(t, 2)
+        if last:
             dmas(OUTQ, [(T.yx[:, 0:L0], ap(own(wn, 0, L0)), [own(wn, 0, L0)], [])])
-            join(t, 1)
-            dmas(OUTQ, [(T.yn[:, 0:v2], ap(own(ln, 0, v2)), [own(ln, 0, v2)], [])])
-            children()
-            dmas(OUTQ, [(T.yx[:, L0:LM], ap(own(wn, L0, LM)), [own(wn, L0, LM)], [])])
+            dmas(OUTQ, [(T.yn[:, 0:C0], ap(own(ln, 0, C0)), [own(ln, 0, C0)], [])])
+            act(OX, own(wn, L0, LM + 8), idx=R("fl", 0, 36))
+            dmas(OUTQ, [(T.yx[:, L0:LM], ap(OX), [OX], [])])
             last_sums()
-            join(t, K - 1)
+            join(t, 1)
+            dmas(OUTQ, [(T.yn[:, C0:L0], ap(own(ln, C0, L0)), [own(ln, C0, L0)], [])])
             twin_join()
-            mothers_links()
             child_links(t)
-            dmas("S", [(T.yn[:, v2:LM], ap(own(ln, v2, LM)), [own(ln, v2, LM)], [])])
+            cp(OL, own(ln, L0, LM + 8), idx=R("fl", 0, 36))
+            dmas("S", [(T.yn[:, L0:LM], ap(OL), [OL], [])])
         else:
             once, twice, pick = relayout_steps(t + 1, 0)
-            run([kept_sums, halve, once, children])
+            run([halve, once])
             copy_x(t + 1, 0)
-            rest = []
-            run([twice, consts[1], pick])
-            if t == 0:
-                consts[0]()
-            else:
-                small = [lambda: rest.extend(twin_list()), lambda: rest[0](), lambda: rest[1](), consts[0]]
+            twice()
+            pick(0, PICK_FIRST)
+            pick(PICK_FIRST, 16)
             steps = ([last_sums, lambda t=t: join(t, 1)] + relayout_steps(t + 1, 1)
-                     + [twin_join, mothers_links, lambda t=t: child_links(t)])
+                     + [twin_join, lambda t=t: child_links(t)])
             if t == 1:
                 steps += relayout_steps(2, 2)
+                steps += [lambda: tt(upto(LB[2], NT[1]), own(LB[2], NT[1], NT[2]), T2[1], A.max, oidx=ML[1])]
             carry = {}
-            for k, f in list(zip(CARRY_AT, steps)) + list(zip(SMALL_AT, small)):
+            for k, f in zip(CARRY_AT, steps):
                 carry[k] = carry.get(k, []) + [f]
 
     for s in total:

from concourse.bass import DstId, RemoteDMATransfer
from concourse.mybir import AluOpType, ActivationFunctionType

N = 8
OFF = (7, 1, 6, 2)
L0, CAP, RO, GH, H = 1024, 192, 3, 512, 80
LM = L0 + RO * CAP
SP = CAP
O0 = SP + GH
TW = O0 + LM + 8
CHUNKS = ((512, 512), (512, 512), (512, 512, CAP))
NP = tuple(sum(c) for c in CHUNKS)
WIDTHS = tuple(sorted(set(w for c in CHUNKS for w in c)))
NMAX = 1408
BIG = 4096.0

QUARTERS = ((0, 4), (4, 4), (8, 4), (12, 4))
HALVES = ((0, 8), (8, 8))
FIRST_GROUPS = ((0, 2), (2, 2), (4, 4), (8, 8))
ENDING = ((0, 8), (8, 4), (12, 4))
B_GROUPS = ((((0, 4), (4, 4), (8, 8)), ENDING), (HALVES, ENDING), (HALVES, ((0, 2), (2, 8), (10, 4), (14, 2))))
PICK_FIRST = 8
DMA_FILLS = 4
B_ON_V = ((), (), ((1, (0, 2), 3),))
A_ON_V = ((4,), (4,), (4,))
B_FIRST = 1
PICK_LATE = 1
B_HELD = (1, 1, 0)
CARRY_AT = (-1, 1, 2, 3, 4, 5, 6, 7, 8, 9, 11)
UPD_AT = (8, 8, 11, 13, 15, 16)
DEFER = (2, 2, 4)
KIN_AT = (9, 9, 10, 10, 11, 11, 12, 12, 13, 14)
JOIN_AT = 11
KEEP_AT, X_AT, SUM_AT, NEXT_AT = 2, 2, 4, 12
HEAD = 8
OUTQ = "Y"
RING = 9216
CS = 6
GHOST0_ENGINES = 4

F, BF, I32, U16 = "float32", "bfloat16", "int32", "uint16"
SCRATCH = {
    "wa": ("sbuf", [128, TW], F), "wb": ("sbuf", [128, TW], F), "wc": ("sbuf", [128, TW], F),
    "la": ("sbuf", [128, TW], F), "lb": ("sbuf", [128, TW], F), "lc": ("sbuf", [128, TW], F),
    "pp": ("sbuf", [128, 16 * NP[-1]], F),
    "pl": ("sbuf", [128, O0 + NMAX], F),
    "gr": ("sbuf", [128, RING], F),
    "gd": ("sbuf", [128, O0 + NMAX], F),
    "tt": ("sbuf", [128, 1056], F), "io3": ("sbuf", [128, 32], F),
    "zr": ("sbuf", [128, NP[-1]], F), "zl": ("sbuf", [128, L0 + 2 * CAP], F),
    "zh": ("sbuf", [128, L0], F),
    "nbi": ("sbuf", [128, L0], I32),
    "id1": ("sbuf", [128, 128], F), "idq": ("sbuf", [128, 128], F),
    "idn": ("sbuf", [128, 128], F), "idb": ("sbuf", [128, 128], F), "idm": ("sbuf", [128, 128], F),
    "xc": ("sbuf", [128, CAP], F), "lk": ("sbuf", [128, CAP], F), "t1": ("sbuf", [128, CAP], F),
    "t2": ("sbuf", [128, 4 * CAP], F), "bg": ("sbuf", [128, CAP], F),
    "gs": ("sbuf", [128, 128], F),
    "cmp": ("sbuf", [128, CS * 512], BF),
    "lt0": ("sbuf", [128, NP[-1]], U16), "lt1": ("sbuf", [128, NP[-1]], U16),
    "vote": ("sbuf", [128, O0 + NMAX], BF),
    "win": ("sbuf", [128, 1600], BF),
    "val": ("sbuf", [128, 176], BF),
    "sb": ("sbuf", [128, 144], BF), "wb16": ("sbuf", [128, 144], BF),
    "negu": ("sbuf", [128, 128], BF), "ones": ("sbuf", [128, 128], BF),
    "rl": ("sbuf", [128, sum(WIDTHS) // 16], U16),
    "ip": ("sbuf", [128, 8], I32), "col": ("sbuf", [128, 32], F),
    "iot": ("sbuf", [128, 36], F), "jj": ("sbuf", [128, 36], F),
    "kf": ("sbuf", [128, 32], F), "ki": ("sbuf", [128, 32], I32),
    "dd": ("sbuf", [128, 12], F),
    "rr": ("sbuf", [128, 16], BF), "rin": ("sbuf", [128, 16], BF),
    "sm": ("sbuf", [128, 48], F), "fa": ("sbuf", [128, 36], F), "fb": ("sbuf", [128, 36], F),
    "pos": ("sbuf", [128, 12], U16), "ml": ("sbuf", [128, 36], U16), "fl": ("sbuf", [128, 36], U16),
    "xx": ("psum", [128, 1024], F), "yy": ("psum", [128, 1024], F),
    "n0": ("psum", [128, 512], F), "n1": ("psum", [128, 512], F),
    "d0": ("psum", [128, 512], F), "mb": ("psum", [128, 512], F),
}
PSUM = ("xx", "yy", "n0", "n1", "d0", "mb")
BANKS = {"n": (("n0", 0), ("n1", 0), ("n0", 0)), "d": (("d0", 0), ("d0", 0), ("yy", 0)),
         "j": (("n0", 0), ("n1", 0), ("d0", 0))}
SEMAPHORES = (["qV", "qS", "qP", "qG"] + ["d%d" % i for i in range(60)]
              + ["ga%d" % t for t in range(RO)] + ["gl%d" % t for t in range(RO)]
              + ["%s%d" % (s, i) for s in ("fa", "fl", "fh", "ra", "rl") for i in range(9)])

A = AluOpType
ACT = ActivationFunctionType


def partner_of(T, topo, core):
    same = [c for c in T.cores if topo.chip(c) == topo.chip(core) and topo.die(c) == topo.die(core)]
    i = same.index(core)
    return same[i + 1] if i % 2 == 0 else same[i - 1]


def rank_program(g, core, T, topo):
    rank = T.rank_of(core)
    if rank is None:
        return
    Q = {"V": g.vector, "S": g.scalar, "P": g.tensor, "G": g, "Y": g.sync}
    count = {"V": 0, "S": 0, "P": 0, "G": 0}
    known = {q: {} for q in Q}
    seen = {}
    total = {}
    ndma = [0]

    def wait(q, tok):
        s, v = tok
        if known[q].get(s, 0) < v:
            Q[q].wait_ge(T.sem[s], v)
            known[q][s] = v

    def before(q, reads, writes):
        need = {}
        for acc, w in ((reads, False), (writes, True)):
            for b, lo, hi in acc:
                for e in seen.get(b, ()):
                    if q == "P" and e[3] == "P":
                        continue
                    meet = e[0] < hi and lo < e[1] and (w or e[2])
                    shared = b in PSUM and e[3] != q and e[0] // 512 <= (hi - 1) // 512 and lo // 512 <= (e[1] - 1) // 512
                    if meet or shared:
                        need[e[4][0]] = max(need.get(e[4][0], 0), e[4][1])
        for s in need:
            wait(q, (s, need[s]))

    def note(q, reads, writes, tok):
        for b, lo, hi in writes:
            seen[b] = [e for e in seen.get(b, ()) if not (lo <= e[0] and e[1] <= hi)]
            seen[b].append([lo, hi, True, q, tok])
        for b, lo, hi in reads:
            keep = [e for e in seen.get(b, ())
                    if not (not e[2] and e[4][0] == tok[0] and lo <= e[0] and e[1] <= hi)]
            keep.append([lo, hi, False, q, tok])
            seen[b] = keep
        total[tok[0]] = max(total.get(tok[0], 0), tok[1])

    def op(q, call, reads, writes):
        before(q, reads, writes)
        count[q] += 1
        call().then_inc(T.sem["q" + q], 1)
        note(q, reads, writes, ("q" + q, count[q]))

    def dmas(q, items):
        s = "d%d" % ndma[0]
        ndma[0] += 1
        for o, i, r, w in items:
            before(q, r, w)
        for o, i, r, w in items:
            Q[q].dma_start(o, i).then_inc(T.sem[s], 16)
        for o, i, r, w in items:
            note("D", r, w, (s, 16 * len(items)))

    def R(b, lo, hi):
        return (b, lo, hi)

    def ap(r):
        return T[r[0]][:, r[1]:r[2]]

    def sc(x):
        return ap(x) if isinstance(x, tuple) else x

    def regs(*xs):
        out = []
        for x in xs:
            if isinstance(x, tuple):
                out += [("gd#%d" % k, x[1], x[2]) for k in range(16)] if x[0] == "gd" else [x]
        return out

    def ts(out, in0, s1, o0, s2=None, o1=None, idx=None, step=None):
        i = ap(in0) if idx is None else ap(in0).indirect(ap(idx))
        o = ap(out) if step is None else T[out[0]][:, out[1]:out[2]:step]
        if o1 is None:
            f = lambda: g.vector.tensor_scalar(o, i, sc(s1), None, o0)
        else:
            f = lambda: g.vector.tensor_scalar(o, i, sc(s1), sc(s2), o0, o1)
        op("V", f, regs(in0, s1, s2, idx), regs(out))

    def tt(out, in0, in1, o, idx=None, oidx=None):
        i = ap(in0) if idx is None else ap(in0).indirect(ap(idx))
        oo = ap(out) if oidx is None else ap(out).indirect(ap(oidx))
        op("V", lambda: g.vector.tensor_tensor(oo, i, ap(in1), o), regs(in0, in1, idx, oidx), regs(out))

    def cp(out, in_, idx=None, oidx=None):
        i = ap(in_) if idx is None else ap(in_).indirect(ap(idx))
        o = ap(out) if oidx is None else ap(out).indirect(ap(oidx))
        op("V", lambda: g.vector.tensor_copy(o, i), regs(in_, idx, oidx), regs(out))

    def ms(out, c):
        op("V", lambda: g.vector.memset(ap(out), c), [], regs(out))

    def act(out, in_, scale=1.0, idx=None, bias=0.0):
        i = ap(in_) if idx is None else ap(in_).indirect(ap(idx))
        op("S", lambda: g.scalar.activation(ap(out), i, ACT.Identity, bias=sc(bias), scale=sc(scale)),
           regs(in_, idx, scale, bias), regs(out))

    def mm(out, lhsT, rhs, start, stop, step=None):
        r = ap(rhs) if step is None else T[rhs[0]][:, rhs[1]:rhs[2]:step]
        op("P", lambda: g.tensor.matmul(ap(out), ap(lhsT), r, start, stop), regs(lhsT, rhs), [out])

    def iota(out, pattern, base, cm):
        if SCRATCH[out[0]][2] == I32:
            f = lambda: g.iota(ap(out), pattern, base, cm)
        else:
            f = lambda: g.iota(ap(out), pattern, base, cm, allow_small_or_imprecise_dtypes=True)
        op("G", f, [], [out])

    def remote(transfers, lsem, reads, waits):
        before("G", reads, [])
        for tok in waits:
            wait("G", tok)
        trs, n = [], 0
        for dst, engs, rsem, srcs, d, alu in transfers:
            rid, pid, se = topo.addr(dst)
            m = 0
            for e in engs:
                m |= 1 << e
            trs.append(RemoteDMATransfer(dst_ids=[DstId(rid=rid, pnc=pid)], dma_engine_mask=m, remote_sem=T.sem[rsem],
                                         srcs=[ap(s) for s in srcs], dsts=[ap(d)], alu_op=alu))
            n += len(engs)
        g.remote_dma_fused(trs, local_sem=T.sem[lsem])
        note("D", reads, [], (lsem, n))
        total[lsem] = n
        return n

    mate = partner_of(T, topo, core)
    mate_engs = topo.engines(core, mate)
    WB = ("wa", "wb", "wc", "wa")
    LB = ("la", "lb", "lc", "la")
    NT = [L0 + CAP * t for t in range(RO + 1)]
    V0 = [[sum(ch[:c]) for c in range(len(ch))] for ch in CHUNKS]
    RLO = {w: sum(x // 16 for x in WIDTHS[:i]) for i, w in enumerate(WIDTHS)}
    PM, PG, PG16, PAR, WGT = (R("col", i, i + 1) for i in range(5))
    RM = [R("col", 8 + t, 9 + t) for t in range(RO)]
    NRM = [R("col", 12 + t, 13 + t) for t in range(RO)]
    NC_ = [R("col", 16 + t, 17 + t) for t in range(RO + 1)]
    PARC = R("col", 20, 21)
    FAR = [R("col", 24 + t, 25 + t) for t in range(RO)]
    ID1, IDQ, IDN, IDB, IDM = (R(b, 0, 128) for b in ("id1", "idq", "idn", "idb", "idm"))
    ONES = R("ones", 0, 128)
    ML = [R("ml", 12 * t, 12 * t + 12) for t in range(RO)]
    TL = [None] + ML
    T2 = [R("t2", CAP * t, CAP * t + CAP) for t in range(RO + 1)]
    KX = R("mb", 128, 128 + 2 * CAP)
    OX, OL = R("lb", 0, RO * CAP), R("lb", RO * CAP, 2 * RO * CAP)
    G1, M1 = R("lb", 6 * CAP, 7 * CAP), R("lb", 7 * CAP, 8 * CAP)

    def own(b, lo, hi):
        return R(b, O0 + lo, O0 + hi)

    def upto(b, n):
        return R(b, 0, O0 + n)

    def places(b, n):
        return R(b, SP, O0 + n)

    def cells(t, c):
        return V0[t][c], V0[t][c] + CHUNKS[t][c]

    def twins(t):
        return NP[t], NP[t] + CAP

    def bank(t, kind, c, lo=0, hi=None):
        b, o = BANKS[kind][c]
        return R(b, o + lo, o + (CHUNKS[t][c] if hi is None else hi))

    def P(t, c, k, n=1):
        C = CHUNKS[t][c]
        o = 16 * V0[t][c] + k * C
        return R("pp", o, o + n * C)

    def LT(t, c, k, n):
        Wc = CHUNKS[t][c] // 16
        o = V0[t][c] + k * Wc
        return R("lt%d" % (t % 2), o, o + n * Wc)

    def send_ghosts(t, src):
        trs, per = [], 0
        for d in range(len(OFF)):
            dst = T.cores[(rank - OFF[d]) % N]
            engs = topo.engines(core, dst)
            per = len(engs) // len(OFF)
            mine = engs[d * per:(d + 1) * per]
            if t == 0:
                mine = mine[::per // GHOST0_ENGINES]
            per = len(mine)
            trs.append((dst, mine, "ga%d" % t, [src], R(WB[t], SP + 128 * d, SP + 128 * d + 128), 0))
        remote(trs, "gl%d" % t, [src], [])
        note("X", [], [R(WB[t], SP, O0)], ("ga%d" % t, per * len(OFF)))

    made = []

    def relayout_consts(C):
        if C in made:
            return []
        made.append(C)
        Wc = C // 16
        kf, ki, j = R("kf", 0, Wc), R("ki", 0, Wc), R("jj", 0, Wc)
        return [lambda: (ts(kf, j, 1.0 / Wc, A.mult, 0.5 / Wc - 0.5, A.add), ts(PARC, PAR, (C + 16) / 16.0, A.mult)),
                lambda: cp(ki, kf),
                lambda: ts(kf, ki, -(C - 1) / 16.0, A.mult, PARC, A.add),
                lambda: tt(kf, kf, j, A.add),
                lambda: ts(R("rl", RLO[C], RLO[C] + Wc), kf, 16.0, A.mult)]

    def turn(out, in_):
        op("V", lambda: g.vector.transpose(ap(out), ap(in_)), [in_], [out])

    def relayout_steps(t, c):
        C, v0 = CHUNKS[t][c], V0[t][c]

        def pick(k0=0, k1=16):
            cp(LT(t, c, k0, k1 - k0), R("tt", 0, 2 * C + 32),
               idx=R("rl", RLO[C] + k0 * C // 256, RLO[C] + k1 * C // 256))
        return [lambda: turn(R("tt", 0, C), own(LB[t], v0, v0 + C)),
                lambda: turn(R("tt", C, 2 * C + 32), own(LB[t], v0 - 16, v0 + C + 16)),
                pick]

    def copy_wide(buf, o, src):
        lo, hi = src[1], src[2]
        while lo < hi:
            n = min(hi - lo, 512 - o % 512)
            mm(R(buf, o, o + n), ID1, R(src[0], lo, lo + n), True, True)
            lo, o = lo + n, o + n

    def copy_x(t, c):
        for i in range(2):
            copy_wide("xx", i * CHUNKS[t][c], own(WB[t], *cells(t, c)))

    def first_planes(t, c):
        copy_wide("yy", 0, P(t, c, 0, 2))

    def copy_d(t, c, stop, kind="d"):
        mm(bank(t, kind, c), ID1, own(WB[t], *cells(t, c)), True, stop)

    def gather_a(t, c):
        for k0, n in (FIRST_GROUPS, HALVES, ((1, 15),))[c]:
            (cp if c == 0 and k0 in A_ON_V[t] else act)(P(t, c, k0, n), places(WB[t], NT[t]), idx=LT(t, c, k0, n))

    slot = [0]

    def gather_b(t, c, grp, ring=False, by=act):
        k0, n = grp
        C, v0 = CHUNKS[t][c], O0 + V0[t][c]
        if c == 0 and not ring:
            b, o = P(t, c, k0, n)[:2]
        else:
            if slot[0] + n * C > RING:
                slot[0] = 0
            b, o = "gr", slot[0]
            slot[0] += n * C
        by(R(b, o, o + n * C), places(LB[t], NT[t]), idx=LT(t, c, k0, n))
        dmas("Y", [(T.gd[k0 + i:128:16, v0:v0 + C], T[b][k0 + i:128:16, o + i * C:o + (i + 1) * C],
                    [R(b, o + i * C, o + (i + 1) * C)], [R("gd#%d" % (k0 + i), v0, v0 + C)]) for i in range(n)])

    cslot = [0]

    def compare(t, c, j, amid=None):
        C = CHUNKS[t][c]
        if cslot[0] + 2 * C > CS * 512:
            cslot[0] = 0
        o = cslot[0]
        cslot[0] += 2 * C
        ks = [k for k in (2 * j, 2 * j + 1) if c < 2 or k > 0]
        x = R("xx", 0, 2 * C) if c < 2 else R(KX[0], KX[1], KX[1] + len(ks) * C)
        tt(R("cmp", o, o + len(ks) * C), P(t, c, ks[0], len(ks)), x, A.is_gt)
        if amid:
            amid()
        for i, k in enumerate(ks):
            mm(bank(t, "n", c), R("sb", 15 - k, 143 - k), R("cmp", o + i * C, o + (i + 1) * C),
               k == (0 if c < 2 else 1), k == 15)

    def Y(t, c):
        return own(WB[t + 1] if t < RO - 1 else WB[1], *cells(t, c))

    def running(t, c, j):
        y = R("yy", 0, 2 * CHUNKS[t][c])
        tt(y, P(t, c, 2 * j, 2), y, A.max)

    def greatest(t, c):
        C, xn = CHUNKS[t][c], Y(t, c)
        return [lambda: tt(xn, P(t, c, 15), R("yy", C, 2 * C), A.max),
                lambda: tt(R("yy", 0, C), P(t, c, 14), R("yy", 0, C), A.max),
                lambda: tt(xn, xn, R("yy", 0, C), A.max)]

    def lands(t, c):
        v0, v1 = cells(t, c)
        if c < 2:
            return [(0, HEAD, 1, R("zh", v0, v1)), (HEAD, 16 - HEAD, 1, R("zl", v0, v1))]
        return [(0, 16, 2, R("zl", v0, v0 + 2 * CAP))]

    def fold(t, c, amid=None):
        i = 3 * t + c
        total["fa%d" % i] = 0
        for j, (k0, n, w, land) in enumerate(lands(t, c)):
            if amid and j == len(lands(t, c)) - 1:
                amid()
            srcs = [P(t, c, k, w) for k in range(k0, k0 + n, w)]
            total["fa%d" % i] += remote([(mate, mate_engs, "fa%d" % i, srcs, land, 3)],
                                        ("fl%d" % i, "fh%d" % i)[j], srcs, [])

    def back(t, c):
        i, C = 3 * t + c, CHUNKS[t][c]
        srcs = [R(x[3][0], x[3][1] + u * C, x[3][1] + (u + 1) * C) for x in lands(t, c) for u in range(x[2])]
        z = R("zr", *cells(t, c))
        n = remote([(mate, mate_engs, "ra%d" % i, srcs, z, 3)], "rl%d" % i, [], [("fa%d" % i, total["fa%d" % i])])
        note("X", [], [z], ("ra%d" % i, n))

    def sum_a(t, c):
        mm(bank(t, "d", c), IDQ, Y(t, c), False, False)

    voted, counted = [], []

    def counts(t, lo, hi):
        voted.append((lo, hi))
        for cb in range(-(-NT[t] // 128)):
            a, b = 128 * cb, min(128 * cb + 128, NT[t])
            if cb not in counted and sum(max(0, min(b, y) - max(a, x)) for x, y in voted) == b - a:
                counted.append(cb)
                mm(R("mb", cb, cb + 1), own("vote", a, a + 128), R("ones", 0, 1), True, True)

    def update_steps(t, c):
        span = cells(t, c)
        z, d, xn = R("zr", *span), bank(t, "d", c), own(WB[t + 1], *span)

        def product():
            tt(z, z, (bank(t, "n", 0), R("xx", 0, CHUNKS[t][c]), R(KX[0], KX[1], KX[1] + CAP))[c], A.mult)

        def difference():
            mm(d, IDN, z, False, True)

        def vote():
            ts(own("vote", *span), d, 1.0, A.is_gt)
            if c == 0 and t < RO - 1:
                mm(R("mb", 128, 256), ONES, own("vote", 0, 128), True, True)
            counts(t, *span)
        return [product, difference, vote, lambda: ts(xn, d, 0.0, A.max, 2.0, A.min)]

    def ghost_steps(t):
        f = R("mb", 128, 256)

        def factor():
            ts(f, f, float(H), A.is_lt, 0.5, A.max)

        def send():
            tt(R("gs", 0, 128), own(WB[t + 1], 0, 128), f, A.mult)
            send_ghosts(t + 1, R("gs", 0, 128))
        return [factor, send]

    def keep(t, c):
        span = cells(t, c)
        tt(own(LB[t + 1], *span), own(LB[t], *span), bank(t, "n", c), A.min)

    def link_span(t, c):
        return cells(t, c) if c < 2 else (L0, NT[t])

    def join_sum(t, c, parts=(0, 1)):
        span = link_span(t, c)
        b = bank(t, "j", c, 0, span[1] - span[0])
        kin = t == RO - 1 and c == 2
        if 0 in parts:
            mm(b, IDB, own(LB[t + 1], *span), True, False)
            if kin:
                mm(bank(t, "j", c, 0, CAP), ID1, G1, False, False)
        if 1 in parts:
            mm(b, IDM if kin else ID1, own("gd", *span), False, True)

    def join(t, c):
        span = link_span(t, c)
        o = own(LB[t + 1], *span)
        tt(o, o, bank(t, "j", c, 0, span[1] - span[0]), A.max)

    def mothers(win, first, s, tmp, out):
        for i in range(16):
            mm(s, R("wb16", 15 - i, 143 - i), R(win, first + i, first + CAP), i == 0, i == 15, step=16)
        return [lambda: tt(tmp, R("jj", 0, 12), s, A.max), lambda: cp(out, tmp)]

    def division_steps(t):
        nb, MB = -(-NT[t] // 128), "mb"
        r, rin = R("rr", 0, nb), R("rin", 0, nb)
        pf = R("sm", 16, 16 + nb)
        s = R(MB, 16, 16 + nb)
        rest = []

        def scan():
            op("V", lambda: g.vector.tensor_tensor_scan(ap(rin), ap(R("ones", 0, nb)), ap(r), 0.0, A.mult, A.add),
               [r, R("ones", 0, nb)], [rin])
            mm(s, ONES, rin, True, False)
            mm(s, R("negu", 0, 128), r, False, True)
            mm(R(MB, 32, 33), ONES, R("rin", nb - 1, nb), True, True)

        def scatter():
            cp(R("win", 0, 1600), R("val", 0, 16 * nb), oidx=R("pos", 0, nb))
            rest.extend(mothers("win", 1, R(MB, 48, 60), R("sm", 32, 44), ML[t]))
        return [lambda: ts(r, R(MB, 0, nb), float(H), A.is_ge),
                scan,
                lambda: tt(pf, R("dd", 0, nb), s, A.min),
                lambda: ts(R("pos", 0, nb), pf, BIG, A.add),
                scatter,
                lambda: rest[0](),
                lambda: ts(NC_[t + 1], R(MB, 32, 33), float(CAP), A.min, NC_[t], A.add),
                lambda: rest[1]()]

    def closing_list():
        a, b, j = R("fa", 0, 36), R("fb", 0, 36), R("jj", 0, 36)
        d0, d1 = R("col", 28, 29), R("col", 29, 30)
        return [lambda: ts(d0, NC_[1], -1.0, A.mult, float(CAP), A.add),
                lambda: ts(d1, NC_[1], NC_[2], A.subtract, float(CAP), A.add),
                lambda: ts(a, j, NC_[1], A.is_ge, d0, A.mult),
                lambda: ts(b, j, NC_[2], A.is_ge, d1, A.mult),
                lambda: tt(a, a, j, A.add),
                lambda: tt(a, a, b, A.add),
                lambda: ts(R("fl", 0, 36), a, float(RO * CAP), A.min)]

    def round_consts(t):
        first = own("pl", L0, NT[1])
        if t == 0:
            act(R("win", 0, 208), R("gd", 0, 208))
            act(T2[0], first, RM[0])
            act(T2[RO], own("pl", NT[1], NT[2]), RM[1])
            return
        dmas("Y", [(T.win[:, 0:208], T.vote[:, 0:208], [R("vote", 0, 208)], [R("win", 0, 208)])])
        if t == 1:
            act(own("pl", NT[t], NT[t + 1]), first, bias=NC_[t])
            act(T2[t], own("pl", NT[t], NT[t + 1]), RM[t])
        else:
            ts(R("col", 27, 28), NC_[t], RM[t], A.mult)
            act(T2[t], first, RM[t], bias=R("col", 27, 28))

    def child_links(t):
        tt(own(LB[t + 1], NT[t], NT[t + 1]), upto(LB[t + 1], NT[t]), R("t1", 0, CAP), A.min, idx=ML[t])

    def run(steps):
        for f in steps:
            f()

    C0 = CHUNKS[0][0]
    dmas("Y", [(ap(own("wa", 0, 128)), T.x0[:, 0:128], [], [own("wa", 0, 128)])])
    C1 = C0 + 16
    dmas("S", [(ap(R("nbi", 0, C1)), T.nb[:, 0:C1], [], [R("nbi", 0, C1)])])
    dmas("S", [(ap(R("nbi", C1, L0)), T.nb[:, C1:L0], [], [R("nbi", C1, L0)])])
    dmas("Y", [(ap(own("wa", 128, L0)), T.x0[:, 128:L0], [], [own("wa", 128, L0)])])
    iota(R("ip", 0, 1), [[1, 1]], 0, 1)
    iota(R("iot", 0, 36), [[16, 36]], 0, 0)
    iota(R("io3", 0, 32), [[1, 16], [256, 2]], 0, 0)
    ms(ID1, 1.0)
    zer = R("gd", 0, O0)
    iota(R("la", O0 - 16, O0), [[1, 16]], GH - 16, 0)
    op("G", lambda: g.affine_select(T.id1[:], T.id1[:], [[-1, 128]], A.is_equal, 0.0, 0, 1), [ID1], [ID1])
    iota(own("pl", L0, NT[2]), [[1, 2 * CAP]], GH + L0, 0)
    send_ghosts(0, own("wa", 0, 128))
    iota(R("la", SP, O0 - 16), [[1, GH - 16]], 0, 0)
    ts(R("ip", 2, 3), R("ip", 0, 1), 4, A.arith_shift_right)
    ts(R("ip", 1, 2), R("ip", 0, 1), 15, A.bitwise_and)
    ms(R("gd", 0, SP), 0.0)
    tt(R("ip", 6, 7), R("ip", 0, 1), R("ip", 2, 3), A.add)
    ts(R("ip", 3, 4), R("ip", 0, 1), 112, A.bitwise_and)
    ms(R("sb", 0, 144), 0.0)
    ts(R("ip", 4, 5), R("ip", 6, 7), 1, A.bitwise_and)
    ms(R("wb16", 0, 144), 0.0)
    ms(own("la", L0, L0 + 16), 0.0)
    cp(R("col", 0, 4), R("ip", 1, 5))
    ms(R("gd", SP, O0), 0.0)
    ts(R("col", 21, 22), PM, 16.0, A.mult)
    ts(R("col", 23, 24), PAR, float(C1), A.mult)
    ts(R("jj", 0, 36), R("iot", 0, 36), PM, A.add)
    ms(R("negu", 0, 128), -1.0)
    ts(R("rl", RLO[C0], RLO[C0] + 32), R("io3", 0, 32), R("col", 21, 22), A.add, R("col", 23, 24), A.add)
    ts(R("col", 8, 11), R("iot", 0, 3), 1.0 / 16, A.mult, PM, A.is_equal)
    ms(ONES, 1.0)
    ts(R("col", 12, 15), R("col", 8, 11), -1.0, A.mult, 1.0, A.add)
    cp(own("la", 0, C1), R("nbi", 0, C1))
    made.append(C0)
    once, twice, pick = relayout_steps(0, 0)
    ms(NC_[0], 0.0)
    once()
    twice()
    cp(own("la", C1, L0), R("nbi", C1, L0))
    pick(0, PICK_FIRST)
    pick(PICK_FIRST, 16)
    ts(R("sb", 15, 143), R("iot", 0, 8), PG16, A.is_equal, BIG, A.mult, step=16)
    spare = WB[:3] + LB[:3] + ("pl",)
    dmas("Y", [(ap(R(b, 0, SP)), T.gd[:, 0:SP], regs(R("gd", 0, SP)), [R(b, 0, SP)]) for b in spare[:DMA_FILLS]])
    for b in spare[DMA_FILLS:]:
        act(R(b, 0, SP), R("gd", 0, SP))
    act(own("lb", L0, L0 + 16), R("gd", 0, 16))
    for b in (WB[RO], LB[RO]):
        act(own(b, LM, LM + 8), R("gd", 0, 8))
    act(R("vote", 0, O0), zer)
    copy_x(0, 0)

    def late_fills():
        act(R("dd", 0, 12), R("jj", 0, 12), bias=NMAX + 1 - BIG)
        act(WGT, RM[0], 16.0, bias=RM[1])
        act(R("col", 24, 27), R("col", 12, 15), BIG)
        act(own("vote", NT[1], NT[1] + 64), R("gd", 0, 64))
        act(IDQ, ID1, 0.25)
        act(IDN, ID1, -0.75)
        act(IDB, ID1, -BIG)
        act(IDM, ID1, NRM[1])
        round_consts(0)

    def late_consts():
        iota(R("xc", 0, 176), [[8, 11], [0, 16]], O0 // 16, 0)
        iota(R("lk", 0, 176), [[0, 11], [1, 16]], 0, 0)
        op("G", lambda: g.affine_select(T.negu[:], T.negu[:], [[-1, 128]], A.is_gt, 0.0, 0, 1),
           [R("negu", 0, 128)], [R("negu", 0, 128)])
        op("G", lambda: g.affine_select(T.negu[:], T.negu[:], [[-1, 128]], A.not_equal, -BIG, 0, 1),
           [R("negu", 0, 128)], [R("negu", 0, 128)])
        iota(places("pl", L0), [[1, GH + L0]], 0, 0)
        once, twice, pick = relayout_steps(0, 1)
        once()
        ts(R("wb16", 15, 143), R("iot", 0, 8), 0.0, A.mult, WGT, A.add, step=16)
        ts(R("xc", 0, 176), R("xc", 0, 176), PG, A.add, RM[0], A.mult)
        ts(R("lk", 0, 176), R("lk", 0, 176), RM[1], A.mult)
        twice()
        tt(R("val", 0, 176), R("xc", 0, 176), R("lk", 0, 176), A.add)
        pick()

    carry = {}
    SMALL = (lambda: [], lambda: relayout_consts(CAP), closing_list)
    for t in range(RO):
        last, K = t == RO - 1, len(CHUNKS[t])
        del voted[:], counted[:]
        bq = [(c, grp) for c in range(2) for grp in B_GROUPS[t][c]]
        if t == 0:
            late_fills()
            for c, grp in bq[:B_FIRST]:
                gather_b(t, c, grp, True)
            late_consts()
            bq = bq[B_FIRST:]
        held = B_HELD[t]
        up = [update_steps(t, c) for c in range(K)]
        extra = {(0, k): carry[k] for k in carry}
        wn, ln = WB[t + 1], LB[t + 1]

        def at(place, f):
            extra[place] = extra.get(place, []) + [f]

        def later_gathers():
            if last:
                x = own(WB[t], *cells(t, 2))
                dmas("Y", [(ap(P(t, 2, 0)), ap(x), [x], [P(t, 2, 0)])])
            for c in range(1, K):
                gather_a(t, c)
            if t > 0:
                round_consts(t)
            fold(t, 1, lambda: back(t, 0))
            if last:
                act(G1, places(LB[t], NT[t]), RM[1], idx=LT(t, 2, 1, 1))
                fold(t, 2)
            for c in range(1, K):
                back(t, c)
        gather_a(t, 0)
        fold(t, 0, (lambda: [iota(R(b, SP, O0), [[1, GH]], 0, 0) for b in LB[1:3]]) if t == 0 else None)
        at((0, NEXT_AT), later_gathers)

        def link_gathers():
            s = "rl%d" % (3 * t + K - 1)
            for c, grp in bq[:len(bq) - held]:
                if c >= PICK_LATE:
                    wait("Y", (s, total[s]))
                gather_b(t, c, grp)
        at((1, 0), link_gathers)
        for c, grp, place in B_ON_V[t]:
            bq.remove((c, grp))
            at((1, place), lambda c=c, grp=grp: gather_b(t, c, grp, True, cp))
        at((1, KEEP_AT), lambda: keep(t, 0))
        at((1, X_AT), lambda: copy_d(t, 0, True, "n"))
        at((1, SUM_AT), lambda: (copy_d(t, 0, False), sum_a(t, 0)))
        for place, f in zip(UPD_AT, up[0] + ([] if last else ghost_steps(t))):
            at((1, place), f)
        at((1, UPD_AT[3]), lambda: copy_d(t, 1, False))
        if last:
            for i in range(2):
                at((0, 16), lambda i=i: copy_wide(KX[0], KX[1] + i * CAP, own(WB[t], *cells(t, 2))))
            kin = [lambda j=j: compare(t, 2, j) for j in range(8)]
            kin += [lambda: tt(M1, P(t, 2, 1), R(KX[0], KX[1], KX[1] + CAP), A.max),
                    lambda: (keep(t, 2), join_sum(t, 0, (0,)))]
            for place, f in zip(KIN_AT, kin):
                at((1, place), f)
        else:
            at((1, JOIN_AT), lambda: join_sum(t, 0, (0,)))
        run(extra.get((0, -1), []))
        for c in range(2):
            first_planes(t, c)
            for j in range(8):
                if c == 0 or j < 8 - DEFER[t]:
                    compare(t, c, j, (lambda: copy_x(t, 1)) if c == 0 and j == 7 else None)
                run(extra.get((c, 2 * j), []))
                if j > 1:
                    running(t, c, j - 1)
                run(extra.get((c, 2 * j + 1), []))
            ends = greatest(t, c)
            run(ends[:2] + extra.get((c, 16), []) + ends[2:])
        sum_a(t, 1)
        late = [lambda j=j: compare(t, 1, j) for j in range(8 - DEFER[t], 8)]
        product, difference, vote, clip = up[1]
        if last:
            tt(Y(t, 2), upto(WB[1], L0), M1, A.max, idx=ML[0])
            copy_d(t, 2, False)
            sum_a(t, 2)
            run(late[:-1] + [product, difference] + up[2][:2] + late[-1:] + [vote] + up[2][2:])
        else:
            run(late[:-1] + [product, difference] + late[-1:] + [vote])
        if t > 0:
            cp(own("vote", *twins(t)), upto("vote", NP[t]), idx=TL[t])
            counts(t, *twins(t))
        small = SMALL[t]()

        def fill(n=1):
            run(small[:n])
            del small[:n]
        ready, scan, place, offsets, scatter, named, number, listed = division_steps(t)
        if last:
            join_sum(t, 0, (1,))
        keep(t, 1)
        fill(2 if last else 0)
        run([ready, fill, scan])
        join_sum(t, *((1, (0,)) if last else (0, (1,))))
        clip()
        if t > 0:
            act(own(wn, *twins(t)), upto(wn, NP[t]), idx=TL[t])
        run([place, fill, offsets, fill, scatter])
        if t > 0:
            tt(own(ln, *twins(t)), upto(ln, NP[t]), T2[t - 1], A.max, idx=TL[t])
        if last:
            join_sum(t, 2, (0,))
        join(t, 0)
        run([named, fill if last else number, listed, fill])
        xc = own(wn, NT[t], NT[t + 1])
        act(xc, upto(wn, NT[t]), 0.5, idx=ML[t])
        act(R("t1", 0, CAP), upto("pl", NT[t]), RM[t], idx=ML[t], bias=FAR[t])
        for c, grp in bq[len(bq) - held:]:
            gather_b(t, c, grp)
        cp(R("bg", 0, CAP), upto(ln, NT[t]), idx=ML[t])

        def halve():
            cp(upto(wn, NT[t]), xc, oidx=ML[t])
        fill(len(small))
        if last:
            halve()
        tt(upto(ln, NT[t]), R("bg", 0, CAP), T2[RO if t == 1 else t], A.max, oidx=ML[t])
        if not last:
            for c in range(1, 2 + t):
                join_sum(t, c, (0,))

        def last_sums(t=t):
            join_sum(t, 1, (1,))
            if t == RO - 1:
                tt(own("gd", *cells(t, 2)), upto("gd", L0), T2[0], A.max, idx=ML[0])
            if t > 0:
                cp(own("gd", *twins(t)), upto("gd", NP[t]), idx=TL[t])
                join_sum(t, 2, (1,))

        def twin_join(t=t):
            if t > 0:
                join(t, 2)
        if last:
            dmas(OUTQ, [(T.yx[:, 0:L0], ap(own(wn, 0, L0)), [own(wn, 0, L0)], [])])
            dmas(OUTQ, [(T.yn[:, 0:C0], ap(own(ln, 0, C0)), [own(ln, 0, C0)], [])])
            act(OX, own(wn, L0, LM + 8), idx=R("fl", 0, 36))
            dmas(OUTQ, [(T.yx[:, L0:LM], ap(OX), [OX], [])])
            last_sums()
            join(t, 1)
            dmas(OUTQ, [(T.yn[:, C0:L0], ap(own(ln, C0, L0)), [own(ln, C0, L0)], [])])
            twin_join()
            child_links(t)
            cp(OL, own(ln, L0, LM + 8), idx=R("fl", 0, 36))
            dmas("S", [(T.yn[:, L0:LM], ap(OL), [OL], [])])
        else:
            once, twice, pick = relayout_steps(t + 1, 0)
            run([halve, once])
            copy_x(t + 1, 0)
            twice()
            pick(0, PICK_FIRST)
            pick(PICK_FIRST, 16)
            steps = ([last_sums, lambda t=t: join(t, 1)] + relayout_steps(t + 1, 1)
                     + [twin_join, lambda t=t: child_links(t)])
            if t == 1:
                steps += relayout_steps(2, 2)
                steps += [lambda: tt(upto(LB[2], NT[1]), own(LB[2], NT[1], NT[2]), T2[1], A.max, oidx=ML[1])]
            carry = {}
            for k, f in zip(CARRY_AT, steps):
                carry[k] = carry.get(k, []) + [f]

    for s in total:
        if max(known[q].get(s, 0) for q in Q) < total[s]:
            wait("G", (s, total[s]))
